import numpy as np, ml_dtypes
CORES = [51,54,179,182]
N = 4
BF = ml_dtypes.bfloat16
W, C, TS, HOP, SA, SX = 2048, 256, 4, 3, 2, 8
def rise(rng):
    return np.sort(rng.integers(0, W - 15, (N, 8, 16, C)), axis=2) + np.arange(16)[:, None]
def inner(rng):
    m = np.sort(rng.integers(0, W - 15, (N, 8, 14, C)), axis=2) + np.arange(14)[:, None] + 1
    return np.concatenate([np.zeros((N, 8, 1, C), np.int64), m, np.full((N, 8, 1, C), W - 1)], axis=2)
def split(rng):
    k = np.arange(16)[:, None]
    return np.where(k < rng.integers(0, 17, (N, 8, 1, C)), k, W - 16 + k)
def signs(rng):
    return 2 * rng.integers(0, 2, (N, 8, C)) - 1
def pack(x, r, a, s, w):
    return {"xt": np.ascontiguousarray(x).reshape(N, 128, W).astype(np.float32).astype(BF), "rl": np.ascontiguousarray(r).reshape(N, 128, C).astype(np.int32),
            "av": np.ascontiguousarray(a).reshape(N, 128, C).astype(np.float32).astype(BF), "sg": s.astype(np.int32), "wt": np.ascontiguousarray(w).reshape(N, 128, 1).astype(np.int32)}
def setup_inputs(rng):
    return pack(rng.integers(0, 256, (N, 8, 16, W)), rise(rng), rng.integers(0, 256, (N, 8, 16, C)), signs(rng), rng.integers(1, 256, (N, 8, 16)))
def setup_inputs_corners(rng):
    k = np.arange(16)[:, None]; z = int(rng.integers(0, N)); z1 = (z + HOP) % N
    x = rng.integers(0, 256, (N, 8, 16, W)); kind = rng.integers(0, 16, (N, 8, 1, W)); x = np.where(kind == 0, 0, np.where(kind == 1, 255, x)); x[np.arange(N) != z1, ..., ::64] = 0
    zero = 64 * (np.sort(rng.integers(0, W // 64 - 15, (N, 8, 16, C)), axis=2) + k)
    high = 64 * (2 * np.sort(rng.integers(0, W // 128 - 7, (N, 8, 16, C)), axis=2) + k) + 32
    typ = rng.integers(0, 8, (N, 8, 1, C)); typ[..., 8:16] = np.arange(8); typ[:, 2, :, C // 2:C - 1] = 8; typ[..., 5] = 7; typ[..., C - 1] = 7; typ[z] = 7
    r = np.choose(typ, [k, W - 16 + k, rng.integers(0, W - 15, (N, 8, 1, C)) + k, inner(rng), split(rng), rng.integers(0, W - 30, (N, 8, 1, C)) + 2 * k, rise(rng), zero, high])
    ka = rng.integers(0, 5, (N, 8, 1, C)); a = np.where(ka == 0, 0, np.where(ka == 1, 255, rng.integers(0, 256, (N, 8, 16, C))))
    a[z, :, :, 0] = rng.integers(1, 256, (8, 16))
    kw = rng.integers(0, 4, (N, 8, 1)); w = np.where(kw == 0, 1, np.where(kw == 1, 255, rng.integers(1, 256, (N, 8, 16))))
    w[:, 2, 0] = 1; w[:, 2, 1] = 16
    y = x[:, 2, :, 32::64]
    rem = (np.where(np.arange(W // 64) % 2 == 0, 4089, 4087) - np.sum(w[:, 2, 2:, None] * y[:, 2:], axis=1)) & 4095
    y[:, 0] = rem & 15; y[:, 1] = rem >> 4
    return pack(x, r, a, signs(rng), w)
def setup_inputs_ends(rng):
    k = np.arange(16)[:, None]; S = W >> 4
    w = 1 + 254 * rng.integers(0, 2, (N, 8, 16)); w[..., 0] = 1; w[..., 15] = 1; w[..., 7] = 255; w[:, 3] = 255; w[:, 5] = 1
    top = np.zeros((16, 1), np.int64); top[[0, 7, 15]] = 1
    kind = rng.integers(0, 6, (N, 8, 1, W)); x = rng.integers(0, 2, (N, 8, 16, W))
    x = np.where(kind == 0, 0, np.where(kind == 1, 1, np.where(kind == 2, top, x)))
    x[..., ::S] = top
    m = rng.random((N, 8, 16)) < 0.4; m[:, ::2] = False; m[..., 15] = True; m[:, 7, rng.integers(0, 4)] = True
    x[..., S - 1::S] = np.where(m[:, :, None, :], 1, x[..., S - 1::S]); x[:, :, 3, S - 1::S] = m
    ka = rng.integers(0, 4, (N, 8, 1, C)); ka[..., [0, 2, C - 2, C - 1]] = 0; ka[..., [1, C - 3]] = 1
    a = np.where(ka == 0, 0, np.where(ka == 1, 1, rng.integers(0, 2, (N, 8, 16, C))))
    typ = np.array([0, 0, 0, 0, 0, 0, 0, 1, 1, 2])[rng.integers(0, 10, (N, 8, 1, C))]; typ[..., [0, 1, 2, C - 3, C - 2, C - 1]] = 2
    return pack(255 * x, np.choose(typ, [split(rng), inner(rng), k * S]), 255 * a, signs(rng), w)
def setup_inputs_shared(rng):
    r = rise(rng); r = np.take_along_axis(r, rng.integers(0, 4, (N, 8, 1, C)), 3)
    x = rng.integers(0, 256, (N, 8, 16, W)); a = rng.integers(0, 256, (N, 8, 16, C)); s = signs(rng)
    r[:, 6] = r[:, 6, :, :1].copy(); s[:, 6] = s[:, 6, :1].copy()
    b = rng.integers(112, 144, (N, 16, 1)); far = rng.integers(0, 64, (N, 16, W)) + 192 * rng.integers(0, 2, (N, 16, W))
    for q in range(N): far[q][:, r[q, 6, :, 0]] = b[q] + rng.integers(-2, 3, (16, 16))
    x[:, 6] = far; a[:, 6] = b + rng.integers(-2, 3, (N, 16, C))
    return pack(x, r, a, s, rng.integers(1, 256, (N, 8, 16)))
def setup_inputs_spread(rng):
    x = np.minimum(np.exp2(9 * rng.random((N, 8, 1, W))) * rng.random((N, 8, 16, W)), 255).astype(np.int64)
    a = np.minimum(np.exp2(9 * rng.random((N, 8, 1, C))) * rng.random((N, 8, 16, C)), 255).astype(np.int64)
    r = np.sort((rng.random((N, 8, 16, C)) ** 3 * (W - 15)).astype(np.int64), axis=2) + np.arange(16)[:, None]
    return pack(x, r, a, signs(rng), np.clip(np.exp2(8 * rng.random((N, 8, 16))).astype(np.int64), 1, 255))
def setup_inputs_ties(rng):
    x = 100 + rng.integers(0, 3, (N, 8, 16, W)); a = 100 + rng.integers(0, 3, (N, 8, 16, C)) + rng.integers(-1, 2, (N, 8, 1, C))
    x[:, 6:] = 100 + SX * rng.integers(-1, 2, (N, 2, 16, W)); a[:, 6:] = 100 + SA * rng.integers(-1, 2, (N, 2, 16, C))
    return pack(x, rise(rng), a, signs(rng), rng.integers(1, 256, (N, 8, 16)))
def check_inputs(d):
    bad = []
    for k, lo, hi in (("xt", 0, 255), ("rl", 0, W - 1), ("av", 0, 255), ("sg", -1, 1), ("wt", 1, 255)):
        v = np.asarray(d[k]).astype(np.float64)
        if not np.all((v >= lo) & (v <= hi)): bad.append("range of " + k)
        elif not np.all(v == np.floor(v)): bad.append("whole numbers of " + k)
    if np.any(np.asarray(d["sg"]) == 0): bad.append("signs of sg")
    r = np.asarray(d["rl"]).astype(np.int64).reshape(N, 8, 16, C)
    if not np.all(r[:, :, 1:] > r[:, :, :-1]): bad.append("rl not rising")
    return bad
def pick(x, ix):
    return np.take_along_axis(x, ix.reshape(8, 1, 16 * C), 2).reshape(8, 16, 16, C)
def reference(xt, rl, av, sg, wt):
    x = xt.astype(np.float32).astype(np.int64).reshape(N, 8, 16, W); R = rl.astype(np.int64).reshape(N, 8, 16, C)
    A = av.astype(np.float32).astype(np.int64).reshape(N, 8, 16, C); sig = sg.astype(np.int64).reshape(N, 8, C)
    w = wt.astype(np.int64).reshape(N, 8, 16, 1, 1); cnt = np.zeros((N, C), np.int64); kk = np.arange(16)[None, :, None]
    for t in range(TS):
        for r in range(N):
            p = (r + HOP * t) % N; X = x[p]; L = R[r].copy(); a = A[r].copy(); s0 = sig[r].copy()
            u = np.sum(w[p] * pick(X, L), axis=1) & 4095
            h = ((u * np.roll(u, -1, axis=1) >> 5) + u + cnt[r]) & 255
            st = (np.concatenate([L[:, 1:], L[:, :1] + W], axis=1) - L) * h >> 8
            q = (L + st) & (W - 1)
            Xq = pick(X, q); E = np.where(st == 0, -1, np.sum(np.abs(Xq - a[:, :, None, :]), axis=1))
            k = np.argmax(E, axis=1); e = np.max(E, axis=1)
            qb = np.take_along_axis(q, k[:, None, :], 1)[:, 0]; xq = np.take_along_axis(Xq, k[:, None, None, :], 2)[:, :, 0]
            s = np.where(np.sum(xq > a, axis=1) >= 8, 1, -1)
            out = k == 15; first = out & (qb < L[:, 0])
            shift = out & (s != np.where(first, s0, -s0))
            place = np.where(out, np.where(first != shift, 0, 15), k + (s != s0 * (1 - 2 * (k & 1))))
            col = np.take_along_axis(L, place[:, None, :], 1)[:, 0]; xl = np.take_along_axis(X, col[:, None, :], 2)
            go = e > np.sum(np.abs(xl - a), axis=1)
            qn = qb[:, None, :]; new = np.where(kk == place[:, None, :], qn, L)
            new = np.where((shift & first)[:, None, :], np.concatenate([qn, L[:, :15]], axis=1), new)
            new = np.where((shift & ~first)[:, None, :], np.concatenate([L[:, 1:], qn], axis=1), new)
            R[r] = np.where(go[:, None, :], new, L); sig[r] = np.where(go & shift, -s0, s0); cnt[r] = np.sum(go, axis=0)
            A[r] = np.where(go[:, None, :], a + np.clip(xq - a, -SA, SA), a)
            back = xl + np.clip(a - xl, -SX, SX)
            for g in range(8):
                c = np.nonzero(go[g])[0]; cols, i = np.unique(col[g, c], return_index=True)
                x[p, g][:, cols] = back[g][:, c[i]]
    return {"yr": R.reshape(N, 128, C).astype(np.float32), "ya": A.reshape(N, 128, C).astype(np.float32).astype(BF),
            "ys": sig.astype(np.float32), "yx": x.reshape(N, 128, W).astype(np.float32).astype(BF)}

@@ -1,0 +1,718 @@
+from concourse.mybir import AluOpType, ActivationFunctionType
+
+ALU = AluOpType
+ACT = ActivationFunctionType
+NS, HOP, W = 4, 3, 2048
+ORDER = (1, 0)
+CFG = {
+    "bmode": {(1, 0): "W", (1, 1): "Z", (0, 0): "Z", (0, 1): "Z"},
+    "aeng": {(1, 0): "V", (1, 1): "A", (0, 0): "A", (0, 1): "A"},
+    "war": True, "slack": 60.0, "lat": 90.0, "split": (False, False), "zsplit": 1, "asplit": 1, "boost": {}, "fix": 0.0,
+    "opt": ("", ""), "fine": {}, "fo": "NPD", "passes": 3, "wire": 2500.0,
+}
+CFG.update({'bmode': {(1, 1): 'WY', (1, 0): 'Z', (0, 1): 'Z', (0, 0): 'WY'}, 'aeng': {(1, 1): 'VA', (1, 0): 'VA', (0, 1): 'A', (0, 0): 'AV'}, 'split': (True, True), 'zsplit': 2, 'asplit': 2, 'slack': 0.0, 'opt': ('acgnr', 'ac'), 'boost': {'f1': 7500.0, 'b1': -7500.0, 'u1': 16400.0, 'u0': -1700.0, 'b0': 14900.0, 'f0': 200.0}, 'passes': 2})
+FINE = "b1Vwb512:296 f0AXR1024:-76 b0Vsf40:-190 u1Vwf640:70 u0Vwf512:-120 f1VD11280:-76 u1Awb256:-50 b0Vwb768:-22 b1VX00:-90 f1AXR1536:-50 b1Vwb1152:4"
+CFG["fine"] = {x.split(":")[0]: 100.0 * int(x.split(":")[1]) for x in FINE.split()}
+
+SCRATCH = {}
+
+
+def _buf(name, cols, dtype, where="sbuf"):
+    SCRATCH[name] = (where, [128] + (list(cols) if isinstance(cols, tuple) else [cols]), dtype)
+
+
+for _n in ("X0", "X1"):
+    _buf(_n, 2080, "bfloat16")
+_buf("iota", 2056, "float32")
+for _n, _c, _d in (("RI", 256, "int32"), ("sgI", 256, "int32"), ("sgB", 256, "bfloat16"), ("wI", 8, "int32"),
+                   ("pI", 16, "int32"), ("pF", 16, "float32"), ("ci", 528, "float32"), ("lst", 96, "uint16"),
+                   ("ones", 144, "bfloat16"), ("Z8", 144, "bfloat16"), ("Zw", 144, "bfloat16"),
+                   ("Zn", 144, "bfloat16"), ("G8", 16, "bfloat16"), ("I1", 128, "bfloat16"), ("I24", 128, "bfloat16"),
+                   ("In", 128, "bfloat16"), ("sameB", 128, "bfloat16"), ("blk", 128, "bfloat16"), ("nblk", 128, "bfloat16"), ("If", 256, "float32"), ("mask", 128, "bfloat16"),
+                   ("d0", 128, "bfloat16"), ("pm", 16, "bfloat16"), ("ysb", 256, "float32")):
+    _buf(_n, _c, _d)
+for _h in (0, 1):
+    for _t in range(NS + 1):
+        _buf("LF%d%d" % (_t, _h), 160, "float32")
+        _buf("LB%d%d" % (_t, _h), 272, "bfloat16")
+    for _t in range(NS):
+        _buf("OF%d%d" % (_t, _h), 152, "float32")
+        _buf("OB%d%d" % (_t, _h), 272, "bfloat16")
+    for _n, _c, _d in (("XR", 2048, "bfloat16"), ("D", 2048, "bfloat16"), ("AD", 2048, "bfloat16"),
+                       ("u16", 320, "uint16"), ("wi", 1168, "int32"), ("KB", (3, 64), "float32"),
+                       ("si", 64, "int32"), ("sf", 208, "float32"), ("wb", 1552, "bfloat16"), ("wf", 768, "float32"),
+                       ("tr", 640, "float32")):
+        _buf("%s%d" % (_n, _h), _c, _d)
+    for _n in ("P", "Q", "S", "E"):
+        _buf("%s%d" % (_n, _h), 512, "float32", "psum")
+
+DMAS = (["ldR", "ldW", "ldS", "ldX0", "cp0", "cp1", "cp2", "cp3", "stX", "stS"]
+        + ["%s%d" % (a, h) for a in ("ldA", "ldB", "stR", "stA") for h in (0, 1)])
+SEMAPHORES = ["V", "A", "T", "G", "sent"] + DMAS + ["arr%s%d%d" % (x, t, h) for x in "FB" for t in range(NS) for h in (0, 1)]
+
+
+def a(name, lo, hi, step=1, p=128):
+    if name[:2] in ("LF", "OF"):
+        lo, hi = lo + 24, hi + 24
+    return ("2", name, lo, hi, step, p)
+
+
+def a3(name, t, lo, hi):
+    return ("3", name, t, lo, hi)
+
+
+def ind(win, off):
+    return ("i", win, off)
+
+
+def dram(name, lo=None, hi=None):
+    return ("d", name, lo, hi)
+
+
+def real(T, s):
+    if not isinstance(s, tuple):
+        return s
+    if s[0] == "2":
+        if s[4] == 1:
+            return T[s[1]][0:s[5], s[2]:s[3]]
+        return T[s[1]][0:s[5], s[2]:s[3]:s[4]]
+    if s[0] == "3":
+        return T[s[1]][:, :, s[3]:s[4]] if s[2] is None else T[s[1]][:, s[2], s[3]:s[4]]
+    if s[0] == "d":
+        return T[s[1]][:] if s[2] is None else T[s[1]][:, s[2]:s[3]]
+    return real(T, s[1]).indirect(real(T, s[2]))
+
+
+def count(s):
+    if s[0] == "2":
+        return len(range(s[2], s[3], s[4]))
+    if s[0] == "3":
+        return (s[4] - s[3]) * (3 if s[2] is None else 1)
+    return 16 * count(s[2])
+
+
+def spans(s):
+    if not isinstance(s, tuple) or s[0] == "d":
+        return []
+    if s[0] == "2":
+        return [(s[1], s[2], s[3])]
+    if s[0] == "3":
+        return [(s[1], s[3], 128 + s[4])] if s[2] is None else [(s[1], 64 * s[2] + s[3], 64 * s[2] + s[4])]
+    return spans(s[1]) + spans(s[2])
+
+
+def where(s):
+    return SCRATCH[s[1]][0] if s[0] != "i" else "sbuf"
+
+
+def width(s):
+    n = s[1] if s[0] != "i" else s[1][1]
+    return 2 if SCRATCH[n][2] in ("bfloat16", "uint16") else 4
+
+
+def build(cfg):
+    ops = []
+    tag = ["setup"]
+    CYC, PEC, GA, SCA, FIX = cfg.get("cyc", 1.0), cfg.get("pec", 0.55), cfg.get("ga", 1.56), cfg.get("sca", 3.8), cfg["fix"]
+
+    def add(eng, call, outs, ins, cost, sem=None, lat=0.0):
+        wr, rd = [], []
+        for s in outs:
+            if s[0] == "i":
+                wr += spans(s[1])
+                rd += spans(s[2])
+            else:
+                wr += spans(s)
+        for s in ins:
+            rd += spans(s)
+        ops.append({"eng": eng, "call": call, "wr": wr, "rd": rd, "cost": cost + FIX, "sem": sem, "lat": lat, "tag": tag[0],
+                    "key": tag[0][0] + tag[0][2:] + eng + (wr[0][0][:2] + str(wr[0][1]) if wr else str(sem))})
+
+    def vcost(out, ins, tt=False):
+        n = count(out)
+        if out[0] == "i":
+            return 50 + SCA * n * CYC
+        if ins[0][0] == "i":
+            return 50 + GA * n * CYC
+        if tt:
+            f = 2.0 if all(where(s) == "sbuf" for s in ins) else 1.0
+        else:
+            f = 0.5 if all(width(s) == 2 for s in [out] + ins) else 1.0
+        return max(64, n * f) * CYC
+
+    def cp(out, in_):
+        add("V", lambda q, T: q.tensor_copy(real(T, out), real(T, in_)), [out], [in_], vcost(out, [in_]))
+
+    def tt(out, x, y, op):
+        add("V", lambda q, T: q.tensor_tensor(real(T, out), real(T, x), real(T, y), op), [out], [x, y], vcost(out, [x, y], True))
+
+    def ts(out, x, s1, op0, s2=None, op1=None):
+        def call(q, T):
+            if op1 is None:
+                return q.tensor_scalar(real(T, out), real(T, x), real(T, s1), None, op0)
+            return q.tensor_scalar(real(T, out), real(T, x), real(T, s1), real(T, s2), op0, op1)
+        add("V", call, [out], [x] + [s for s in (s1, s2) if isinstance(s, tuple)], vcost(out, [x]))
+
+    def ms(out, v):
+        add("V", lambda q, T: q.memset(real(T, out), v), [out], [], max(64, count(out) * width(out) / 4) * CYC)
+
+    def act(out, in_, func=ACT.Identity, bias=0.0, scale=1.0):
+        n = count(out)
+        c = 65 + GA * n * CYC if in_[0] == "i" else max(64, n) * CYC
+        if bias == 0.0 and func == ACT.Identity:
+            func = ACT.Copy
+        if func == ACT.Copy:
+            add("A", lambda q, T: q.activation(real(T, out), real(T, in_), func, scale=scale), [out], [in_], c)
+        else:
+            add("A", lambda q, T: q.activation(real(T, out), real(T, in_), func, bias=bias, scale=scale), [out], [in_], c)
+
+    def gat(eng, out, in_):
+        if eng == "V":
+            cp(out, in_)
+        else:
+            act(out, in_)
+
+    def mm(items):
+        def call(q, T):
+            r = None
+            for o, l, x, st, sp in items:
+                r = q.matmul(real(T, o), real(T, l), real(T, x), st, sp)
+            return r
+        add("T", call, [i[0] for i in items], [i[1] for i in items] + [i[2] for i in items],
+            60 + sum(max(min(64, count(i[1])), count(i[2])) * (4 if width(i[1]) == 4 else 1) for i in items) * PEC)
+
+    def iota(out, pattern, base=0, cm=0):
+        if SCRATCH[out[1]][2] == "int32":
+            add("G", lambda q, T: q.iota(real(T, out), pattern, base, cm), [out], [], 130 + 2 * count(out) * CYC)
+        else:
+            add("G", lambda q, T: q.iota(real(T, out), pattern, base, cm, allow_small_or_imprecise_dtypes=True),
+                [out], [], 130 + 2 * count(out) * CYC)
+
+    def dma(out, in_, sem, nbytes, eng="S"):
+        add(eng, lambda q, T: q.dma_start(real(T, out), real(T, in_)), [out], [in_], 60, sem, 1800 + nbytes / 150.0)
+
+    def transpose(tr):
+        add("V", lambda q, T: q.transpose(T[tr][:, 256:512], T[tr][:, 0:256]), [a(tr, 256, 512)], [a(tr, 0, 256)], 256 * CYC)
+
+    def zwin(name, b, p=128):
+        return a(name, 15 - b, 143 - b, 1, p)
+
+    dma(a("RI", 0, 256), dram("rl"), "ldR", 131072, "A")
+    dma(a("X0", 0, W), dram("xt"), "ldX0", 600000)
+    dma(a("wI", 0, 1), dram("wt"), "ldW", 512, "A")
+    dma(a("sgI", 0, 256, 1, 8), dram("sg"), "ldS", 8192, "A")
+    for h in ORDER:
+        dma(a("LB0%d" % h, 0, 128), dram("av", 128 * h, 128 * h + 128), "ldA%d" % h, 32768)
+        dma(a("LB0%d" % h, 128, 256), dram("av", 128 * h, 128 * h + 128), "ldB%d" % h, 32768)
+    iota(a("pI", 0, 1), [[0, 1]], 0, 1)
+    col = lambda j: a("pF", j, j + 1)
+    PP, PR, PR7, PG, P31, P16, PR3, PRH, PR1, PW, PN, PD, PT = range(13)
+    for j, (sh, mk) in enumerate(((0, 15), (0, 7), (4, 7), (0, 31), (0, 16), (2, 2), (1, 7), (0, 1))):
+        ts(a("pI", j + 1, j + 2), a("pI", 0, 1), sh, ALU.arith_shift_right, mk, ALU.bitwise_and)
+    cp(a("pF", 0, 9), a("pI", 0, 9))
+    cp(col(PW), a("wI", 0, 1))
+    ts(col(13), col(PR7), 32.0, ALU.mult, col(P16), ALU.add)
+    ts(col(PN), col(13), col(PR3), ALU.add)
+    ts(col(PD), col(PR), 2049.0, ALU.add)
+    ts(col(14), col(PR1), -8.0, ALU.mult, col(PRH), ALU.add)
+    ts(col(PT), col(14), 8.0, ALU.add, 8.0, ALU.mult)
+    DUP, N2T, BCB, BCK, T2W, W2N = (a("lst", 0, 32), a("lst", 32, 40), a("lst", 40, 48), a("lst", 48, 56),
+                                    a("lst", 64, 80), a("lst", 80, 88))
+    for lst, pat, base, c in ((DUP, [[16, 16], [0, 2]], 0, PR), (N2T, [[-1, 2], [4, 4]], 1, PN), (BCB, [[1, 8]], 0, None),
+                              (BCK, [[0, 8]], 0, PR7), (T2W, [[1, 8], [0, 2]], 0, PT), (W2N, [[32, 8]], 0, P31)):
+        src = a("ci", lst[2], lst[3])
+        iota(src, pat, base)
+        if c is None:
+            cp(lst, src)
+        else:
+            ts(lst, src, col(c), ALU.add)
+    iota(a("ci", 88, 96), [[16, 8]])
+    for h in ORDER:
+        ts(a("sf%d" % h, 0, 8), a("ci", 88, 96), col(PR), ALU.add, -128.0 if "s" in cfg["opt"][h] else 0.0, ALU.add)
+        ms(a("wb%d" % h, 1536, 1552), 0.0)
+    IB, IG, IC = a("ci", 128, 256), a("ci", 256, 384), a("ci", 384, 512)
+    iota(IB, [[0, 8], [1, 16]])
+    iota(IG, [[1, 8], [0, 16]])
+    iota(IC, [[1, 128]])
+    ts(a("G8", 0, 8), a("ci", 40, 48), col(PG), ALU.is_equal)
+    ms(a("Zw", 0, 144), 0.0)
+    ms(a("Zn", 0, 144), 0.0)
+    ts(a("Zw", 15, 143, 16), a("G8", 0, 8), col(PW), ALU.mult)
+    ts(a("Zn", 15, 143, 16), a("G8", 0, 8), -4096.0, ALU.mult)
+    ts(a("I1", 0, 128), IC, col(PP), ALU.is_equal)
+    ts(a("I24", 0, 128), a("I1", 0, 128), 8388608.0 if "P" in cfg["fo"] else 16777216.0, ALU.mult)
+    if "D" in cfg["fo"]:
+        act(a("If", 0, 128), a("I1", 0, 128))
+        act(a("If", 128, 256), a("I1", 0, 128), scale=-1.0)
+    ts(a("In", 0, 128), a("I1", 0, 128), -1.0, ALU.mult)
+    ts(a("sameB", 0, 128), IB, col(PR), ALU.is_equal)
+    ts(a("blk", 0, 128), IG, col(PG), ALU.is_equal, 2.0 ** -12, ALU.mult)
+    if "r" in cfg["opt"][0] + cfg["opt"][1]:
+        ts(a("nblk", 0, 128), a("blk", 0, 128), -1.0, ALU.mult)
+    ts(a("mask", 0, 128), IB, col(PR), ALU.is_gt, -1.0, ALU.mult)
+    ts(a("d0", 0, 128), IB, col(PR), ALU.not_equal, 1.0 / 32, ALU.max)
+    ms(a("d0", 0, 128, 16), 0.0)
+    ms(a("ones", 0, 144), 1.0)
+    add("G", lambda q, T: q.affine_select(T["Z8"][0:8, 0:144], T["ones"][0:8, 0:144], [[1, 144]], ALU.is_equal, 0.0, -15, -16),
+        [a("Z8", 0, 144)], [a("ones", 0, 144)], 170 + 288 * CYC)
+    ms(a("pm", 0, 1), -1.0)
+    ms(a("pm", 1, 16), 1.0)
+    for x in ("X0", "X1"):
+        ms(a(x, W, 2080), 4096.0)
+    iota(a("iota", 0, 2056), [[2, 2056]])
+    cp(a("sgB", 0, 256, 1, 8), a("sgI", 0, 256, 1, 8))
+    mm([(a("E0", 0, 16), zwin("Z8", b, 8), a("sgB", b, 256, 16, 8), b == 0, b == 15) for b in range(16)])
+    for h in ORDER:
+        tr = "tr%d" % h
+        ms(a("S%d" % h, 264, 272), -1.0)
+        cp(a(tr, 0, 256), ind(a("RI", 0, 256), a("lst", 16 * h, 16 * h + 16)))
+        transpose(tr)
+        cp(a("LF0%d" % h, 0, 128), ind(a(tr, 256, 512), N2T))
+        act(a("OF0%d" % h, -8, 0), a("E0", 8 * h, 8 * h + 8), scale=1.0 if "c" in cfg["opt"][h] else 2.0)
+
+    def names(t, h):
+        return ("LF%d%d" % (t, h), "LB%d%d" % (t, h), "P%d" % h, "Q%d" % h, "S%d" % h, "u16%d" % h, "wi%d" % h,
+                "wb%d" % h, "X%d" % (t % 2))
+
+    def flip(h, out, new, old, sg):
+        f8 = lambda j, n=1: a("sf%d" % h, 8 * j, 8 * (j + n))
+        tt(f8(20, 2), new, old, ALU.is_equal)
+        tt(f8(22), f8(20), f8(21), ALU.max)
+        act(f8(23), f8(22), bias=-1.0, scale=2.0)
+        tt(out, f8(23), sg, ALU.mult)
+
+    def send(dst, src, sem):
+        add("G", ("send", dst, src), [dst], [src], 250, sem, cfg["wire"])
+
+    def front(t, h):
+        tag[0] = "f%d%d" % (t, h)
+        LF, LB, P, Q, S, U, WI, WB, X = names(t, h)
+        XR, D, AD, KB = "XR%d" % h, "D%d" % h, "AD%d" % h, "KB%d" % h
+        win = a(X, 0, W + 1)
+        NXT = (72, 0)
+        cp(a(U, 0, 128), a(LF, 0, 128))
+        fo, TBO = cfg["fo"], 1280
+        act(a(LF, 128, 136), a(LF, 64, 72), bias=2048.0)
+        act(a(S, 0, 136), a(LF, 0, 136))
+        OF = "OF%d%d" % (t, h)
+        if t > 0:
+            flip(h, a(OF, -8, 0), a(LF, 24, 40), a(LF, -24, -8), a(LF, -8, 0))
+        if t < NS - 1:
+            act(a(OF, -24, -8), a(LF, 24, 40))
+        if "D" in fo:
+            mm([x for f in (0, 1) for x in
+                ((a(S, 136 + 64 * f, 200 + 64 * f), a("If", 0, 128), a(LF, NXT[f], NXT[f] + 64), True, False),
+                 (a(S, 136 + 64 * f, 200 + 64 * f), a("If", 128, 256), a(LF, 64 * f, 64 * f + 64), False, True))])
+        else:
+            for f in (0, 1):
+                tt(a(S, 136 + 64 * f, 200 + 64 * f), a(S, NXT[f], NXT[f] + 64), a(LF, 64 * f, 64 * f + 64), ALU.subtract)
+        if t > 0:
+            mm([(a(P, 256 + 8 * k, 264 + 8 * k), a("sameB", 0, 128), a(LB, 256, 264), True, True) for k in range(16)])
+        for f in (0, 1):
+            e = cfg["aeng"][(h, f)]
+            n = cfg["asplit"] if len(e) == 1 else len(e)
+            for j in range(n):
+                c, w = 64 * f + j * 64 // n, 64 // n
+                gat(e[j % len(e)], a(XR, 16 * c, 16 * (c + w)), ind(win, a(U, c, c + w)))
+        withn = t > 0 and "N" in fo
+        if withn:
+            act(a(WB, TBO, TBO + 128), a(P, 256, 384))
+        for f in (0, 1):
+            o = a(P, 64 * f, 64 * f + 64)
+            mm(([(o, a("I1", 0, 128), a(WB, TBO + 64 * f, TBO + 64 * f + 64), True, False)] if withn else [])
+               + [(o, zwin("Zw", b), a(XR, 1024 * f + b, 1024 * f + 1024, 16), b == 0 and not withn, b == 15) for b in range(16)])
+        UI, UU, W1, W2, W3, W4, W5, W6, QQ = 0, 128, 272, 400, 528, 656, 784, 912, 1040
+        parts = ((0, 64), (64, 128)) if cfg["split"][h] else ((0, 128),)
+        wi = lambda b, p: a(WI, b + p[0], b + p[1])
+        for p in parts:
+            if withn:
+                tt(wi(UI, p), a(P, p[0], p[1]), a(WB, TBO + p[0], TBO + p[1]), ALU.subtract)
+            else:
+                cp(wi(UI, p), a(P, p[0], p[1]))
+            ts(wi(UU, p), wi(UI, p), 4095, ALU.bitwise_and)
+        for lo, hi, nx in ((64, 128, 0), (0, 56, 72), (56, 64, 64)):
+            tt(a(WI, W1 + lo, W1 + hi), a(WI, UU + lo, UU + hi), a(WI, UU + nx, UU + nx + hi - lo), ALU.mult)
+        for p in parts[::-1]:
+            ts(wi(W2, p), wi(W1, p), 5, ALU.arith_shift_right)
+            tt(wi(W3, p), wi(W2, p), a(P, p[0], p[1]), ALU.add)
+            if t > 0 and "N" not in fo:
+                tt(wi(W3, p), wi(W3, p), a(P, 256 + p[0], 256 + p[1]), ALU.add)
+            ts(wi(W4, p), wi(W3, p), 255, ALU.bitwise_and)
+            if "P" in fo:
+                dh = a("wf%d" % h, 384 + p[0], 384 + p[1])
+                tt(dh, wi(W4, p), a(S, 136 + p[0], 136 + p[1]), ALU.mult)
+                ts(wi(W6, p), dh, 1.0 / 256, ALU.mult, -0.498046875, ALU.add)
+                act(a(WB, p[0], p[1]), dh, ACT.Sign, bias=255.5, scale=-1.0)
+            else:
+                tt(wi(W5, p), wi(W4, p), a(S, 136 + p[0], 136 + p[1]), ALU.mult)
+                ts(wi(W6, p), wi(W5, p), 8, ALU.arith_shift_right)
+                ts(a(WB, p[0], p[1]), wi(W6, p), 0.0, ALU.is_equal)
+            tt(wi(QQ, p), wi(W6, p), a(S, p[0], p[1]), ALU.add)
+            if p[1] == 128:
+                cp(a(U, 192, 256), a(WI, QQ + 64, QQ + 128))
+            if p[0] == 0:
+                ts(a(WI, W1, W1 + 64), a(WI, QQ, QQ + 64), 2047, ALU.bitwise_and)
+                cp(a(U, 128, 192), a(WI, W1, W1 + 64))
+        AA = a(LB, 0, 256)
+        for f in (1, 0):
+            mode = cfg["bmode"][(h, f)]
+            o = 1024 * f
+            for j in (0, 1):
+                md = mode[j % len(mode)]
+                x, y, c = a(AD, o + 512 * j, o + 512 * j + 512), a(D, o + 512 * j, o + 512 * j + 512), 128 + 64 * f + 32 * j
+                if md == "Z":
+                    if len(mode) == 2 or cfg["zsplit"] == 2:
+                        act(y, ind(win, a(U, c, c + 32)), scale=-1.0)
+                    elif j == 0:
+                        act(a(D, o, o + 1024), ind(win, a(U, c, c + 64)), scale=-1.0)
+                    e = "E%d" % j
+                    mm([(a(e, 0, 512), a("I1", 0, 128), y, True, False),
+                        (a(e, 0, 256), a("I1", 0, 128), AA, False, False),
+                        (a(e, 256, 512), a("I1", 0, 128), AA, False, True)])
+                    act(x, a(e, 0, 512), ACT.Abs)
+                else:
+                    for i in (0, 1):
+                        tt(a(D, y[2] + 256 * i, y[2] + 256 * i + 256), ind(win, a(U, c + 16 * i, c + 16 * i + 16)), AA, ALU.subtract)
+                    if md == "W":
+                        ts(x, y, 0.0, ALU.min, -2.0, ALU.mult)
+                    else:
+                        act(x, y, ACT.Abs)
+            kb, ko = (Q, 0) if f == 0 else (P, 128)
+            K = a(kb, ko, ko + 64)
+            it = [(K, a("I24", 0, 128), a(WB, 64 * f, 64 * f + 64), True, False)]
+            if "P" in fo:
+                it += [(K, a("I24", 0, 128), a("ones", 0, 64), False, False)]
+            if mode == "W":
+                it += [(K, zwin("Zn", b), a(D, o + b, o + 1024, 16), False, False) for b in range(16)]
+            else:
+                for j in range(len(mode)):
+                    if mode[j] == "W":
+                        it += [(a(kb, ko + 32 * j, ko + 32 * j + 32), zwin("Zn", b), a(D, o + 512 * j + b, o + 512 * j + 512, 16),
+                                False, False) for b in range(16)]
+            it += [(K, zwin("Zn", b), a(AD, o + b, o + 1024, 16), False, b == 15) for b in range(16)]
+            mm(it)
+            ev = a(LF, 72, 136) if f == 0 else a(LF, 64, 128)
+            for j, pay in enumerate((a(WI, QQ + 64 * f, QQ + 64 * f + 64), ev, a(LF, 0, 64))):
+                tt(a3(KB, j, 0, 64) if f == 1 else a(S, 272 + 64 * j, 336 + 64 * j), K, pay, ALU.add)
+
+    def back(t, h):
+        tag[0] = "b%d%d" % (t, h)
+        LF, LB, P, Q, S, U, WI, WB, X = names(t, h)
+        KB, SI, SF, WF = "KB%d" % h, "si%d" % h, "sf%d" % h, "wf%d" % h
+        OF, OB, XN = "OF%d%d" % (t, h), "OB%d%d" % (t, h), "X%d" % ((t + 1) % 2)
+        win = a(X, 0, W + 1)
+        A0 = a(LB, 0, 128)
+        f8 = lambda j, n=1: a(SF, 8 * j, 8 * (j + n))
+        tt(a3(KB, None, 0, 64), a3(KB, None, 0, 64), a(S, 272, 464), ALU.min)
+        tt(a3(KB, None, 0, 32), a3(KB, None, 0, 32), a3(KB, None, 32, 64), ALU.min)
+        tt(a3(KB, None, 0, 16), a3(KB, None, 0, 16), a3(KB, None, 16, 32), ALU.min)
+        tt(a(SI, 0, 24), a3(KB, None, 0, 8), a3(KB, None, 8, 16), ALU.min)
+        ts(a(SI, 24, 48), a(SI, 0, 24), 2047, ALU.bitwise_and)
+        cp(a(U, 256, 264), a(SI, 24, 32))
+        DQ, GT, AQ, DL, RL, NE, VAL, SC, CL, TB, CQ = [a(WB, 128 * j, 128 * j + 128) for j in range(1, 12)]
+        tt(DQ, ind(win, a(U, 256, 264)), A0, ALU.subtract)
+        opt = cfg["opt"][h]
+        if "g" in opt:
+            act(GT, DQ, ACT.Sign, bias=-0.5)
+        else:
+            ts(GT, DQ, 0.0, ALU.is_gt, 0.5, ALU.subtract)
+        mm([(a(P, 384, 392), zwin("Zn", b), a(WB, 256 + b, 384, 16), b == 0, b == 15) for b in range(16)])
+        act(AQ, DQ, ACT.Abs)
+        ts(f8(5, 3), a(SI, 0, 24), 0.0, ALU.is_ge, 2048.0, ALU.mult)
+        tt(f8(2, 3), a(SI, 24, 48), f8(5, 3), ALU.max)
+        EV, OD, SG, L = f8(3), f8(4), a(OF, -8, 0), f8(1)
+        tt(f8(8), EV, OD, ALU.subtract)
+        tt(f8(9), f8(8), SG, ALU.mult)
+        tt(f8(10), EV, OD, ALU.add)
+        if "c" in opt:
+            act(f8(11), a(P, 384, 392), ACT.Sign, bias=1024.0, scale=-1.0)
+        else:
+            ts(f8(11), a(P, 384, 392), 1024.0, ALU.is_lt, 0.5, ALU.subtract)
+        tt(f8(12), f8(11), f8(9), ALU.mult)
+        tt(L, f8(12), f8(10), ALU.add)
+        ts(a(U, 264, 272), L, 0.5, ALU.mult)
+        tt(DL, ind(win, a(U, 264, 272)), A0, ALU.subtract)
+        E = a(P, 256, 384)
+        it = [(E, a("I1", 0, 128), a("mask", 0, 128), True, False), (E, a("blk", 0, 128), AQ, False, False)]
+        if "r" in opt:
+            act(RL, DL, ACT.Abs)
+            mm(it + [(E, a("nblk", 0, 128), RL, False, True)])
+        else:
+            ts(RL, DL, 0.0, ALU.max, -2.0, ALU.mult)
+            mm(it + [(E, a("blk", 0, 128), DL, False, False), (E, a("blk", 0, 128), RL, False, True)])
+        act(a(WF, 0, 128), ind(L, BCB))
+        tt(NE, ind(a("iota", 0, 2056), a(U, 264, 272)), a(WF, 0, 128), ALU.not_equal)
+        tt(VAL, E, NE, ALU.is_gt)
+        add("V", lambda q, T: q.tensor_tensor_scan(real(T, SC), T["d0"][:, 0:128], real(T, VAL), 0.0, ALU.mult, ALU.add),
+            [SC], [VAL, a("d0", 0, 128)], 64 * CYC)
+        FIN = a(WB, SC[2] + 15, SC[3], 16)
+        if "n" in opt:
+            act(f8(13), FIN, ACT.Abs, bias=-262144.0, scale=262144.0)
+        else:
+            ts(f8(13), FIN, 1.0, ALU.not_equal, 8192.0, ALU.mult)
+        tt(f8(14), f8(13), L, ALU.add)
+        ts(a(U, 288, 304, 2), f8(14), 0.5, ALU.mult, col(PD), ALU.min)
+        ts(CL, DL, -8.0, ALU.max, 8.0, ALU.min)
+        B = a(Q, 128, 256)
+        mm([(B, a("I1", 0, 128), A0, True, False), (B, a("I1", 0, 128), DL, False, False), (B, a("In", 0, 128), CL, False, True)])
+        act(TB, B)
+        for m in range(7, -1, -1):
+            cp(ind(a(XN, 0, 2080), a(U, 288 + 2 * m, 289 + 2 * m)), a(WB, TB[2] + 16 * m, TB[2] + 16 * m + 16))
+        tag[0] = "u%d%d" % (t, h)
+        ts(CQ, DQ, -2.0, ALU.max, 2.0, ALU.min)
+        last = t == NS - 1
+        tr = "tr%d" % h
+        RB, ro = (tr, 512) if last else (OF, 0)
+        GO = a(OB, 256, 264)
+        if "s" in opt or not last:
+            ts(GO, FIN, 1.0, ALU.is_ge)
+        if "s" in opt:
+            act(a(WF, 128, 256), ind(L, BCK), scale=0.5)
+            act(a(WF, 256, 384), ind(f8(2), BCK))
+            tt(f8(16), GO, f8(0), ALU.mult)
+            ts(a(U, 272, 280), f8(16), 128.0, ALU.add)
+            r1, o1 = WF, 128
+        else:
+            NG = f8(15)
+            ts(NG, FIN, 1.0, ALU.is_lt, 4096.0, ALU.mult)
+            tt(f8(16, 4), ind(NG, a("lst", 48, 50)), f8(0, 4), ALU.add)
+            act(a(WF, 128, 256), ind(f8(17), BCK), scale=0.5)
+            act(a(WF, 256, 384), ind(f8(18), BCK))
+            ts(a(U, 272, 280), f8(16), 128.0, ALU.min)
+            r1, o1 = RB, ro
+        tt(a(WF, 384, 512), a(WF, 128, 256), a(S, 0, 128), ALU.is_le)
+        tt(a(WF, 512, 640), a(WF, 384, 512), a(S, 136, 264), ALU.mult)
+        tt(a(S, 272, 400), a(WF, 512, 640), a(S, 0, 128), ALU.add)
+        tt(a(WF, 640, 768), a(WF, 256, 384), a(S, 272, 400), ALU.min)
+        tt(a(r1, o1, o1 + 64), a(WF, 640, 704), a(S, 336, 400), ALU.max)
+        tt(a(r1, o1 + 64, o1 + 128), a(WF, 704, 768), a(S, 264, 328), ALU.max)
+        if "s" in opt:
+            tt(a(WF, 384, 512), a(WF, 128, 256), a(S, 0, 128), ALU.subtract)
+            tt(a(WF, 512, 640), ind(GO, BCK), a(WF, 384, 512), ALU.mult)
+            tt(a(RB, ro, ro + 128), a(WF, 512, 640), a(S, 0, 128), ALU.add)
+        AN = a(OB, 0, 128)
+        if "a" in opt:
+            act(GT, ind(a(WB, CQ[2], CQ[3] + 16), a(U, 272, 280)))
+            AN = a(Q, 256, 384)
+            mm([(AN, a("I1", 0, 128), A0, True, False), (AN, a("I1", 0, 128), GT, False, True)])
+            act(a(OB, 0, 128), AN)
+        else:
+            tt(AN, ind(a(WB, CQ[2], CQ[3] + 16), a(U, 272, 280)), A0, ALU.add)
+        LF2, LB2 = "LF%d%d" % (t + 1, h), "LB%d%d" % (t + 1, h)
+        if not last:
+            act(a(OB, 128, 256), AN)
+            send(a(LF2, -24, 128), a(OF, -24, 128), "arrF%d%d" % (t, h))
+            send(a(LB2, 0, 264), a(OB, 0, 264), "arrB%d%d" % (t, h))
+        else:
+            flip(h, f8(24), a(RB, ro + 24, ro + 40), a(LF, 24, 40), SG)
+            ts(a(U, 280, 288), f8(24), 0.0, ALU.is_gt)
+            act(a(OB, 128, 256), ind(a("pm", 0, 16), a(U, 280, 288)))
+            act(a(tr, 0, 256), ind(a(tr, 512, 640), T2W))
+            transpose(tr)
+            act(a(OF, 0, 128), ind(a(tr, 256, 512), W2N))
+            send(a(LF2, 0, 128), a(OF, 0, 128), "arrF%d%d" % (t, h))
+            send(a(LB2, 0, 256), a(OB, 0, 256), "arrB%d%d" % (t, h))
+
+    for t in range(NS):
+        tag[0] = "copy"
+        dma(a("X%d" % ((t + 1) % 2), 0, W), a("X%d" % (t % 2), 0, W), "cp%d" % t, 524288)
+        for h in ORDER:
+            front(t, h)
+        for h in ORDER:
+            back(t, h)
+    tag[0] = "end"
+    dma(dram("yx"), a("X%d" % (NS % 2), 0, W), "stX", 524288)
+    for h in ORDER:
+        LF, LB = "LF%d%d" % (NS, h), "LB%d%d" % (NS, h)
+        dma(dram("yr", 128 * h, 128 * h + 128), a(LF, 0, 128), "stR%d" % h, 65536)
+        dma(dram("ya", 128 * h, 128 * h + 128), a(LB, 0, 128), "stA%d" % h, 32768)
+        mm([(a("E%d" % h, 0, 128, 1, 8), a("G8", 0, 8), a(LB, 128, 256), True, True)])
+        act(a("ysb", 128 * h, 128 * h + 128, 1, 8), a("E%d" % h, 0, 128, 1, 8), scale=1.0 / 16)
+    dma(dram("ys"), a("ysb", 0, 256, 1, 8), "stS", 8192, "A")
+    return ops
+
+
+def link(ops, cfg):
+    hist = {}
+    for i, o in enumerate(ops):
+        deps = {}
+        for kind, lst in (("r", o["rd"]), ("w", o["wr"])):
+            for name, lo, hi in lst:
+                ps = SCRATCH[name][0] == "psum"
+                for j, k2, l2, h2 in hist.get(name, ()):
+                    if j == i:
+                        continue
+                    other = ops[j]["eng"] != o["eng"] or ops[j]["sem"] is not None or o["sem"] is not None
+                    if ps and other:
+                        deps[j] = True
+                    elif lo < h2 and l2 < hi and (kind == "w" or k2 == "w"):
+                        deps[j] = deps.get(j, False) or other or (o["eng"] != "T" and (k2 == "w" or cfg["war"]))
+        for kind, lst in (("r", o["rd"]), ("w", o["wr"])):
+            for name, lo, hi in sorted(set(lst)):
+                old = hist.get(name, [])
+                if kind == "w" and SCRATCH[name][0] != "psum":
+                    old = [e for e in old if not (lo <= e[2] and e[3] <= hi) or e[0] == i]
+                hist[name] = old + [(i, kind, lo, hi)]
+        o["deps"] = deps
+
+
+def arrange(ops, cfg):
+    n, LAT = len(ops), cfg["lat"]
+    succ = [[] for _ in ops]
+    for i, o in enumerate(ops):
+        for j in o["deps"]:
+            succ[j].append(i)
+    prio = [0.0] * n
+    for i in range(n - 1, -1, -1):
+        o = ops[i]
+        prio[i] = o["cost"] + o["lat"] + max([prio[j] + (LAT if ops[j]["deps"][i] else 0.0) for j in succ[i]] + [0.0])
+    for i in range(n):
+        g = ops[i]["tag"]
+        prio[i] += cfg["boost"].get(g[0] + g[2:], 0.0) + cfg["fine"].get(ops[i]["key"], 0.0)
+    left = [len(o["deps"]) for o in ops]
+    ready = {e: [] for e in "VATGS"}
+    avail = [0.0] * n
+    for i in range(n):
+        if left[i] == 0:
+            ready[ops[i]["eng"]].append(i)
+    free = {e: 0.0 for e in "VATGS"}
+    order = {e: [] for e in "VATGS"}
+    fin = [0.0] * n
+    for _ in range(n):
+        best = None
+        for e in "VATGS":
+            if ready[e]:
+                s = max(free[e], min(avail[i] for i in ready[e]))
+                if best is None or s < best[0]:
+                    best = (s, e)
+        s, e = best
+        i = max((i for i in ready[e] if avail[i] <= s + cfg["slack"]), key=lambda i: (prio[i], -i))
+        ready[e].remove(i)
+        st = max(free[e], avail[i])
+        o = ops[i]
+        o["start"] = st
+        free[e] = st + o["cost"]
+        fin[i] = free[e] + o["lat"]
+        order[e].append(i)
+        for j in succ[i]:
+            avail[j] = max(avail[j], fin[i] + (LAT if ops[j]["deps"][i] else 0.0))
+            left[j] -= 1
+            if left[j] == 0:
+                ready[ops[j]["eng"]].append(j)
+    pre = [[(j, ops[j]["lat"] + (LAT if w else 0.0)) for j, w in o["deps"].items()] for o in ops]
+    post = [[] for _ in ops]
+    for i in range(n):
+        for j, d in pre[i]:
+            post[j].append((i, d))
+    start = [o["start"] for o in ops]
+    best = (max(fin), start)
+    for _ in range(cfg["passes"]):
+        back = place(ops, sorted(range(n), key=lambda i: (-start[i] - ops[i]["cost"], -i)), post, [o["lat"] for o in ops])
+        start = place(ops, sorted(range(n), key=lambda i: (-back[i] - ops[i]["cost"], i)), pre, [0.0] * n)
+        end = max(start[i] + ops[i]["cost"] + ops[i]["lat"] for i in range(n))
+        if end < best[0]:
+            best = (end, start)
+    start = best[1]
+    order = {e: [] for e in "VATGS"}
+    for i in sorted(range(n), key=lambda i: (start[i], i)):
+        ops[i]["start"] = start[i]
+        order[ops[i]["eng"]].append(i)
+    return order, [start[i] + ops[i]["cost"] + ops[i]["lat"] for i in range(n)]
+
+
+def place(ops, seq, pre, first):
+    at = [0.0] * len(ops)
+    busy = {e: ([], []) for e in "VATGS"}
+    for i in seq:
+        s, c = first[i], ops[i]["cost"]
+        for j, d in pre[i]:
+            x = at[j] + ops[j]["cost"] + d
+            if x > s:
+                s = x
+        lo, hi = busy[ops[i]["eng"]]
+        k = len(lo)
+        while k > 0 and hi[k - 1] > s:
+            k -= 1
+        while k < len(lo) and lo[k] < s + c:
+            s = max(s, hi[k])
+            k += 1
+        lo.insert(k, s)
+        hi.insert(k, s + c)
+        at[i] = s
+    return at
+
+
+def plan(cfg):
+    ops = build(cfg)
+    link(ops, cfg)
+    order, fin = arrange(ops, cfg)
+    pos = {}
+    for e in order:
+        for k, i in enumerate(order[e]):
+            pos[i] = k
+    need = set()
+    waits = {}
+    for e in order:
+        seen = {}
+        for i in order[e]:
+            top = {}
+            for j, w in ops[i]["deps"].items():
+                if not w:
+                    continue
+                key = ops[j]["sem"] or ops[j]["eng"]
+                if pos[j] > seen.get(key, -1) and (key not in top or pos[j] > pos[top[key]]):
+                    top[key] = j
+            for key, j in top.items():
+                seen[key] = pos[j]
+                need.add(j)
+            waits[i] = list(top.values())
+    cnt = {}
+    for e in order:
+        c = 0
+        for i in order[e]:
+            if ops[i]["sem"] is None and i in need:
+                c += 1
+                cnt[i] = c
+    return {"ops": ops, "order": order, "waits": waits, "cnt": cnt, "need": need, "end": max(fin), "fin": fin}
+
+
+_PLAN = {}
+
+
+def rank_program(g, core, T, topo):
+    rank = T.rank_of(core)
+    if rank is None:
+        return
+    if "p" not in _PLAN:
+        _PLAN["p"] = plan(CFG)
+    p = _PLAN["p"]
+    ops, cores = p["ops"], T.cores
+    nxt, prv = cores[(rank + HOP) % len(cores)], cores[(rank - HOP) % len(cores)]
+    rid, pid = topo.addr(nxt, core)
+    eng, mask = topo.engines(core, nxt), topo.mask(core, nxt)
+    arrive = len(topo.engines(prv, core))
+    queues = {"V": g.vector, "A": g.scalar, "T": g.tensor, "G": g, "S": g.sync}
+    sent = 0
+    for e in "SGTAV":
+        q = queues[e]
+        for i in p["order"][e]:
+            o = ops[i]
+            for j in p["waits"][i]:
+                s = ops[j]["sem"]
+                if s is None:
+                    q.wait_ge(T.sem[ops[j]["eng"]], p["cnt"][j])
+                else:
+                    q.wait_ge(T.sem[s], arrive if s.startswith("arr") else 16)
+            if isinstance(o["call"], tuple):
+                q.remote_dma(real(T, o["call"][1]), real(T, o["call"][2]), T.sem[o["sem"]], T.sem.sent, pid, rid, mask)
+                sent += len(eng)
+            else:
+                r = o["call"](q, T)
+                if o["sem"] is not None:
+                    r.then_inc(T.sem[o["sem"]], 16)
+                elif i in p["cnt"]:
+                    r.then_inc(T.sem[e], 1)
+    g.wait_ge(T.sem.sent, sent)
+    for i, o in enumerate(ops):
+        if o["sem"] in DMAS and i not in p["need"]:
+            g.sync.wait_ge(T.sem[o["sem"]], 16)

@@ -1,18 +1,23 @@
+import math
+from concourse.bass import DstId, RemoteDMATransfer
 from concourse.mybir import AluOpType, ActivationFunctionType
 
 ALU = AluOpType
 ACT = ActivationFunctionType
 NS, HOP, W = 4, 3, 2048
 ORDER = (1, 0)
+X0, VOID, BIG = 32, 2048, 262144.0
+RT = "float16"
 CFG = {
-    "bmode": {(1, 0): "W", (1, 1): "Z", (0, 0): "Z", (0, 1): "Z"},
-    "aeng": {(1, 0): "V", (1, 1): "A", (0, 0): "A", (0, 1): "A"},
-    "war": True, "slack": 60.0, "lat": 90.0, "split": (False, False), "zsplit": 1, "asplit": 1, "boost": {}, "fix": 0.0,
-    "opt": ("", ""), "fine": {}, "fo": "NPD", "passes": 3, "wire": 2500.0,
+    "bmode": {(1, 1): "WY", (1, 0): "ZZ", (0, 1): "ZZ", (0, 0): "WY"},
+    "aeng": {(1, 1): "VA", (1, 0): "VA", (0, 1): "AA", (0, 0): "AA"},
+    "split": (True, True), "gt": ("A", "A"), "sg": ("A", "A"), "rl": ("A", "A"),
+    "slack": 0.0, "lat": 120.0, "fix": 0.0, "passes": 2, "wire": 3500.0, "cyc": 1.04, "pec": 0.52,
+    "boost": {}, "fine": {}, "opt": ("", ""), "optall": "qlvsnexc",
 }
-CFG.update({'bmode': {(1, 1): 'WY', (1, 0): 'Z', (0, 1): 'Z', (0, 0): 'WY'}, 'aeng': {(1, 1): 'VA', (1, 0): 'VA', (0, 1): 'A', (0, 0): 'AV'}, 'split': (True, True), 'zsplit': 2, 'asplit': 2, 'slack': 0.0, 'opt': ('acgnr', 'ac'), 'boost': {'f1': 7500.0, 'b1': -7500.0, 'u1': 16400.0, 'u0': -1700.0, 'b0': 14900.0, 'f0': 200.0}, 'passes': 2})
-FINE = "b1Vwb512:296 f0AXR1024:-76 b0Vsf40:-190 u1Vwf640:70 u0Vwf512:-120 f1VD11280:-76 u1Awb256:-50 b0Vwb768:-22 b1VX00:-90 f1AXR1536:-50 b1Vwb1152:4"
-CFG["fine"] = {x.split(":")[0]: 100.0 * int(x.split(":")[1]) for x in FINE.split()}
+CFG.update({'bmode': {(1, 1): 'WZ', (1, 0): 'ZW', (0, 1): 'ZY', (0, 0): 'YZ'}, 'aeng': {(1, 1): 'VA', (1, 0): 'VA', (0, 1): 'VA', (0, 0): 'AA'}, 'split': (True, True), 'gt': ('G', 'G'), 'sg': ('A', 'A'), 'rl': ('A', 'A'), 'slack': 30.0, 'lat': 120.0, 'passes': 3, 'boost': {}, 'opt': ('ev', 'ev'),
+            "rounds": 18000, "seed": 1, "heat": 40.0,
+            "models": ({"lat": 150.0, "wire": 2500.0}, {"lat": 110.0, "wire": 3500.0, "gc": 1000.0})})
 
 SCRATCH = {}
 
@@ -22,43 +27,46 @@ def _buf(name, cols, dtype, where="sbuf"):
 
 
 for _n in ("X0", "X1"):
-    _buf(_n, 2080, "bfloat16")
-_buf("iota", 2056, "float32")
+    _buf(_n, X0 + VOID + 16, "bfloat16")
+_buf("iota", VOID + 8, "float32")
 for _n, _c, _d in (("RI", 256, "int32"), ("sgI", 256, "int32"), ("sgB", 256, "bfloat16"), ("wI", 8, "int32"),
-                   ("pI", 16, "int32"), ("pF", 16, "float32"), ("ci", 528, "float32"), ("lst", 96, "uint16"),
+                   ("pI", 16, "int32"), ("pF", 16, "float32"), ("ci", 528, "float32"), ("lst", 112, "uint16"),
                    ("ones", 144, "bfloat16"), ("Z8", 144, "bfloat16"), ("Zw", 144, "bfloat16"),
-                   ("Zn", 144, "bfloat16"), ("G8", 16, "bfloat16"), ("I1", 128, "bfloat16"), ("I24", 128, "bfloat16"),
-                   ("In", 128, "bfloat16"), ("sameB", 128, "bfloat16"), ("blk", 128, "bfloat16"), ("nblk", 128, "bfloat16"), ("If", 256, "float32"), ("mask", 128, "bfloat16"),
+                   ("Zn", 144, "bfloat16"), ("G8", 16, "bfloat16"), ("I1", 128, "bfloat16"), ("I23", 128, "bfloat16"),
+                   ("In", 128, "bfloat16"), ("Ik", 384, "bfloat16"), ("CC", 512, "bfloat16"), ("MB", 2192, "bfloat16"), ("sameB", 128, "bfloat16"),
+                   ("blk", 128, "bfloat16"), ("nblk", 128, "bfloat16"), ("If", 512, "bfloat16"), ("mask", 128, "bfloat16"),
                    ("d0", 128, "bfloat16"), ("pm", 16, "bfloat16"), ("ysb", 256, "float32")):
     _buf(_n, _c, _d)
 for _h in (0, 1):
     for _t in range(NS + 1):
-        _buf("LF%d%d" % (_t, _h), 160, "float32")
-        _buf("LB%d%d" % (_t, _h), 272, "bfloat16")
+        _buf("LF%d%d" % (_t, _h), *((160, RT) if _t < NS else (264, "float32")))
+        _buf("LB%d%d" % (_t, _h), 256, "bfloat16")
     for _t in range(NS):
-        _buf("OF%d%d" % (_t, _h), 152, "float32")
-        _buf("OB%d%d" % (_t, _h), 272, "bfloat16")
+        _buf("OF%d%d" % (_t, _h), *((160, RT) if _t < NS - 1 else (264, "float32")))
+        _buf("OB%d%d" % (_t, _h), 256, "bfloat16")
     for _n, _c, _d in (("XR", 2048, "bfloat16"), ("D", 2048, "bfloat16"), ("AD", 2048, "bfloat16"),
                        ("u16", 320, "uint16"), ("wi", 1168, "int32"), ("KB", (3, 64), "float32"),
-                       ("si", 64, "int32"), ("sf", 208, "float32"), ("wb", 1552, "bfloat16"), ("wf", 768, "float32"),
-                       ("tr", 640, "float32")):
+                       ("si", 64, "int32"), ("sf", 208, "float32"), ("wb", 2704, "bfloat16"), ("hh", 32, RT), ("wf", 768, "float32"),
+                       ("tr", 640, "float32"), ("VB", 128, "bfloat16"), ("SC", 128, "bfloat16"),
+                       ("ZA", (2, 4, 2, 8), "float32"), ("ZB", (2, 4, 2, 8), "float32")):
         _buf("%s%d" % (_n, _h), _c, _d)
     for _n in ("P", "Q", "S", "E"):
         _buf("%s%d" % (_n, _h), 512, "float32", "psum")
 
-DMAS = (["ldR", "ldW", "ldS", "ldX0", "cp0", "cp1", "cp2", "cp3", "stX", "stS"]
-        + ["%s%d" % (a, h) for a in ("ldA", "ldB", "stR", "stA") for h in (0, 1)])
+DMAS = (["ldR", "ldW", "ldS", "ldX0", "cp0", "cp1", "cp2", "cp3", "stX"]
+        + ["%s%d" % (a, h) for a in ("ldA", "ldB", "stR", "stA", "stS") for h in (0, 1)])
 SEMAPHORES = ["V", "A", "T", "G", "sent"] + DMAS + ["arr%s%d%d" % (x, t, h) for x in "FB" for t in range(NS) for h in (0, 1)]
 
 
 def a(name, lo, hi, step=1, p=128):
     if name[:2] in ("LF", "OF"):
-        lo, hi = lo + 24, hi + 24
-    return ("2", name, lo, hi, step, p)
+        lo, hi = lo + 8, hi + 8
+    return ("n", name, ((lo, hi, step),), p)
 
 
-def a3(name, t, lo, hi):
-    return ("3", name, t, lo, hi)
+def nd(name, *ix):
+    shape = SCRATCH[name][1][1:]
+    return ("n", name, tuple((0, n, 1) if x is None else (x + (1,) if isinstance(x, tuple) else x) for x, n in zip(ix, shape)), 128)
 
 
 def ind(win, off):
@@ -72,33 +80,42 @@ def dram(name, lo=None, hi=None):
 def real(T, s):
     if not isinstance(s, tuple):
         return s
-    if s[0] == "2":
-        if s[4] == 1:
-            return T[s[1]][0:s[5], s[2]:s[3]]
-        return T[s[1]][0:s[5], s[2]:s[3]:s[4]]
-    if s[0] == "3":
-        return T[s[1]][:, :, s[3]:s[4]] if s[2] is None else T[s[1]][:, s[2], s[3]:s[4]]
+    if s[0] == "n":
+        return T[s[1]][(slice(0, s[3]) if s[3] > 0 else slice(0, 128, -s[3]),) + tuple(slice(x[0], x[1], x[2] if x[2] != 1 else None) if isinstance(x, tuple) else x for x in s[2])]
     if s[0] == "d":
         return T[s[1]][:] if s[2] is None else T[s[1]][:, s[2]:s[3]]
     return real(T, s[1]).indirect(real(T, s[2]))
 
 
 def count(s):
-    if s[0] == "2":
-        return len(range(s[2], s[3], s[4]))
-    if s[0] == "3":
-        return (s[4] - s[3]) * (3 if s[2] is None else 1)
-    return 16 * count(s[2])
+    if s[0] == "i":
+        return 16 * count(s[2])
+    n = 1
+    for x in s[2]:
+        if isinstance(x, tuple):
+            n *= len(range(*x))
+    return n
 
 
 def spans(s):
     if not isinstance(s, tuple) or s[0] == "d":
         return []
-    if s[0] == "2":
-        return [(s[1], s[2], s[3])]
-    if s[0] == "3":
-        return [(s[1], s[3], 128 + s[4])] if s[2] is None else [(s[1], 64 * s[2] + s[3], 64 * s[2] + s[4])]
-    return spans(s[1]) + spans(s[2])
+    if s[0] == "i":
+        return spans(s[1]) + spans(s[2])
+    shape = SCRATCH[s[1]][1][1:]
+    at = [0]
+    for x, n in zip(s[2][:-1], shape):
+        at = [v * n + r for v in at for r in (range(*x) if isinstance(x, tuple) else [x])]
+    x = s[2][-1]
+    r = range(*x) if isinstance(x, tuple) else [x]
+    runs = []
+    for v in at:
+        lo, hi = v * shape[-1] + r[0], v * shape[-1] + r[-1] + 1
+        if runs and runs[-1][2] == lo:
+            runs[-1] = (s[1], runs[-1][1], hi)
+        else:
+            runs.append((s[1], lo, hi))
+    return runs
 
 
 def where(s):
@@ -107,13 +124,14 @@ def where(s):
 
 def width(s):
     n = s[1] if s[0] != "i" else s[1][1]
-    return 2 if SCRATCH[n][2] in ("bfloat16", "uint16") else 4
+    return 2 if SCRATCH[n][2] in ("bfloat16", "uint16", "float16") else 4
 
 
 def build(cfg):
     ops = []
     tag = ["setup"]
-    CYC, PEC, GA, SCA, FIX = cfg.get("cyc", 1.0), cfg.get("pec", 0.55), cfg.get("ga", 1.56), cfg.get("sca", 3.8), cfg["fix"]
+    CYC, PEC, GA, SCA, FIX = cfg["cyc"], cfg["pec"], cfg.get("ga", 1.56), cfg.get("sca", 3.8), cfg["fix"]
+    FL, VF = cfg.get("fl", 64), cfg.get("vf", 0)
 
     def add(eng, call, outs, ins, cost, sem=None, lat=0.0):
         wr, rd = [], []
@@ -138,7 +156,7 @@ def build(cfg):
             f = 2.0 if all(where(s) == "sbuf" for s in ins) else 1.0
         else:
             f = 0.5 if all(width(s) == 2 for s in [out] + ins) else 1.0
-        return max(64, n * f) * CYC
+        return (VF + max(FL, n * f)) * CYC
 
     def cp(out, in_):
         add("V", lambda q, T: q.tensor_copy(real(T, out), real(T, in_)), [out], [in_], vcost(out, [in_]))
@@ -154,11 +172,11 @@ def build(cfg):
         add("V", call, [out], [x] + [s for s in (s1, s2) if isinstance(s, tuple)], vcost(out, [x]))
 
     def ms(out, v):
-        add("V", lambda q, T: q.memset(real(T, out), v), [out], [], max(64, count(out) * width(out) / 4) * CYC)
+        add("V", lambda q, T: q.memset(real(T, out), v), [out], [], (VF + max(FL, count(out) * width(out) / 4)) * CYC)
 
     def act(out, in_, func=ACT.Identity, bias=0.0, scale=1.0):
         n = count(out)
-        c = 65 + GA * n * CYC if in_[0] == "i" else max(64, n) * CYC
+        c = 65 + GA * n * CYC if in_[0] == "i" else (VF + max(FL, n)) * CYC
         if bias == 0.0 and func == ACT.Identity:
             func = ACT.Copy
         if func == ACT.Copy:
@@ -189,47 +207,59 @@ def build(cfg):
                 [out], [], 130 + 2 * count(out) * CYC)
 
     def dma(out, in_, sem, nbytes, eng="S"):
-        add(eng, lambda q, T: q.dma_start(real(T, out), real(T, in_)), [out], [in_], 60, sem, 1800 + nbytes / 150.0)
+        add(eng, lambda q, T: q.dma_start(real(T, out), real(T, in_)), [out], [in_], 60, sem, 1500 + nbytes / 300.0)
 
     def transpose(tr):
-        add("V", lambda q, T: q.transpose(T[tr][:, 256:512], T[tr][:, 0:256]), [a(tr, 256, 512)], [a(tr, 0, 256)], 256 * CYC)
+        add("V", lambda q, T: q.transpose(T[tr][:, 256:512], T[tr][:, 0:256]), [a(tr, 256, 512)], [a(tr, 0, 256)], (VF + 256) * CYC)
 
     def zwin(name, b, p=128):
         return a(name, 15 - b, 143 - b, 1, p)
 
+    def send(dsts, srcs, sem):
+        add("G", ("send", dsts, srcs), dsts, srcs, cfg.get("gc", 250), sem, cfg["wire"])
+
+    def zone(t):
+        return 144 if t % 2 else -8
+
     dma(a("RI", 0, 256), dram("rl"), "ldR", 131072, "A")
-    dma(a("X0", 0, W), dram("xt"), "ldX0", 600000)
+    dma(a("X0", X0, X0 + W), dram("xt"), "ldX0", 600000)
     dma(a("wI", 0, 1), dram("wt"), "ldW", 512, "A")
     dma(a("sgI", 0, 256, 1, 8), dram("sg"), "ldS", 8192, "A")
     for h in ORDER:
-        dma(a("LB0%d" % h, 0, 128), dram("av", 128 * h, 128 * h + 128), "ldA%d" % h, 32768)
-        dma(a("LB0%d" % h, 128, 256), dram("av", 128 * h, 128 * h + 128), "ldB%d" % h, 32768)
+        dma(a("LB0%d" % h, 0, 128), dram("av", 128 * h, 128 * h + 128), "ldA%d" % h, 400000)
+        dma(a("LB0%d" % h, 128, 256), dram("av", 128 * h, 128 * h + 128), "ldB%d" % h, 400000)
     iota(a("pI", 0, 1), [[0, 1]], 0, 1)
     col = lambda j: a("pF", j, j + 1)
-    PP, PR, PR7, PG, P31, P16, PR3, PRH, PR1, PW, PN, PD, PT = range(13)
+    PP, PR, PR7, PG, P31, P16, PR3, PRH, PR1, PW, PN, PK, PT = range(13)
     for j, (sh, mk) in enumerate(((0, 15), (0, 7), (4, 7), (0, 31), (0, 16), (2, 2), (1, 7), (0, 1))):
         ts(a("pI", j + 1, j + 2), a("pI", 0, 1), sh, ALU.arith_shift_right, mk, ALU.bitwise_and)
     cp(a("pF", 0, 9), a("pI", 0, 9))
     cp(col(PW), a("wI", 0, 1))
     ts(col(13), col(PR7), 32.0, ALU.mult, col(P16), ALU.add)
     ts(col(PN), col(13), col(PR3), ALU.add)
-    ts(col(PD), col(PR), 2049.0, ALU.add)
     ts(col(14), col(PR1), -8.0, ALU.mult, col(PRH), ALU.add)
     ts(col(PT), col(14), 8.0, ALU.add, 8.0, ALU.mult)
-    DUP, N2T, BCB, BCK, T2W, W2N = (a("lst", 0, 32), a("lst", 32, 40), a("lst", 40, 48), a("lst", 48, 56),
-                                    a("lst", 64, 80), a("lst", 80, 88))
+    DUP, N2T, BCB, T2W, W2N, BCK = (a("lst", 0, 32), a("lst", 32, 40), a("lst", 40, 48), a("lst", 64, 80), a("lst", 80, 88),
+                                    a("lst", 96, 105))
     for lst, pat, base, c in ((DUP, [[16, 16], [0, 2]], 0, PR), (N2T, [[-1, 2], [4, 4]], 1, PN), (BCB, [[1, 8]], 0, None),
-                              (BCK, [[0, 8]], 0, PR7), (T2W, [[1, 8], [0, 2]], 0, PT), (W2N, [[32, 8]], 0, P31)):
-        src = a("ci", lst[2], lst[3])
+                              (T2W, [[1, 8], [0, 2]], 0, PT), (W2N, [[32, 8]], 0, P31)):
+        lo, hi = lst[2][0][:2]
+        src = a("ci", lo, hi)
         iota(src, pat, base)
         if c is None:
             cp(lst, src)
         else:
             ts(lst, src, col(c), ALU.add)
+    iota(a("ci", 96, 104), [[0, 8]])
+    ts(a("lst", 96, 104), a("ci", 96, 104), col(PR7), ALU.add)
+    ts(a("lst", 104, 105), col(PR), 8.0, ALU.min)
     iota(a("ci", 88, 96), [[16, 8]])
     for h in ORDER:
-        ts(a("sf%d" % h, 0, 8), a("ci", 88, 96), col(PR), ALU.add, -128.0 if "s" in cfg["opt"][h] else 0.0, ALU.add)
+        ts(a("sf%d" % h, 0, 8), a("ci", 88, 96), col(PR), ALU.add, -128.0, ALU.add)
+        ms(a("sf%d" % h, 136, 168), -5.0)
         ms(a("wb%d" % h, 1536, 1552), 0.0)
+        for t in range(NS - 1):
+            cp(a("LF%d%d" % (t, h), zone(t + 1), zone(t + 1) + 8), a("wb%d" % h, 1536, 1544))
     IB, IG, IC = a("ci", 128, 256), a("ci", 256, 384), a("ci", 384, 512)
     iota(IB, [[0, 8], [1, 16]])
     iota(IG, [[1, 8], [0, 16]])
@@ -239,18 +269,32 @@ def build(cfg):
     ms(a("Zn", 0, 144), 0.0)
     ts(a("Zw", 15, 143, 16), a("G8", 0, 8), col(PW), ALU.mult)
     ts(a("Zn", 15, 143, 16), a("G8", 0, 8), -4096.0, ALU.mult)
-    ts(a("I1", 0, 128), IC, col(PP), ALU.is_equal)
-    ts(a("I24", 0, 128), a("I1", 0, 128), 8388608.0 if "P" in cfg["fo"] else 16777216.0, ALU.mult)
-    if "D" in cfg["fo"]:
-        act(a("If", 0, 128), a("I1", 0, 128))
-        act(a("If", 128, 256), a("I1", 0, 128), scale=-1.0)
-    ts(a("In", 0, 128), a("I1", 0, 128), -1.0, ALU.mult)
+    I1, IN = a("I1", 0, 128), a("In", 0, 128)
+    ts(I1, IC, col(PP), ALU.is_equal)
+    IF, IFP, IFN = a("If", 0, 128), a("If", 128, 256), a("If", 256, 384)
+    I4N, IKP, IKN = a("Ik", 0, 128), a("Ik", 128, 256), a("Ik", 256, 384)
+    IFM, IFH = IN, a("If", 384, 512)
+    for o, v in ((IFP, 1.0 / 256), (IFN, -1.0 / 256), (IFH, -0.5), (I4N, -4.0), (IKN, -1024.0), (IKP, -BIG),
+                 (a("I23", 0, 128), 8388608.0), (IN, -1.0)):
+        act(o, I1, scale=v)
+    IF = I1
+    CD, CR, CK, CX = [a("CC", 128 * j, 128 * j + 128, 1, 2) for j in range(4)]
+    for lo, v0, v1 in ((0, 4.0, 0.0), (128, 0.0, -255.0 / 512), (256, 8388608.0, -1024.0), (384, BIG, -float(X0))):
+        ms(a("CC", lo, lo + 128, 1, 2), v1)
+        if v0 != v1:
+            ms(a("CC", lo, lo + 128, 1, 1), v0)
     ts(a("sameB", 0, 128), IB, col(PR), ALU.is_equal)
     ts(a("blk", 0, 128), IG, col(PG), ALU.is_equal, 2.0 ** -12, ALU.mult)
-    if "r" in cfg["opt"][0] + cfg["opt"][1]:
-        ts(a("nblk", 0, 128), a("blk", 0, 128), -1.0, ALU.mult)
+    act(a("nblk", 0, 128), a("blk", 0, 128), scale=-1.0)
+    if "n" in cfg["opt"][0] + cfg["opt"][1]:
+        act(a("If", 0, 128), I1, scale=-1.0 / 8)
+        mm([(a("E1", 0, 128), I1, a("blk", 0, 128), True, False), (a("E1", 0, 128), IFP, a("If", 0, 128), False, True)])
+        act(a("MB", 2048, 2176), a("E1", 0, 128), scale=4096.0)
+        act(a("MB", 2176, 2192), a("sameB", 0, 16), bias=-1.0)
+        for b in range(16):
+            ts(a("MB", 128 * b, 128 * b + 128), a("MB", 2048, 2176), a("MB", 2176 + b, 2177 + b), ALU.max, a("sameB", b, b + 1), ALU.min)
     ts(a("mask", 0, 128), IB, col(PR), ALU.is_gt, -1.0, ALU.mult)
-    ts(a("d0", 0, 128), IB, col(PR), ALU.not_equal, 1.0 / 32, ALU.max)
+    ts(a("d0", 0, 128), a("sameB", 0, 128), -33.0 / 32, ALU.mult, 1.0, ALU.add)
     ms(a("d0", 0, 128, 16), 0.0)
     ms(a("ones", 0, 144), 1.0)
     add("G", lambda q, T: q.affine_select(T["Z8"][0:8, 0:144], T["ones"][0:8, 0:144], [[1, 144]], ALU.is_equal, 0.0, -15, -16),
@@ -258,281 +302,307 @@ def build(cfg):
     ms(a("pm", 0, 1), -1.0)
     ms(a("pm", 1, 16), 1.0)
     for x in ("X0", "X1"):
-        ms(a(x, W, 2080), 4096.0)
-    iota(a("iota", 0, 2056), [[2, 2056]])
+        ms(a(x, X0 + VOID, X0 + VOID + 16), 4096.0)
+        ms(a(x, 0, X0), 0.0)
+    iota(a("iota", 0, VOID + 8), [[2, VOID + 8]])
     cp(a("sgB", 0, 256, 1, 8), a("sgI", 0, 256, 1, 8))
     mm([(a("E0", 0, 16), zwin("Z8", b, 8), a("sgB", b, 256, 16, 8), b == 0, b == 15) for b in range(16)])
     for h in ORDER:
         tr = "tr%d" % h
-        ms(a("S%d" % h, 264, 272), -1.0)
         cp(a(tr, 0, 256), ind(a("RI", 0, 256), a("lst", 16 * h, 16 * h + 16)))
         transpose(tr)
         cp(a("LF0%d" % h, 0, 128), ind(a(tr, 256, 512), N2T))
-        act(a("OF0%d" % h, -8, 0), a("E0", 8 * h, 8 * h + 8), scale=1.0 if "c" in cfg["opt"][h] else 2.0)
+        cp(a("LF0%d" % h, 128, 136), a("LF0%d" % h, 64, 72))
+        ts(a("LF0%d" % h, 136, 144), a("E0", 8 * h, 8 * h + 8), 1.0 if cfg["sg"][h] == "A" else 2.0, ALU.mult)
 
     def names(t, h):
         return ("LF%d%d" % (t, h), "LB%d%d" % (t, h), "P%d" % h, "Q%d" % h, "S%d" % h, "u16%d" % h, "wi%d" % h,
                 "wb%d" % h, "X%d" % (t % 2))
 
-    def flip(h, out, new, old, sg):
-        f8 = lambda j, n=1: a("sf%d" % h, 8 * j, 8 * (j + n))
-        tt(f8(20, 2), new, old, ALU.is_equal)
-        tt(f8(22), f8(20), f8(21), ALU.max)
-        act(f8(23), f8(22), bias=-1.0, scale=2.0)
-        tt(out, f8(23), sg, ALU.mult)
-
-    def send(dst, src, sem):
-        add("G", ("send", dst, src), [dst], [src], 250, sem, cfg["wire"])
-
     def front(t, h):
         tag[0] = "f%d%d" % (t, h)
         LF, LB, P, Q, S, U, WI, WB, X = names(t, h)
         XR, D, AD, KB = "XR%d" % h, "D%d" % h, "AD%d" % h, "KB%d" % h
-        win = a(X, 0, W + 1)
         NXT = (72, 0)
         cp(a(U, 0, 128), a(LF, 0, 128))
-        fo, TBO = cfg["fo"], 1280
-        act(a(LF, 128, 136), a(LF, 64, 72), bias=2048.0)
-        act(a(S, 0, 136), a(LF, 0, 136))
-        OF = "OF%d%d" % (t, h)
-        if t > 0:
-            flip(h, a(OF, -8, 0), a(LF, 24, 40), a(LF, -24, -8), a(LF, -8, 0))
-        if t < NS - 1:
-            act(a(OF, -24, -8), a(LF, 24, 40))
-        if "D" in fo:
-            mm([x for f in (0, 1) for x in
-                ((a(S, 136 + 64 * f, 200 + 64 * f), a("If", 0, 128), a(LF, NXT[f], NXT[f] + 64), True, False),
-                 (a(S, 136 + 64 * f, 200 + 64 * f), a("If", 128, 256), a(LF, 64 * f, 64 * f + 64), False, True))])
-        else:
-            for f in (0, 1):
-                tt(a(S, 136 + 64 * f, 200 + 64 * f), a(S, NXT[f], NXT[f] + 64), a(LF, 64 * f, 64 * f + 64), ALU.subtract)
-        if t > 0:
-            mm([(a(P, 256 + 8 * k, 264 + 8 * k), a("sameB", 0, 128), a(LB, 256, 264), True, True) for k in range(16)])
+        SGN, DD, RR, ones2 = a(WB, 1280, 1408), a(S, 0, 128), a(S, 128, 256), a("ones", 0, 128, 1, 2)
+        raw = lambda o, f, end: [(a(S, o + 64 * f, o + 64 + 64 * f), IFP, a(LF, NXT[f], NXT[f] + 64), True, False),
+                                 (a(S, o + 64 * f, o + 64 + 64 * f), IFN, a(LF, 64 * f, 64 * f + 64), False, end)]
+        mm(raw(256, 0, True) + raw(256, 1, True))
+        act(SGN, a(S, 256, 384), ACT.Sign)
+        mm([x for f in (0, 1) for x in raw(0, f, False)
+            + [(a(S, 64 * f, 64 * f + 64), I4N, a(WB, 1280 + 64 * f, 1344 + 64 * f), False, False),
+               (a(S, 64 * f, 64 * f + 64), CD, a("ones", 0, 64, 1, 2), False, True)]])
+        mm([(RR, IF, a(LF, 0, 128), True, False), (RR, CR, ones2, False, True)])
         for f in (0, 1):
             e = cfg["aeng"][(h, f)]
-            n = cfg["asplit"] if len(e) == 1 else len(e)
-            for j in range(n):
-                c, w = 64 * f + j * 64 // n, 64 // n
-                gat(e[j % len(e)], a(XR, 16 * c, 16 * (c + w)), ind(win, a(U, c, c + w)))
-        withn = t > 0 and "N" in fo
-        if withn:
-            act(a(WB, TBO, TBO + 128), a(P, 256, 384))
+            for j in range(len(e)):
+                w = 64 // len(e)
+                c = 64 * f + j * w
+                gat(e[j], a(XR, 16 * c, 16 * (c + w)), ind(a(X, X0, X0 + W), a(U, c, c + w)))
+        TB = a(WB, 1552, 1616)
+        if t > 0:
+            mm([(a(Q, 384 + 8 * k, 392 + 8 * k), a("sameB", 0, 128), a(LF, zone(t), zone(t) + 8), True, True) for k in range(8)])
+            act(TB, a(Q, 384, 448))
         for f in (0, 1):
             o = a(P, 64 * f, 64 * f + 64)
-            mm(([(o, a("I1", 0, 128), a(WB, TBO + 64 * f, TBO + 64 * f + 64), True, False)] if withn else [])
-               + [(o, zwin("Zw", b), a(XR, 1024 * f + b, 1024 * f + 1024, 16), b == 0 and not withn, b == 15) for b in range(16)])
-        UI, UU, W1, W2, W3, W4, W5, W6, QQ = 0, 128, 272, 400, 528, 656, 784, 912, 1040
+            mm([(o, zwin("Zw", b), a(XR, 1024 * f + b, 1024 * f + 1024, 16), b == 0, b == 15 and t == 0) for b in range(16)]
+               + ([(o, I1, TB, False, True)] if t > 0 else []))
+        UI, UU, W1, W2, W3, W4, QQ = 0, 128, 272, 400, 528, 656, 1040
         parts = ((0, 64), (64, 128)) if cfg["split"][h] else ((0, 128),)
         wi = lambda b, p: a(WI, b + p[0], b + p[1])
-        for p in parts:
-            if withn:
-                tt(wi(UI, p), a(P, p[0], p[1]), a(WB, TBO + p[0], TBO + p[1]), ALU.subtract)
+        for p in ((0, 64), (64, 128)):
+            if t > 0:
+                tt(wi(UI, p), a(P, p[0], p[1]), TB, ALU.subtract)
             else:
                 cp(wi(UI, p), a(P, p[0], p[1]))
+        for p in parts:
             ts(wi(UU, p), wi(UI, p), 4095, ALU.bitwise_and)
         for lo, hi, nx in ((64, 128, 0), (0, 56, 72), (56, 64, 64)):
             tt(a(WI, W1 + lo, W1 + hi), a(WI, UU + lo, UU + hi), a(WI, UU + nx, UU + nx + hi - lo), ALU.mult)
         for p in parts[::-1]:
             ts(wi(W2, p), wi(W1, p), 5, ALU.arith_shift_right)
             tt(wi(W3, p), wi(W2, p), a(P, p[0], p[1]), ALU.add)
-            if t > 0 and "N" not in fo:
-                tt(wi(W3, p), wi(W3, p), a(P, 256 + p[0], 256 + p[1]), ALU.add)
             ts(wi(W4, p), wi(W3, p), 255, ALU.bitwise_and)
-            if "P" in fo:
-                dh = a("wf%d" % h, 384 + p[0], 384 + p[1])
-                tt(dh, wi(W4, p), a(S, 136 + p[0], 136 + p[1]), ALU.mult)
-                ts(wi(W6, p), dh, 1.0 / 256, ALU.mult, -0.498046875, ALU.add)
-                act(a(WB, p[0], p[1]), dh, ACT.Sign, bias=255.5, scale=-1.0)
-            else:
-                tt(wi(W5, p), wi(W4, p), a(S, 136 + p[0], 136 + p[1]), ALU.mult)
-                ts(wi(W6, p), wi(W5, p), 8, ALU.arith_shift_right)
-                ts(a(WB, p[0], p[1]), wi(W6, p), 0.0, ALU.is_equal)
-            tt(wi(QQ, p), wi(W6, p), a(S, p[0], p[1]), ALU.add)
-            if p[1] == 128:
-                cp(a(U, 192, 256), a(WI, QQ + 64, QQ + 128))
-            if p[0] == 0:
-                ts(a(WI, W1, W1 + 64), a(WI, QQ, QQ + 64), 2047, ALU.bitwise_and)
-                cp(a(U, 128, 192), a(WI, W1, W1 + 64))
+            dh = a("wf%d" % h, 384 + p[0], 384 + p[1])
+            tt(dh, wi(W4, p), a(S, p[0], p[1]), ALU.mult)
+            tt(wi(QQ, p), dh, a(S, 128 + p[0], 128 + p[1]), ALU.add)
+            if t > 0 or p[0] == 0:
+                ts(wi(QQ, p), wi(QQ, p), W - 1, ALU.bitwise_and)
+            cp(a(U, 128 + p[0], 128 + p[1]), wi(QQ, p))
+            act(a(WB, p[0], p[1]), dh, ACT.Sign, bias=255.5 / 256, scale=-1.0)
+        win = a(X, X0, X0 + VOID)
         AA = a(LB, 0, 256)
         for f in (1, 0):
             mode = cfg["bmode"][(h, f)]
             o = 1024 * f
             for j in (0, 1):
-                md = mode[j % len(mode)]
-                x, y, c = a(AD, o + 512 * j, o + 512 * j + 512), a(D, o + 512 * j, o + 512 * j + 512), 128 + 64 * f + 32 * j
+                md = mode[j]
+                lo = o + 512 * j
+                x, y, c = a(AD, lo, lo + 512), a(D, lo, lo + 512), 128 + 64 * f + 32 * j
                 if md == "Z":
-                    if len(mode) == 2 or cfg["zsplit"] == 2:
-                        act(y, ind(win, a(U, c, c + 32)), scale=-1.0)
-                    elif j == 0:
-                        act(a(D, o, o + 1024), ind(win, a(U, c, c + 64)), scale=-1.0)
+                    act(y, ind(win, a(U, c, c + 32)), scale=-1.0)
                     e = "E%d" % j
-                    mm([(a(e, 0, 512), a("I1", 0, 128), y, True, False),
-                        (a(e, 0, 256), a("I1", 0, 128), AA, False, False),
-                        (a(e, 256, 512), a("I1", 0, 128), AA, False, True)])
+                    mm([(a(e, 0, 512), I1, y, True, False), (a(e, 0, 256), I1, AA, False, False),
+                        (a(e, 256, 512), I1, AA, False, True)])
                     act(x, a(e, 0, 512), ACT.Abs)
                 else:
                     for i in (0, 1):
-                        tt(a(D, y[2] + 256 * i, y[2] + 256 * i + 256), ind(win, a(U, c + 16 * i, c + 16 * i + 16)), AA, ALU.subtract)
+                        tt(a(D, lo + 256 * i, lo + 256 * i + 256), ind(win, a(U, c + 16 * i, c + 16 * i + 16)), AA, ALU.subtract)
                     if md == "W":
                         ts(x, y, 0.0, ALU.min, -2.0, ALU.mult)
                     else:
                         act(x, y, ACT.Abs)
             kb, ko = (Q, 0) if f == 0 else (P, 128)
             K = a(kb, ko, ko + 64)
-            it = [(K, a("I24", 0, 128), a(WB, 64 * f, 64 * f + 64), True, False)]
-            if "P" in fo:
-                it += [(K, a("I24", 0, 128), a("ones", 0, 64), False, False)]
-            if mode == "W":
-                it += [(K, zwin("Zn", b), a(D, o + b, o + 1024, 16), False, False) for b in range(16)]
-            else:
-                for j in range(len(mode)):
-                    if mode[j] == "W":
-                        it += [(a(kb, ko + 32 * j, ko + 32 * j + 32), zwin("Zn", b), a(D, o + 512 * j + b, o + 512 * j + 512, 16),
-                                False, False) for b in range(16)]
-            it += [(K, zwin("Zn", b), a(AD, o + b, o + 1024, 16), False, b == 15) for b in range(16)]
+            it = [(K, a("I23", 0, 128), a(WB, 64 * f, 64 * f + 64), True, False), (K, CK, a("ones", 0, 64, 1, 2), False, False),
+                  (K, IKN, a(WB, 1280 + 64 * f, 1344 + 64 * f), False, False)]
             mm(it)
+            if mode == "WW":
+                mm([(K, zwin("Zn", b), a(D, o + b, o + 1024, 16), False, False) for b in range(16)])
+            else:
+                for j in (0, 1):
+                    if mode[j] == "W":
+                        mm([(a(kb, ko + 32 * j, ko + 32 * j + 32), zwin("Zn", b), a(D, o + 512 * j + b, o + 512 * j + 512, 16),
+                             False, False) for b in range(16)])
+            mm([(K, zwin("Zn", b), a(AD, o + b, o + 1024, 16), False, b == 15) for b in range(16)])
             ev = a(LF, 72, 136) if f == 0 else a(LF, 64, 128)
             for j, pay in enumerate((a(WI, QQ + 64 * f, QQ + 64 * f + 64), ev, a(LF, 0, 64))):
-                tt(a3(KB, j, 0, 64) if f == 1 else a(S, 272 + 64 * j, 336 + 64 * j), K, pay, ALU.add)
+                tt(nd(KB, j, None) if f == 1 else a(S, 272 + 64 * j, 336 + 64 * j), K, pay, ALU.add)
 
     def back(t, h):
         tag[0] = "b%d%d" % (t, h)
         LF, LB, P, Q, S, U, WI, WB, X = names(t, h)
-        KB, SI, SF, WF = "KB%d" % h, "si%d" % h, "sf%d" % h, "wf%d" % h
+        KB, SI, SF, WF, VB, SC = ["%s%d" % (x, h) for x in ("KB", "si", "sf", "wf", "VB", "SC")]
         OF, OB, XN = "OF%d%d" % (t, h), "OB%d%d" % (t, h), "X%d" % ((t + 1) % 2)
-        win = a(X, 0, W + 1)
+        win = a(X, X0, X0 + VOID + 1)
         A0 = a(LB, 0, 128)
         f8 = lambda j, n=1: a(SF, 8 * j, 8 * (j + n))
-        tt(a3(KB, None, 0, 64), a3(KB, None, 0, 64), a(S, 272, 464), ALU.min)
-        tt(a3(KB, None, 0, 32), a3(KB, None, 0, 32), a3(KB, None, 32, 64), ALU.min)
-        tt(a3(KB, None, 0, 16), a3(KB, None, 0, 16), a3(KB, None, 16, 32), ALU.min)
-        tt(a(SI, 0, 24), a3(KB, None, 0, 8), a3(KB, None, 8, 16), ALU.min)
+        tt(nd(KB, None, None), nd(KB, None, None), a(S, 272, 464), ALU.min)
+        tt(nd(KB, None, (0, 32)), nd(KB, None, (0, 32)), nd(KB, None, (32, 64)), ALU.min)
+        tt(nd(KB, None, (0, 16)), nd(KB, None, (0, 16)), nd(KB, None, (16, 32)), ALU.min)
+        tt(a(SI, 0, 24), nd(KB, None, (0, 8)), nd(KB, None, (8, 16)), ALU.min)
         ts(a(SI, 24, 48), a(SI, 0, 24), 2047, ALU.bitwise_and)
         cp(a(U, 256, 264), a(SI, 24, 32))
-        DQ, GT, AQ, DL, RL, NE, VAL, SC, CL, TB, CQ = [a(WB, 128 * j, 128 * j + 128) for j in range(1, 12)]
-        tt(DQ, ind(win, a(U, 256, 264)), A0, ALU.subtract)
-        opt = cfg["opt"][h]
-        if "g" in opt:
+        DQ, GT, AQ, DL, RL, NE, CL, TB = [a(WB, 128 * j, 128 * j + 128) for j in range(1, 9)]
+        CQ = a(WB, 1408, 1536)
+        XQ, XL, C1, C2, SS, R1, R2 = [a(WB, 1664 + 128 * j, 1792 + 128 * j) for j in range(7)]
+        YA, HH = a(WB, 2560, 2704), "hh%d" % h
+        qw = ind(a(X, X0, X0 + W), a(U, 256, 264))
+        gt, opt = cfg["gt"][h], cfg["opt"][h]
+        if gt == "G":
+            tt(GT, qw, A0, ALU.is_gt)
+        if "q" in opt:
+            act(XQ, qw)
+            DQ = a(Q, 256, 384)
+            mm([(DQ, I1, XQ, True, False), (DQ, IN, A0, False, True)])
+        else:
+            tt(DQ, qw, A0, ALU.subtract)
+        if gt == "A":
             act(GT, DQ, ACT.Sign, bias=-0.5)
-        else:
-            ts(GT, DQ, 0.0, ALU.is_gt, 0.5, ALU.subtract)
-        mm([(a(P, 384, 392), zwin("Zn", b), a(WB, 256 + b, 384, 16), b == 0, b == 15) for b in range(16)])
+        elif gt == "V":
+            ts(GT, DQ, 0.0, ALU.is_gt)
+        thr = 1024.0 if gt == "A" else -7.5 * 4096
         act(AQ, DQ, ACT.Abs)
-        ts(f8(5, 3), a(SI, 0, 24), 0.0, ALU.is_ge, 2048.0, ALU.mult)
-        tt(f8(2, 3), a(SI, 24, 48), f8(5, 3), ALU.max)
-        EV, OD, SG, L = f8(3), f8(4), a(OF, -8, 0), f8(1)
-        tt(f8(8), EV, OD, ALU.subtract)
-        tt(f8(9), f8(8), SG, ALU.mult)
-        tt(f8(10), EV, OD, ALU.add)
-        if "c" in opt:
-            act(f8(11), a(P, 384, 392), ACT.Sign, bias=1024.0, scale=-1.0)
+        if "v" not in opt:
+            ts(CQ, DQ, -2.0, ALU.max, 2.0, ALU.min)
+        ts(f8(5, 3), a(SI, 0, 24), 8192.0, ALU.is_ge, float(VOID), ALU.mult)
+        tt(a(HH, 0, 24), a(SI, 24, 48), f8(5, 3), ALU.max)
+        QH, EV, OD, L2H = [a(HH, 8 * j, 8 * j + 8) for j in range(4)]
+        SG, L2, LL, DE, DF, SM = a(LF, 136, 144), f8(1), f8(17), f8(19), f8(8), f8(10)
+        if "s" in opt:
+            DF, SM = a(P, 392, 400), a(P, 400, 408)
+            mm([(DF, IF, EV, True, False), (DF, IFM, OD, False, True), (SM, IF, EV, True, False), (SM, IF, OD, False, True)])
         else:
-            ts(f8(11), a(P, 384, 392), 1024.0, ALU.is_lt, 0.5, ALU.subtract)
+            tt(DF, EV, OD, ALU.subtract)
+            tt(SM, EV, OD, ALU.add)
+        tt(f8(9), DF, SG, ALU.mult)
+        mm([(a(P, 384, 392), zwin("Zn", b), a(WB, 256 + b, 384, 16), b == 0, b == 15) for b in range(16)])
+        if cfg["sg"][h] == "A":
+            act(f8(11), a(P, 384, 392), ACT.Sign, bias=thr, scale=-1.0)
+        else:
+            ts(f8(11), a(P, 384, 392), thr, ALU.is_lt, 0.5, ALU.subtract)
         tt(f8(12), f8(11), f8(9), ALU.mult)
-        tt(L, f8(12), f8(10), ALU.add)
-        ts(a(U, 264, 272), L, 0.5, ALU.mult)
-        tt(DL, ind(win, a(U, 264, 272)), A0, ALU.subtract)
-        E = a(P, 256, 384)
-        it = [(E, a("I1", 0, 128), a("mask", 0, 128), True, False), (E, a("blk", 0, 128), AQ, False, False)]
-        if "r" in opt:
+        wide, narrow = not all(x in opt for x in "nexs"), any(x in opt for x in "nexs")
+        if wide:
+            tt(L2, f8(12), SM, ALU.add)
+        if narrow:
+            tt(L2H, f8(12), SM, ALU.add)
+        ts(a(U, 264, 272), L2 if wide else L2H, 0.5, ALU.mult)
+        lw = ind(win, a(U, 264, 272))
+        if "l" in opt:
+            act(XL, lw)
+            DL = a(S, 0, 128)
+            mm([(DL, I1, XL, True, False), (DL, IN, A0, False, True)])
+        else:
+            tt(DL, lw, A0, ALU.subtract)
+        if "n" in opt:
+            mm([(a(Q, 384 + b, 512, 16), a("MB", 128 * b, 128 * b + 128), L2H, True, True) for b in range(16)])
+            act(NE, a(Q, 384, 512), ACT.Abs)
+        else:
+            act(a(WF, 0, 128), ind(L2, BCB))
+            tt(NE, ind(a("iota", 0, VOID + 8), a(U, 264, 272)), a(WF, 0, 128), ALU.not_equal)
+        BLK, NBLK = a("blk", 0, 128), a("nblk", 0, 128)
+        if cfg["rl"][h] == "A" or "l" in opt:
             act(RL, DL, ACT.Abs)
-            mm(it + [(E, a("nblk", 0, 128), RL, False, True)])
+            margin = lambda o, st: [(o, BLK, AQ, st, False), (o, NBLK, RL, False, True)]
         else:
             ts(RL, DL, 0.0, ALU.max, -2.0, ALU.mult)
-            mm(it + [(E, a("blk", 0, 128), DL, False, False), (E, a("blk", 0, 128), RL, False, True)])
-        act(a(WF, 0, 128), ind(L, BCB))
-        tt(NE, ind(a("iota", 0, 2056), a(U, 264, 272)), a(WF, 0, 128), ALU.not_equal)
-        tt(VAL, E, NE, ALU.is_gt)
-        add("V", lambda q, T: q.tensor_tensor_scan(real(T, SC), T["d0"][:, 0:128], real(T, VAL), 0.0, ALU.mult, ALU.add),
-            [SC], [VAL, a("d0", 0, 128)], 64 * CYC)
-        FIN = a(WB, SC[2] + 15, SC[3], 16)
-        if "n" in opt:
-            act(f8(13), FIN, ACT.Abs, bias=-262144.0, scale=262144.0)
+            margin = lambda o, st: [(o, BLK, AQ, st, False), (o, BLK, DL, False, False), (o, BLK, RL, False, True)]
+        E = a(P, 256, 384)
+        mm([(E, I1, a("mask", 0, 128), True, False)] + margin(E, False) + (margin(a(P, 0, 128), True) if "v" in opt else []))
+        if "e" not in opt or "s" not in opt:
+            act(LL, L2, scale=0.5)
+        if "x" not in opt:
+            act(f8(14), L2, bias=X0 / BIG - 1.0, scale=0.5 / BIG)
+        tt(a(VB, 0, 128), E, NE, ALU.is_gt)
+        add("V", lambda q, T: q.tensor_tensor_scan(T[SC][:, 0:128], T["d0"][:, 0:128], T[VB][:, 0:128], 0.0, ALU.mult, ALU.add),
+            [a(SC, 0, 128)], [a(VB, 0, 128), a("d0", 0, 128)], (VF + 64) * CYC)
+        FIN = a(SC, 15, 128, 16)
+        DD = a(P, 408, 416) if "s" in opt else f8(13)
+        it = [(DD, IF, QH, True, False), (DD, IFH, L2H, False, True)] if "s" in opt else []
+        if "x" in opt:
+            XX = a(P, 416, 424)
+            mm(it + [(XX, CX, a("ones", 0, 8, 1, 2), True, False), (XX, IFH, L2H, False, False), (XX, IKP, FIN, False, True)])
+            ts(a(U, 288, 304, 2), XX, -1.0, ALU.mult, col(PR), ALU.max)
         else:
-            ts(f8(13), FIN, 1.0, ALU.not_equal, 8192.0, ALU.mult)
-        tt(f8(14), f8(13), L, ALU.add)
-        ts(a(U, 288, 304, 2), f8(14), 0.5, ALU.mult, col(PD), ALU.min)
-        ts(CL, DL, -8.0, ALU.max, 8.0, ALU.min)
-        B = a(Q, 128, 256)
-        mm([(B, a("I1", 0, 128), A0, True, False), (B, a("I1", 0, 128), DL, False, False), (B, a("In", 0, 128), CL, False, True)])
+            if it:
+                mm(it)
+            tt(f8(15), FIN, f8(14), ALU.add)
+            ts(a(U, 288, 304, 2), f8(15), BIG, ALU.mult, col(PR), ALU.max)
+        EQ = a(WF, 128, 272)
+        if "e" in opt:
+            mm([(a(Q, 0, 144), IF, a(LF, 0, 144), True, False)]
+               + [(a(Q, 8 * k, 8 * k + 8), IFH, L2H, False, k == 16) for k in range(17)])
+            act(YA, a(Q, 0, 144), ACT.Abs)
+            act(EQ, YA, ACT.Relu, bias=1.0, scale=-1.0)
+        B = a(Q, 256, 384)
+        if "c" in opt:
+            act(C1, DL, ACT.Relu, bias=-8.0)
+            act(C2, DL, ACT.Relu, bias=-8.0, scale=-1.0)
+            mm([(B, I1, A0, True, False), (B, I1, C1, False, False), (B, IN, C2, False, True)])
+        else:
+            ts(CL, DL, -8.0, ALU.max, 8.0, ALU.min)
+            mm(([(B, I1, XL, True, False)] if "l" in opt else [(B, I1, A0, True, False), (B, I1, DL, False, False)])
+               + [(B, IN, CL, False, True)])
         act(TB, B)
         for m in range(7, -1, -1):
-            cp(ind(a(XN, 0, 2080), a(U, 288 + 2 * m, 289 + 2 * m)), a(WB, TB[2] + 16 * m, TB[2] + 16 * m + 16))
+            cp(ind(a(XN, 0, X0 + W), a(U, 288 + 2 * m, 289 + 2 * m)), a(WB, 1024 + 16 * m, 1040 + 16 * m))
         tag[0] = "u%d%d" % (t, h)
-        ts(CQ, DQ, -2.0, ALU.max, 2.0, ALU.min)
         last = t == NS - 1
-        tr = "tr%d" % h
-        RB, ro = (tr, 512) if last else (OF, 0)
-        GO = a(OB, 256, 264)
-        if "s" in opt or not last:
-            ts(GO, FIN, 1.0, ALU.is_ge)
-        if "s" in opt:
-            act(a(WF, 128, 256), ind(L, BCK), scale=0.5)
-            act(a(WF, 256, 384), ind(f8(2), BCK))
+        GO = a(OF, zone(t + 1), zone(t + 1) + 8)
+        if "s" not in opt:
+            tt(DD, QH, LL, ALU.subtract)
+        if "e" not in opt:
+            tt(EQ, ind(f8(17, 2), BCK), a(LF, 0, 144), ALU.is_equal)
+        ts(GO, FIN, 0.5, ALU.is_gt)
+        tt(DE, DD, GO, ALU.mult)
+        LF2, LB2 = "LF%d%d" % (t + 1, h), "LB%d%d" % (t + 1, h)
+        TT = a(WF, 272, 416) if last else a(OF, 0, 144)
+        tt(TT, ind(f8(19, 2), BCK), a(WF, 128, 272), ALU.mult)
+        if not last:
+            lo = min(0, zone(t + 1))
+            send([a(LF2, lo, lo + 152)], [a(LF, lo, lo + 152), a(OF, lo, lo + 152)], "arrF%d%d" % (t, h))
+        if "v" in opt:
+            act(SS, a(P, 0, 128), ACT.Sign, bias=-2.0 ** -13)
+            for o, r, pos, neg in ((a(S, 128, 256), R1, I1, IN), (a(Q, 384, 512), R2, IN, I1)):
+                mm(([(o, pos, XQ, True, False), (o, neg, A0, False, False)] if "q" in opt else [(o, pos, DQ, True, False)])
+                   + [(o, IN, SS, False, True)])
+                act(r, o, ACT.Relu, bias=-1.0)
+            G = a(S, 256, 384)
+            mm(([(G, I1, XQ, True, False)] if "q" in opt else [(G, I1, A0, True, False), (G, I1, DQ, False, False)])
+               + [(G, IN, R1, False, False), (G, I1, R2, False, True)])
+            act(a(OB, 0, 128), G)
+            srcs = [a(OB, 0, 128)]
+        else:
             tt(f8(16), GO, f8(0), ALU.mult)
             ts(a(U, 272, 280), f8(16), 128.0, ALU.add)
-            r1, o1 = WF, 128
-        else:
-            NG = f8(15)
-            ts(NG, FIN, 1.0, ALU.is_lt, 4096.0, ALU.mult)
-            tt(f8(16, 4), ind(NG, a("lst", 48, 50)), f8(0, 4), ALU.add)
-            act(a(WF, 128, 256), ind(f8(17), BCK), scale=0.5)
-            act(a(WF, 256, 384), ind(f8(18), BCK))
-            ts(a(U, 272, 280), f8(16), 128.0, ALU.min)
-            r1, o1 = RB, ro
-        tt(a(WF, 384, 512), a(WF, 128, 256), a(S, 0, 128), ALU.is_le)
-        tt(a(WF, 512, 640), a(WF, 384, 512), a(S, 136, 264), ALU.mult)
-        tt(a(S, 272, 400), a(WF, 512, 640), a(S, 0, 128), ALU.add)
-        tt(a(WF, 640, 768), a(WF, 256, 384), a(S, 272, 400), ALU.min)
-        tt(a(r1, o1, o1 + 64), a(WF, 640, 704), a(S, 336, 400), ALU.max)
-        tt(a(r1, o1 + 64, o1 + 128), a(WF, 704, 768), a(S, 264, 328), ALU.max)
-        if "s" in opt:
-            tt(a(WF, 384, 512), a(WF, 128, 256), a(S, 0, 128), ALU.subtract)
-            tt(a(WF, 512, 640), ind(GO, BCK), a(WF, 384, 512), ALU.mult)
-            tt(a(RB, ro, ro + 128), a(WF, 512, 640), a(S, 0, 128), ALU.add)
-        AN = a(OB, 0, 128)
-        if "a" in opt:
-            act(GT, ind(a(WB, CQ[2], CQ[3] + 16), a(U, 272, 280)))
-            AN = a(Q, 256, 384)
-            mm([(AN, a("I1", 0, 128), A0, True, False), (AN, a("I1", 0, 128), GT, False, True)])
-            act(a(OB, 0, 128), AN)
-        else:
-            tt(AN, ind(a(WB, CQ[2], CQ[3] + 16), a(U, 272, 280)), A0, ALU.add)
-        LF2, LB2 = "LF%d%d" % (t + 1, h), "LB%d%d" % (t + 1, h)
+            cw = ind(a(WB, 1408, 1552), a(U, 272, 280))
+            if last:
+                tt(a(OB, 0, 128), cw, A0, ALU.add)
+            else:
+                act(a(OB, 0, 128), cw)
+            srcs = [A0, a(OB, 0, 128)]
         if not last:
-            act(a(OB, 128, 256), AN)
-            send(a(LF2, -24, 128), a(OF, -24, 128), "arrF%d%d" % (t, h))
-            send(a(LB2, 0, 264), a(OB, 0, 264), "arrB%d%d" % (t, h))
-        else:
-            flip(h, f8(24), a(RB, ro + 24, ro + 40), a(LF, 24, 40), SG)
-            ts(a(U, 280, 288), f8(24), 0.0, ALU.is_gt)
-            act(a(OB, 128, 256), ind(a("pm", 0, 16), a(U, 280, 288)))
-            act(a(tr, 0, 256), ind(a(tr, 512, 640), T2W))
-            transpose(tr)
-            act(a(OF, 0, 128), ind(a(tr, 256, 512), W2N))
-            send(a(LF2, 0, 128), a(OF, 0, 128), "arrF%d%d" % (t, h))
-            send(a(LB2, 0, 256), a(OB, 0, 256), "arrB%d%d" % (t, h))
+            send([a(LB2, 0, 128), a(LB2, 128, 256)], srcs, "arrB%d%d" % (t, h))
+            return
+        ZA, ZB, tr = "ZA%d" % h, "ZB%d" % h, "tr%d" % h
+        tt(nd(ZA, None, None, None, None), a(WF, 272, 400), a(LF, 0, 128), ALU.add)
+        for src, dst in ((ZA, ZB), (ZB, ZA), (ZA, ZB)):
+            for j, op in enumerate((ALU.min, ALU.max)):
+                tt(nd(dst, None, None, j, None), nd(src, None, (0, 2), None, None), nd(src, None, (2, 4), None, None), op)
+        od, ev = nd(ZB, 0, None, None, None), nd(ZB, 1, None, None, None)
+        tt(a(tr, 512, 576), od, ev, ALU.max)
+        tt(a(tr, 576, 640), od, ev, ALU.min)
+        act(a(tr, 0, 256), ind(a(tr, 512, 640), T2W))
+        transpose(tr)
+        act(a(OF, 0, 128), ind(a(tr, 256, 512), W2N))
+        send([a(LB2, 0, 128)], [a(OB, 0, 128)], "arrB%d%d" % (t, h))
+        tt(f8(22), nd(ZB, 0, 0, 0, None), nd(ZB, 1, 0, 0, None), ALU.subtract)
+        tt(f8(23), f8(22), SG, ALU.mult)
+        ts(a(U, 280, 288), f8(23), 0.0, ALU.is_gt)
+        act(a(OF, 128, 256), ind(a("pm", 0, 16), a(U, 280, 288)))
+        send([a(LF2, 0, 256)], [a(OF, 0, 256)], "arrF%d%d" % (t, h))
 
     for t in range(NS):
         tag[0] = "copy"
-        dma(a("X%d" % ((t + 1) % 2), 0, W), a("X%d" % (t % 2), 0, W), "cp%d" % t, 524288)
+        X, XN = "X%d" % (t % 2), "X%d" % ((t + 1) % 2)
+        dma(a(XN, X0, X0 + W), a(X, X0, X0 + W), "cp%d" % t, 524288)
         for h in ORDER:
             front(t, h)
         for h in ORDER:
             back(t, h)
     tag[0] = "end"
-    dma(dram("yx"), a("X%d" % (NS % 2), 0, W), "stX", 524288)
+    dma(dram("yx"), a("X%d" % (NS % 2), X0, X0 + W), "stX", 524288)
     for h in ORDER:
         LF, LB = "LF%d%d" % (NS, h), "LB%d%d" % (NS, h)
         dma(dram("yr", 128 * h, 128 * h + 128), a(LF, 0, 128), "stR%d" % h, 65536)
         dma(dram("ya", 128 * h, 128 * h + 128), a(LB, 0, 128), "stA%d" % h, 32768)
-        mm([(a("E%d" % h, 0, 128, 1, 8), a("G8", 0, 8), a(LB, 128, 256), True, True)])
-        act(a("ysb", 128 * h, 128 * h + 128, 1, 8), a("E%d" % h, 0, 128, 1, 8), scale=1.0 / 16)
-    dma(dram("ys"), a("ysb", 0, 256, 1, 8), "stS", 8192, "A")
+        dma(dram("ys", 128 * h, 128 * h + 128), a(LF, 128, 256, 1, -16), "stS%d" % h, 4096, "A")
     return ops
 
 
-def link(ops, cfg):
+def link(ops):
     hist = {}
     for i, o in enumerate(ops):
         deps = {}
@@ -545,13 +615,22 @@ def link(ops, cfg):
                     other = ops[j]["eng"] != o["eng"] or ops[j]["sem"] is not None or o["sem"] is not None
                     if ps and other:
                         deps[j] = True
+                    elif ps and o["eng"] == "T":
+                        deps[j] = deps.get(j, False)
                     elif lo < h2 and l2 < hi and (kind == "w" or k2 == "w"):
-                        deps[j] = deps.get(j, False) or other or (o["eng"] != "T" and (k2 == "w" or cfg["war"]))
+                        deps[j] = deps.get(j, False) or other or o["eng"] != "T"
         for kind, lst in (("r", o["rd"]), ("w", o["wr"])):
             for name, lo, hi in sorted(set(lst)):
                 old = hist.get(name, [])
                 if kind == "w" and SCRATCH[name][0] != "psum":
                     old = [e for e in old if not (lo <= e[2] and e[3] <= hi) or e[0] == i]
+                if SCRATCH[name][0] == "psum":
+                    k, turns, e = len(old), 0, o["eng"]
+                    while k > 0 and (turns < 1 or ops[old[k - 1][0]]["eng"] == e):
+                        if ops[old[k - 1][0]]["eng"] != e:
+                            turns, e = turns + 1, ops[old[k - 1][0]]["eng"]
+                        k -= 1
+                    old = old[k:]
                 hist[name] = old + [(i, kind, lo, hi)]
         o["deps"] = deps
 
@@ -576,7 +655,6 @@ def arrange(ops, cfg):
         if left[i] == 0:
             ready[ops[i]["eng"]].append(i)
     free = {e: 0.0 for e in "VATGS"}
-    order = {e: [] for e in "VATGS"}
     fin = [0.0] * n
     for _ in range(n):
         best = None
@@ -593,7 +671,6 @@ def arrange(ops, cfg):
         o["start"] = st
         free[e] = st + o["cost"]
         fin[i] = free[e] + o["lat"]
-        order[e].append(i)
         for j in succ[i]:
             avail[j] = max(avail[j], fin[i] + (LAT if ops[j]["deps"][i] else 0.0))
             left[j] -= 1
@@ -642,10 +719,98 @@ def place(ops, seq, pre, first):
     return at
 
 
+def improve(ops, cfg):
+    n, seen, key, step = len(ops), {}, [], []
+    for o in ops:
+        g = o["tag"]
+        seen[g, o["key"]] = seen.get((g, o["key"]), 0) + 1
+        each = len(g) == 3 and g != "end"
+        key.append("copy" if g == "copy" else ("" if each and g[:2] not in ("f0", "b3", "u3") else g) + o["key"].replace("X1", "X0") + "#%d" % seen[g, o["key"]])
+        step.append(int(o["sem"][2]) if g == "copy" else int(g[1]) if each else 0)
+    first = [min(o["start"] for o in ops if o["tag"] == "f%d1" % t and o["eng"] == "V") for t in range(NS)]
+    period = (first[3] - first[1]) / 2
+    tau = {}
+    for t in (2, 1, 3, 0):
+        for i, o in enumerate(ops):
+            if step[i] == t and key[i] not in tau:
+                tau[key[i]] = o["start"] - period * t
+    eng = ["VATGS".index(o["eng"]) for o in ops]
+    deps = [list(o["deps"]) for o in ops]
+    models = []
+    for m in cfg["models"]:
+        alt = build(dict(cfg, **m))
+        models.append(([o["cost"] for o in alt], [o["lat"] for o in alt],
+                       [[(j, alt[j]["lat"] + (m["lat"] if w else 0.0)) for j, w in o["deps"].items()] for o in ops]))
+
+    def run():
+        at = [0.0] * n
+        for i in range(n):
+            x = tau[key[i]] + period * step[i]
+            for j in deps[i]:
+                if at[j] > x:
+                    x = at[j]
+            at[i] = x
+        seq = sorted(range(n), key=lambda i: at[i])
+        total, arcs = 0.0, []
+        for cost, lat, pre in models:
+            fin, free, last, why, end, top = [0.0] * n, [0.0] * 5, [-1] * 5, [0] * n, 0.0, 0
+            for i in seq:
+                e = eng[i]
+                s, w = free[e], -2 - last[e]
+                for j, d in pre[i]:
+                    if fin[j] + d > s:
+                        s, w = fin[j] + d, j
+                s += cost[i]
+                why[i], free[e], fin[i], last[e] = w, s, s, i
+                if s + lat[i] > end:
+                    end, top = s + lat[i], i
+            total += end
+            while why[top] != -1:
+                if why[top] < 0:
+                    arcs.append((-2 - why[top], top))
+                    top = -2 - why[top]
+                else:
+                    top = why[top]
+        return total / len(models), arcs, seq
+
+    seed = [cfg["seed"]]
+
+    def rnd():
+        seed[0] = (seed[0] * 1103515245 + 12345) % 2147483648
+        return seed[0] / 2147483648.0
+
+    keys = sorted(tau)
+    cur, arcs, seq = run()
+    best = (cur, seq)
+    for r in range(cfg["rounds"]):
+        far = (1.0, 1.0, 100.0, 400.0, 1000.0, 3000.0)[int(6 * rnd())] * rnd()
+        u = rnd()
+        j, i = arcs[int(len(arcs) * rnd())]
+        if u < 0.4:
+            k, v = key[i], tau[key[j]] + period * (step[j] - step[i]) - far
+        elif u < 0.8:
+            k, v = key[j], tau[key[i]] + period * (step[i] - step[j]) + far
+        else:
+            k = keys[int(len(keys) * rnd())]
+            v = tau[k] + (far if u < 0.9 else -far)
+        old, tau[k] = tau[k], v
+        s, a2, seq = run()
+        if s <= cur or rnd() < math.exp((cur - s) / (3.0 + cfg["heat"] * (1.0 - r / cfg["rounds"]))):
+            cur, arcs = s, a2
+            if s < best[0]:
+                best = (s, seq)
+        else:
+            tau[k] = old
+    order = {e: [i for i in best[1] if ops[i]["eng"] == e] for e in "VATGS"}
+    return order, [best[0]]
+
+
 def plan(cfg):
     ops = build(cfg)
-    link(ops, cfg)
+    link(ops)
     order, fin = arrange(ops, cfg)
+    if cfg["rounds"]:
+        order, fin = improve(ops, cfg)
     pos = {}
     for e in order:
         for k, i in enumerate(order[e]):
@@ -702,9 +867,15 @@ def rank_program(g, core, T, topo):
                 if s is None:
                     q.wait_ge(T.sem[ops[j]["eng"]], p["cnt"][j])
                 else:
-                    q.wait_ge(T.sem[s], arrive if s.startswith("arr") else 16)
+                    q.wait_ge(T.sem[s], arrive * len(ops[j]["call"][1]) if s.startswith("arr") else 16)
             if isinstance(o["call"], tuple):
-                q.remote_dma(real(T, o["call"][1]), real(T, o["call"][2]), T.sem[o["sem"]], T.sem.sent, pid, rid, mask)
+                dsts, srcs = [real(T, s) for s in o["call"][1]], [real(T, s) for s in o["call"][2]]
+                if len(srcs) == 1 and len(dsts) == 1:
+                    q.remote_dma(dsts[0], srcs[0], T.sem[o["sem"]], T.sem.sent, pid, rid, mask)
+                else:
+                    q.remote_dma_fused([RemoteDMATransfer(dst_ids=[DstId(rid=rid, pnc=pid)] * len(dsts), dma_engine_mask=mask,
+                                                          remote_sem=T.sem[o["sem"]], srcs=srcs, dsts=dsts, alu_op=len(srcs) - 1)],
+                                       local_sem=T.sem.sent)
                 sent += len(eng)
             else:
                 r = o["call"](q, T)

@@ -6,7 +6,7 @@ ALU = AluOpType
 ACT = ActivationFunctionType
 NS, HOP, W = 4, 3, 2048
 ORDER = (1, 0)
-X0, VOID, BIG = 32, 2048, 262144.0
+X0, VOID, BIG = 32, 4096, 262144.0
 RT = "float16"
 CFG = {
     "bmode": {(1, 1): "WY", (1, 0): "ZZ", (0, 1): "ZZ", (0, 0): "WY"},
@@ -15,9 +15,9 @@ CFG = {
     "slack": 0.0, "lat": 120.0, "fix": 0.0, "passes": 2, "wire": 3500.0, "cyc": 1.04, "pec": 0.52,
     "boost": {}, "fine": {}, "opt": ("", ""), "optall": "qlvsnexc",
 }
-CFG.update({'bmode': {(1, 1): 'WZ', (1, 0): 'ZW', (0, 1): 'ZY', (0, 0): 'YZ'}, 'aeng': {(1, 1): 'VA', (1, 0): 'VA', (0, 1): 'VA', (0, 0): 'AA'}, 'split': (True, True), 'gt': ('G', 'G'), 'sg': ('A', 'A'), 'rl': ('A', 'A'), 'slack': 30.0, 'lat': 120.0, 'passes': 3, 'boost': {}, 'opt': ('ev', 'ev'),
-            "rounds": 18000, "seed": 1, "heat": 40.0,
-            "models": ({"lat": 150.0, "wire": 2500.0}, {"lat": 110.0, "wire": 3500.0, "gc": 1000.0})})
+CFG.update({'bmode': {(1, 1): 'WZ', (1, 0): 'ZW', (0, 1): 'ZY', (0, 0): 'YZ'}, 'aeng': {(1, 1): 'VA', (1, 0): 'VA', (0, 1): 'VA', (0, 0): 'AA'}, 'split': (True, True), 'gt': ('G', 'G'), 'sg': ('A', 'A'), 'rl': ('A', 'A'), 'slack': 30.0, 'lat': 120.0, 'passes': 1, 'boost': {}, 'opt': ('adeqv', 'adeqv'),
+            "rounds": 45000, "seed": 5, "heat": 60.0,
+            "models": ({"lat": 150.0, "wire": 2800.0, "gc": 400.0},)})
 
 SCRATCH = {}
 
@@ -30,12 +30,13 @@ for _n in ("X0", "X1"):
     _buf(_n, X0 + VOID + 16, "bfloat16")
 _buf("iota", VOID + 8, "float32")
 for _n, _c, _d in (("RI", 256, "int32"), ("sgI", 256, "int32"), ("sgB", 256, "bfloat16"), ("wI", 8, "int32"),
-                   ("pI", 16, "int32"), ("pF", 16, "float32"), ("ci", 528, "float32"), ("lst", 112, "uint16"),
+                   ("pI", 16, "int32"), ("pF", 24, "float32"), ("ci", 792, "float32"), ("lst", 128, "uint16"),
+                   ("Zc", 144, "bfloat16"), ("QB", 64, RT),
                    ("ones", 144, "bfloat16"), ("Z8", 144, "bfloat16"), ("Zw", 144, "bfloat16"),
                    ("Zn", 144, "bfloat16"), ("G8", 16, "bfloat16"), ("I1", 128, "bfloat16"), ("I23", 128, "bfloat16"),
-                   ("In", 128, "bfloat16"), ("Ik", 384, "bfloat16"), ("CC", 512, "bfloat16"), ("MB", 2192, "bfloat16"), ("sameB", 128, "bfloat16"),
-                   ("blk", 128, "bfloat16"), ("nblk", 128, "bfloat16"), ("If", 512, "bfloat16"), ("mask", 128, "bfloat16"),
-                   ("d0", 128, "bfloat16"), ("pm", 16, "bfloat16"), ("ysb", 256, "float32")):
+                   ("In", 128, "bfloat16"), ("Ik", 768, "bfloat16"), ("CC", 512, "bfloat16"), ("MB", 2192, "bfloat16"), ("sameB", 128, "bfloat16"),
+                   ("blk", 128, "bfloat16"), ("nblk", 128, "bfloat16"), ("If", 512, "bfloat16"), ("mask", 368, "bfloat16"),
+                   ("d0", 368, "bfloat16"), ("pm", 16, "bfloat16"), ("ysb", 256, "float32")):
     _buf(_n, _c, _d)
 for _h in (0, 1):
     for _t in range(NS + 1):
@@ -46,14 +47,14 @@ for _h in (0, 1):
         _buf("OB%d%d" % (_t, _h), 256, "bfloat16")
     for _n, _c, _d in (("XR", 2048, "bfloat16"), ("D", 2048, "bfloat16"), ("AD", 2048, "bfloat16"),
                        ("u16", 320, "uint16"), ("wi", 1168, "int32"), ("KB", (3, 64), "float32"),
-                       ("si", 64, "int32"), ("sf", 208, "float32"), ("wb", 2704, "bfloat16"), ("hh", 32, RT), ("wf", 768, "float32"),
-                       ("tr", 640, "float32"), ("VB", 128, "bfloat16"), ("SC", 128, "bfloat16"),
+                       ("si", 64, "int32"), ("sf", 208, "float32"), ("wb", 2944, "bfloat16"), ("hh", 32, RT), ("wf", 768, "float32"),
+                       ("tr", 640, "float32"), ("VB", 240, "bfloat16"), ("SC", 240, "bfloat16"),
                        ("ZA", (2, 4, 2, 8), "float32"), ("ZB", (2, 4, 2, 8), "float32")):
         _buf("%s%d" % (_n, _h), _c, _d)
     for _n in ("P", "Q", "S", "E"):
         _buf("%s%d" % (_n, _h), 512, "float32", "psum")
 
-DMAS = (["ldR", "ldW", "ldS", "ldX0", "cp0", "cp1", "cp2", "cp3", "stX"]
+DMAS = (["ldR", "ldW", "ldS", "ldX0", "ldX1", "cp0", "cp1", "cp2", "cp3", "tw1", "tw2", "tw3", "stX"]
         + ["%s%d" % (a, h) for a in ("ldA", "ldB", "stR", "stA", "stS") for h in (0, 1)])
 SEMAPHORES = ["V", "A", "T", "G", "sent"] + DMAS + ["arr%s%d%d" % (x, t, h) for x in "FB" for t in range(NS) for h in (0, 1)]
 
@@ -108,6 +109,8 @@ def spans(s):
         at = [v * n + r for v in at for r in (range(*x) if isinstance(x, tuple) else [x])]
     x = s[2][-1]
     r = range(*x) if isinstance(x, tuple) else [x]
+    if 1 < len(r) <= 8 and len(at) == 1 and x[2] > 1:
+        return [(s[1], v, v + 1) for v in r]
     runs = []
     for v in at:
         lo, hi = v * shape[-1] + r[0], v * shape[-1] + r[-1] + 1
@@ -182,7 +185,8 @@ def build(cfg):
         if func == ACT.Copy:
             add("A", lambda q, T: q.activation(real(T, out), real(T, in_), func, scale=scale), [out], [in_], c)
         else:
-            add("A", lambda q, T: q.activation(real(T, out), real(T, in_), func, bias=bias, scale=scale), [out], [in_], c)
+            add("A", lambda q, T: q.activation(real(T, out), real(T, in_), func, bias=real(T, bias), scale=scale), [out],
+                [in_] + ([bias] if isinstance(bias, tuple) else []), c)
 
     def gat(eng, out, in_):
         if eng == "V":
@@ -228,6 +232,7 @@ def build(cfg):
     for h in ORDER:
         dma(a("LB0%d" % h, 0, 128), dram("av", 128 * h, 128 * h + 128), "ldA%d" % h, 400000)
         dma(a("LB0%d" % h, 128, 256), dram("av", 128 * h, 128 * h + 128), "ldB%d" % h, 400000)
+    dma(a("X0", X0 + W, X0 + 2 * W), dram("xt"), "ldX1", 1000000)
     iota(a("pI", 0, 1), [[0, 1]], 0, 1)
     col = lambda j: a("pF", j, j + 1)
     PP, PR, PR7, PG, P31, P16, PR3, PRH, PR1, PW, PN, PK, PT = range(13)
@@ -274,12 +279,12 @@ def build(cfg):
     IF, IFP, IFN = a("If", 0, 128), a("If", 128, 256), a("If", 256, 384)
     I4N, IKP, IKN = a("Ik", 0, 128), a("Ik", 128, 256), a("Ik", 256, 384)
     IFM, IFH = IN, a("If", 384, 512)
-    for o, v in ((IFP, 1.0 / 256), (IFN, -1.0 / 256), (IFH, -0.5), (I4N, -4.0), (IKN, -1024.0), (IKP, -BIG),
+    for o, v in ((IFP, 1.0 / 256), (IFN, -1.0 / 256), (IFH, -0.5), (I4N, -4.0), (IKN, -1024.0), (IKP, -BIG), (a("Ik", 640, 768), 1024.0),
                  (a("I23", 0, 128), 8388608.0), (IN, -1.0)):
         act(o, I1, scale=v)
     IF = I1
     CD, CR, CK, CX = [a("CC", 128 * j, 128 * j + 128, 1, 2) for j in range(4)]
-    for lo, v0, v1 in ((0, 4.0, 0.0), (128, 0.0, -255.0 / 512), (256, 8388608.0, -1024.0), (384, BIG, -float(X0))):
+    for lo, v0, v1 in ((0, 4.0, 0.0), (128, 1024.0, -255.0 / 512), (256, 8388608.0, -1024.0), (384, BIG, -float(X0))):
         ms(a("CC", lo, lo + 128, 1, 2), v1)
         if v0 != v1:
             ms(a("CC", lo, lo + 128, 1, 1), v0)
@@ -296,6 +301,34 @@ def build(cfg):
     ts(a("mask", 0, 128), IB, col(PR), ALU.is_gt, -1.0, ALU.mult)
     ts(a("d0", 0, 128), a("sameB", 0, 128), -33.0 / 32, ALU.mult, 1.0, ALU.add)
     ms(a("d0", 0, 128, 16), 0.0)
+    every = cfg["opt"][0] + cfg["opt"][1]
+    if "d" in every:
+        iota(a("ci", 528, 656), [[0, 4], [100, 2], [1, 16]], -100)
+        iota(a("ci", 656, 664), [[2, 4], [0, 2]], 1)
+        ts(col(17), col(PR), 16.0, ALU.add)
+        cp(a("lst", 112, 119), a("ci", 40, 47))
+        cp(a("lst", 119, 127), a("ci", 656, 664))
+        act(a("mask", 128, 240), a("mask", 0, 112))
+        ts(a("mask", 240, 368), a("ci", 528, 656), col(PR), ALU.is_gt, -1.0, ALU.mult)
+        act(a("d0", 128, 240), a("d0", 0, 112))
+        ts(a("ci", 664, 792), a("ci", 528, 656), col(PR), ALU.is_equal, -65.0 / 64, ALU.mult)
+        act(a("d0", 240, 368), a("ci", 664, 792), bias=1.0)
+        ms(a("d0", 240, 368, 32), 0.0)
+        for h in ORDER:
+            act(a("wb%d" % h, 2704, 2816), a("mask", 0, 112))
+    if "k" in every:
+        ts(a("wI", 1, 2), a("wI", 0, 1), 128.0, ALU.add)
+        ts(a("wI", 2, 3), a("wI", 1, 2), 255, ALU.bitwise_and)
+        ts(col(15), a("wI", 2, 3), -128.0, ALU.add)
+        ms(a("Zc", 0, 144), 0.0)
+        ts(a("Zc", 15, 143, 16), a("G8", 0, 8), col(15), ALU.mult, 32.0, ALU.mult)
+        ts(a("G8", 8, 9), col(15), 0.0, ALU.max)
+        mm([(a("E1", 128, 129), a("blk", 0, 128), a("G8", 8, 9), True, True)])
+        ts(a("wI", 3, 4), a("E1", 128, 129), 4080.0, ALU.mult)
+        ts(col(16), a("wI", 3, 4), 1.0, ALU.add)
+        ts(a("QB", 0, 64), a("ci", 128, 192), 0.0, ALU.mult, col(16), ALU.add)
+        act(a("Ik", 384, 512), I1, scale=-8192.0)
+        act(a("Ik", 512, 640), a("sameB", 0, 128), scale=32.0)
     ms(a("ones", 0, 144), 1.0)
     add("G", lambda q, T: q.affine_select(T["Z8"][0:8, 0:144], T["ones"][0:8, 0:144], [[1, 144]], ALU.is_equal, 0.0, -15, -16),
         [a("Z8", 0, 144)], [a("ones", 0, 144)], 170 + 288 * CYC)
@@ -333,26 +366,32 @@ def build(cfg):
         mm([x for f in (0, 1) for x in raw(0, f, False)
             + [(a(S, 64 * f, 64 * f + 64), I4N, a(WB, 1280 + 64 * f, 1344 + 64 * f), False, False),
                (a(S, 64 * f, 64 * f + 64), CD, a("ones", 0, 64, 1, 2), False, True)]])
-        mm([(RR, IF, a(LF, 0, 128), True, False), (RR, CR, ones2, False, True)])
+        mm([(RR, IF, a(LF, 0, 128), True, False), (RR, a("Ik", 640, 768), SGN, False, False), (RR, CR, ones2, False, True)])
         for f in (0, 1):
             e = cfg["aeng"][(h, f)]
             for j in range(len(e)):
                 w = 64 // len(e)
                 c = 64 * f + j * w
                 gat(e[j], a(XR, 16 * c, 16 * (c + w)), ind(a(X, X0, X0 + W), a(U, c, c + w)))
-        TB = a(WB, 1552, 1616)
-        if t > 0:
-            mm([(a(Q, 384 + 8 * k, 392 + 8 * k), a("sameB", 0, 128), a(LF, zone(t), zone(t) + 8), True, True) for k in range(8)])
+        TB, GO, two = a(WB, 1552, 1616), a(LF, zone(t), zone(t) + 8), "k" in cfg["opt"][h]
+        withn = t > 0 and not two
+        if withn:
+            mm([(a(Q, 384 + 8 * k, 392 + 8 * k), a("sameB", 0, 128), GO, True, True) for k in range(8)])
             act(TB, a(Q, 384, 448))
         for f in (0, 1):
             o = a(P, 64 * f, 64 * f + 64)
-            mm([(o, zwin("Zw", b), a(XR, 1024 * f + b, 1024 * f + 1024, 16), b == 0, b == 15 and t == 0) for b in range(16)]
-               + ([(o, I1, TB, False, True)] if t > 0 else []))
+            mm([(o, zwin("Zw", b), a(XR, 1024 * f + b, 1024 * f + 1024, 16), b == 0, b == 15 and not withn) for b in range(16)]
+               + ([(o, I1, TB, False, True)] if withn else []))
+        for f in (1, 0) if two else ():
+            o = a(Q, 128 + 64 * f, 192 + 64 * f)
+            mm([(o, a("Ik", 384, 512), a("QB", 0, 64), True, False)]
+               + [(a(Q, 128 + 64 * f + 8 * k, 136 + 64 * f + 8 * k), a("Ik", 512, 640), GO, False, False) for k in range(8 if t > 0 else 0)]
+               + [(o, zwin("Zc", b), a(XR, 1024 * f + b, 1024 * f + 1024, 16), False, b == 15) for b in range(16)])
         UI, UU, W1, W2, W3, W4, QQ = 0, 128, 272, 400, 528, 656, 1040
         parts = ((0, 64), (64, 128)) if cfg["split"][h] else ((0, 128),)
         wi = lambda b, p: a(WI, b + p[0], b + p[1])
-        for p in ((0, 64), (64, 128)):
-            if t > 0:
+        for p in ((0, 64), (64, 128)) if withn else parts:
+            if withn:
                 tt(wi(UI, p), a(P, p[0], p[1]), TB, ALU.subtract)
             else:
                 cp(wi(UI, p), a(P, p[0], p[1]))
@@ -361,14 +400,16 @@ def build(cfg):
         for lo, hi, nx in ((64, 128, 0), (0, 56, 72), (56, 64, 64)):
             tt(a(WI, W1 + lo, W1 + hi), a(WI, UU + lo, UU + hi), a(WI, UU + nx, UU + nx + hi - lo), ALU.mult)
         for p in parts[::-1]:
-            ts(wi(W2, p), wi(W1, p), 5, ALU.arith_shift_right)
-            tt(wi(W3, p), wi(W2, p), a(P, p[0], p[1]), ALU.add)
-            ts(wi(W4, p), wi(W3, p), 255, ALU.bitwise_and)
+            if two:
+                tt(wi(W3, p), wi(W1, p), a(Q, 128 + p[0], 128 + p[1]), ALU.add)
+                ts(wi(W4, p), wi(W3, p), 5, ALU.arith_shift_right, 255, ALU.bitwise_and)
+            else:
+                ts(wi(W2, p), wi(W1, p), 5, ALU.arith_shift_right)
+                tt(wi(W3, p), wi(W2, p), a(P, p[0], p[1]), ALU.add)
+                ts(wi(W4, p), wi(W3, p), 255, ALU.bitwise_and)
             dh = a("wf%d" % h, 384 + p[0], 384 + p[1])
             tt(dh, wi(W4, p), a(S, p[0], p[1]), ALU.mult)
             tt(wi(QQ, p), dh, a(S, 128 + p[0], 128 + p[1]), ALU.add)
-            if t > 0 or p[0] == 0:
-                ts(wi(QQ, p), wi(QQ, p), W - 1, ALU.bitwise_and)
             cp(a(U, 128 + p[0], 128 + p[1]), wi(QQ, p))
             act(a(WB, p[0], p[1]), dh, ACT.Sign, bias=255.5 / 256, scale=-1.0)
         win = a(X, X0, X0 + VOID)
@@ -451,17 +492,17 @@ def build(cfg):
         QH, EV, OD, L2H = [a(HH, 8 * j, 8 * j + 8) for j in range(4)]
         SG, L2, LL, DE, DF, SM = a(LF, 136, 144), f8(1), f8(17), f8(19), f8(8), f8(10)
         if "s" in opt:
-            DF, SM = a(P, 392, 400), a(P, 400, 408)
+            DF, SM = a(S, 464, 472), a(S, 472, 480)
             mm([(DF, IF, EV, True, False), (DF, IFM, OD, False, True), (SM, IF, EV, True, False), (SM, IF, OD, False, True)])
         else:
             tt(DF, EV, OD, ALU.subtract)
             tt(SM, EV, OD, ALU.add)
         tt(f8(9), DF, SG, ALU.mult)
-        mm([(a(P, 384, 392), zwin("Zn", b), a(WB, 256 + b, 384, 16), b == 0, b == 15) for b in range(16)])
+        mm([(a(P, 128, 136), zwin("Zn", b), a(WB, 256 + b, 384, 16), b == 0, b == 15) for b in range(16)])
         if cfg["sg"][h] == "A":
-            act(f8(11), a(P, 384, 392), ACT.Sign, bias=thr, scale=-1.0)
+            act(f8(11), a(P, 128, 136), ACT.Sign, bias=thr, scale=-1.0)
         else:
-            ts(f8(11), a(P, 384, 392), thr, ALU.is_lt, 0.5, ALU.subtract)
+            ts(f8(11), a(P, 128, 136), thr, ALU.is_lt, 0.5, ALU.subtract)
         tt(f8(12), f8(11), f8(9), ALU.mult)
         wide, narrow = not all(x in opt for x in "nexs"), any(x in opt for x in "nexs")
         if wide:
@@ -479,30 +520,55 @@ def build(cfg):
         if "n" in opt:
             mm([(a(Q, 384 + b, 512, 16), a("MB", 128 * b, 128 * b + 128), L2H, True, True) for b in range(16)])
             act(NE, a(Q, 384, 512), ACT.Abs)
+        elif "a" in opt:
+            act(f8(24), L2, scale=-1.0)
+            act(a(WF, 0, 128), ind(a("iota", 0, VOID + 8), a(U, 264, 272)))
+            for m in range(8):
+                lo, k, to = (16 * m - 16, 32, 96 + 16 * m) if "d" in opt and m % 2 else (16 * m, 16, 16 * m)
+                act(a(WB, 2704 + to, 2704 + to + k), a(WF, lo, lo + k), ACT.Abs, bias=a(SF, 192 + m, 193 + m))
+            NE = a(WB, 2704, 2944 if "d" in opt else 2832)
+        elif "d" in opt:
+            act(a(WF, 512, 752), ind(L2, a("lst", 112, 127)))
+            for lo, k in ((0, 7), (112, 8)):
+                tt(a(WB, 2704 + lo, 2704 + lo + 16 * k), ind(a("iota", 0, VOID + 8), a(U, 264, 264 + k)),
+                   a(WF, 512 + lo, 512 + lo + 16 * k), ALU.not_equal)
+            NE = a(WB, 2704, 2944)
         else:
             act(a(WF, 0, 128), ind(L2, BCB))
             tt(NE, ind(a("iota", 0, VOID + 8), a(U, 264, 272)), a(WF, 0, 128), ALU.not_equal)
         BLK, NBLK = a("blk", 0, 128), a("nblk", 0, 128)
+        cut = lambda s, n: a(s[1], s[2][0][0], s[2][0][0] + n)
         if cfg["rl"][h] == "A" or "l" in opt:
             act(RL, DL, ACT.Abs)
-            margin = lambda o, st: [(o, BLK, AQ, st, False), (o, NBLK, RL, False, True)]
+            terms = ((BLK, AQ), (NBLK, RL))
         else:
             ts(RL, DL, 0.0, ALU.max, -2.0, ALU.mult)
-            margin = lambda o, st: [(o, BLK, AQ, st, False), (o, BLK, DL, False, False), (o, BLK, RL, False, True)]
-        E = a(P, 256, 384)
-        mm([(E, I1, a("mask", 0, 128), True, False)] + margin(E, False) + (margin(a(P, 0, 128), True) if "v" in opt else []))
+            terms = ((BLK, AQ), (BLK, DL), (BLK, RL))
+        margin = lambda o, st: [(o, l, cut(x, count(o)), st and x is AQ, x is RL) for l, x in terms]
+        n, mk, d0 = (240, 128, 128) if "d" in opt else (128, 0, 0)
+        E = a(P, 256, 256 + n)
+        cuts = [a(P, 256 + lo, 256 + hi) for lo, hi in (((0, 112), (112, 240)) if "d" in opt else ((0, 128),))]
+        mm([(E, I1, a("mask", mk, mk + n), True, False)] + [(o, BLK, cut(AQ, count(o)), False, False) for o in cuts])
+        mm([(o, l, cut(x, count(o)), False, x is RL and o is cuts[-1]) for o in cuts for l, x in terms[1:]])
         if "e" not in opt or "s" not in opt:
             act(LL, L2, scale=0.5)
         if "x" not in opt:
             act(f8(14), L2, bias=X0 / BIG - 1.0, scale=0.5 / BIG)
-        tt(a(VB, 0, 128), E, NE, ALU.is_gt)
-        add("V", lambda q, T: q.tensor_tensor_scan(T[SC][:, 0:128], T["d0"][:, 0:128], T[VB][:, 0:128], 0.0, ALU.mult, ALU.add),
-            [a(SC, 0, 128)], [a(VB, 0, 128), a("d0", 0, 128)], (VF + 64) * CYC)
+        tt(a(VB, 0, n), E, NE, ALU.is_gt)
+        add("V", lambda q, T: q.tensor_tensor_scan(T[SC][:, 0:n], T["d0"][:, d0:d0 + n], T[VB][:, 0:n], 0.0, ALU.mult, ALU.add),
+            [a(SC, 0, n)], [a(VB, 0, n), a("d0", d0, d0 + n)], (VF + max(FL, n / 2)) * CYC)
         FIN = a(SC, 15, 128, 16)
-        DD = a(P, 408, 416) if "s" in opt else f8(13)
+        DD = a(P, 152, 160) if "s" in opt else f8(13)
         it = [(DD, IF, QH, True, False), (DD, IFH, L2H, False, True)] if "s" in opt else []
-        if "x" in opt:
-            XX = a(P, 416, 424)
+        if "d" in opt:
+            if it:
+                mm(it)
+            for e in (0, 1):
+                tt(a(SF, 120 + e, 128, 2), a(SC, 15 + 128 * e, 128 + 112 * e, 32), a(SF, 112 + e, 120, 2), ALU.add)
+            for e in (0, 1):
+                ts(a(U, 288 + e, 296, 2), a(SF, 120 + e, 128, 2), BIG, ALU.mult, col(17 if e else PR), ALU.max)
+        elif "x" in opt:
+            XX = a(P, 160, 168)
             mm(it + [(XX, CX, a("ones", 0, 8, 1, 2), True, False), (XX, IFH, L2H, False, False), (XX, IKP, FIN, False, True)])
             ts(a(U, 288, 304, 2), XX, -1.0, ALU.mult, col(PR), ALU.max)
         else:
@@ -526,8 +592,9 @@ def build(cfg):
             mm(([(B, I1, XL, True, False)] if "l" in opt else [(B, I1, A0, True, False), (B, I1, DL, False, False)])
                + [(B, IN, CL, False, True)])
         act(TB, B)
-        for m in range(7, -1, -1):
-            cp(ind(a(XN, 0, X0 + W), a(U, 288 + 2 * m, 289 + 2 * m)), a(WB, 1024 + 16 * m, 1040 + 16 * m))
+        z = 2 if "d" in opt else 1
+        for m in range(8 // z - 1, -1, -1):
+            cp(ind(a(XN, 0, X0 + W), a(U, 288 + 2 * m, 288 + 2 * m + z)), a(WB, 1024 + 16 * z * m, 1024 + 16 * z * (m + 1)))
         tag[0] = "u%d%d" % (t, h)
         last = t == NS - 1
         GO = a(OF, zone(t + 1), zone(t + 1) + 8)
@@ -535,7 +602,11 @@ def build(cfg):
             tt(DD, QH, LL, ALU.subtract)
         if "e" not in opt:
             tt(EQ, ind(f8(17, 2), BCK), a(LF, 0, 144), ALU.is_equal)
-        ts(GO, FIN, 0.5, ALU.is_gt)
+        if "d" in opt:
+            for e in (0, 1):
+                ts(a(OF, zone(t + 1) + e, zone(t + 1) + 8, 2), a(SC, 15 + 128 * e, 128 + 112 * e, 32), 0.5, ALU.is_gt)
+        else:
+            ts(GO, FIN, 0.5, ALU.is_gt)
         tt(DE, DD, GO, ALU.mult)
         LF2, LB2 = "LF%d%d" % (t + 1, h), "LB%d%d" % (t + 1, h)
         TT = a(WF, 272, 416) if last else a(OF, 0, 144)
@@ -544,6 +615,7 @@ def build(cfg):
             lo = min(0, zone(t + 1))
             send([a(LF2, lo, lo + 152)], [a(LF, lo, lo + 152), a(OF, lo, lo + 152)], "arrF%d%d" % (t, h))
         if "v" in opt:
+            mm(margin(a(P, 0, 128), True))
             act(SS, a(P, 0, 128), ACT.Sign, bias=-2.0 ** -13)
             for o, r, pos, neg in ((a(S, 128, 256), R1, I1, IN), (a(Q, 384, 512), R2, IN, I1)):
                 mm(([(o, pos, XQ, True, False), (o, neg, A0, False, False)] if "q" in opt else [(o, pos, DQ, True, False)])
@@ -587,7 +659,11 @@ def build(cfg):
     for t in range(NS):
         tag[0] = "copy"
         X, XN = "X%d" % (t % 2), "X%d" % ((t + 1) % 2)
-        dma(a(XN, X0, X0 + W), a(X, X0, X0 + W), "cp%d" % t, 524288)
+        if t > 0:
+            tag[0] = "twin"
+            dma(a(X, X0 + W, X0 + 2 * W), a(X, X0, X0 + W), "tw%d" % t, 524288)
+            tag[0] = "copy"
+        dma(a(XN, X0, X0 + W), a(X, X0, X0 + W), "cp%d" % t, 1048576)
         for h in ORDER:
             front(t, h)
         for h in ORDER:
@@ -725,8 +801,8 @@ def improve(ops, cfg):
         g = o["tag"]
         seen[g, o["key"]] = seen.get((g, o["key"]), 0) + 1
         each = len(g) == 3 and g != "end"
-        key.append("copy" if g == "copy" else ("" if each and g[:2] not in ("f0", "b3", "u3") else g) + o["key"].replace("X1", "X0") + "#%d" % seen[g, o["key"]])
-        step.append(int(o["sem"][2]) if g == "copy" else int(g[1]) if each else 0)
+        key.append(g if g in ("copy", "twin") else ("" if each and g[:2] not in ("f0", "b3", "u3") else g) + o["key"].replace("X1", "X0") + "#%d" % seen[g, o["key"]])
+        step.append(int(o["sem"][2]) if g in ("copy", "twin") else int(g[1]) if each else 0)
     first = [min(o["start"] for o in ops if o["tag"] == "f%d1" % t and o["eng"] == "V") for t in range(NS)]
     period = (first[3] - first[1]) / 2
     tau = {}
@@ -735,12 +811,20 @@ def improve(ops, cfg):
             if step[i] == t and key[i] not in tau:
                 tau[key[i]] = o["start"] - period * t
     eng = ["VATGS".index(o["eng"]) for o in ops]
-    deps = [list(o["deps"]) for o in ops]
+    below, deps = [0] * n, []
+    for i, o in enumerate(ops):
+        cover = 0
+        for j, w in o["deps"].items():
+            if w:
+                cover |= below[j]
+        deps.append([j for j in o["deps"] if not cover >> j & 1])
+        for j in o["deps"]:
+            below[i] |= below[j] | 1 << j
     models = []
     for m in cfg["models"]:
         alt = build(dict(cfg, **m))
         models.append(([o["cost"] for o in alt], [o["lat"] for o in alt],
-                       [[(j, alt[j]["lat"] + (m["lat"] if w else 0.0)) for j, w in o["deps"].items()] for o in ops]))
+                       [[(j, alt[j]["lat"] + (m["lat"] if o["deps"][j] else 0.0)) for j in d] for o, d in zip(ops, deps)]))
 
     def run():
         at = [0.0] * n
@@ -786,21 +870,27 @@ def improve(ops, cfg):
         far = (1.0, 1.0, 100.0, 400.0, 1000.0, 3000.0)[int(6 * rnd())] * rnd()
         u = rnd()
         j, i = arcs[int(len(arcs) * rnd())]
-        if u < 0.4:
-            k, v = key[i], tau[key[j]] + period * (step[j] - step[i]) - far
+        if u < 0.35:
+            new = {key[i]: tau[key[j]] + period * (step[j] - step[i]) - far}
+        elif u < 0.7:
+            new = {key[j]: tau[key[i]] + period * (step[i] - step[j]) + far}
         elif u < 0.8:
-            k, v = key[j], tau[key[i]] + period * (step[i] - step[j]) + far
-        else:
             k = keys[int(len(keys) * rnd())]
-            v = tau[k] + (far if u < 0.9 else -far)
-        old, tau[k] = tau[k], v
+            new = {k: tau[k] + (far if u < 0.75 else -far)}
+        else:
+            k = key[i] if u < 0.9 else key[j]
+            wide, by = 3000.0 * rnd(), (-1500.0 if u < 0.9 else 1500.0) * rnd()
+            side = 1.0 if rnd() < 0.5 else -1.0
+            new = {x: tau[x] + by for x in keys if x[:2] == k[:2] and 0.0 <= (tau[k] - tau[x]) * side <= wide}
+        old = {k: tau[k] for k in new}
+        tau.update(new)
         s, a2, seq = run()
         if s <= cur or rnd() < math.exp((cur - s) / (3.0 + cfg["heat"] * (1.0 - r / cfg["rounds"]))):
             cur, arcs = s, a2
             if s < best[0]:
                 best = (s, seq)
         else:
-            tau[k] = old
+            tau.update(old)
     order = {e: [i for i in best[1] if ops[i]["eng"] == e] for e in "VATGS"}
     return order, [best[0]]
 

@@ -6,18 +6,16 @@ ALU = AluOpType
 ACT = ActivationFunctionType
 NS, HOP, W = 4, 3, 2048
 ORDER = (1, 0)
-X0, VOID, BIG = 32, 4096, 262144.0
+X0, BIG = 32, 262144.0
+TW = X0 + W
 RT = "float16"
-CFG = {
-    "bmode": {(1, 1): "WY", (1, 0): "ZZ", (0, 1): "ZZ", (0, 0): "WY"},
-    "aeng": {(1, 1): "VA", (1, 0): "VA", (0, 1): "AA", (0, 0): "AA"},
-    "split": (True, True), "gt": ("A", "A"), "sg": ("A", "A"), "rl": ("A", "A"),
-    "slack": 0.0, "lat": 120.0, "fix": 0.0, "passes": 2, "wire": 3500.0, "cyc": 1.04, "pec": 0.52,
-    "boost": {}, "fine": {}, "opt": ("", ""), "optall": "qlvsnexc",
-}
-CFG.update({'bmode': {(1, 1): 'WZ', (1, 0): 'ZW', (0, 1): 'ZY', (0, 0): 'YZ'}, 'aeng': {(1, 1): 'VA', (1, 0): 'VA', (0, 1): 'VA', (0, 0): 'AA'}, 'split': (True, True), 'gt': ('G', 'G'), 'sg': ('A', 'A'), 'rl': ('A', 'A'), 'slack': 30.0, 'lat': 120.0, 'passes': 1, 'boost': {}, 'opt': ('adeqv', 'adeqv'),
-            "rounds": 45000, "seed": 5, "heat": 60.0,
-            "models": ({"lat": 150.0, "wire": 2800.0, "gc": 400.0},)})
+CFG = {"bmode": {(1, 1): "WW", (1, 0): "ZZ", (0, 1): "ZY", (0, 0): "YZ"},
+       "aeng": {(1, 1): "VA", (1, 0): "VA", (0, 1): "VA", (0, 0): "AA"},
+       "slack": 30.0, "lat": 170.0, "passes": 1, "wire": 2500.0, "cyc": 0.9, "pec": 0.56,
+       "rounds": 30000, "apart": 30000, "seed": 5, "heat": 30.0, "heat2": 5.0, "opt": ("vfqi", "vf"), "own": ("s3", "b3", "u3"), "lin": (0, 1), "dl": 1200.0,
+       "models": ({"cyc": 1.04, "pec": 0.59, "lat": 100.0, "wire": 2600.0, "gc": 400.0, "dl": 1000.0},
+                  {"cyc": 0.9, "pec": 0.52, "lat": 200.0, "wire": 3200.0, "gc": 450.0, "dl": 1000.0},
+                  {"cyc": 1.2, "pec": 0.7, "ga": 1.9, "sca": 5.0, "lat": 200.0, "wire": 3600.0, "gc": 500.0})}
 
 SCRATCH = {}
 
@@ -26,17 +24,14 @@ def _buf(name, cols, dtype, where="sbuf"):
     SCRATCH[name] = (where, [128] + (list(cols) if isinstance(cols, tuple) else [cols]), dtype)
 
 
-for _n in ("X0", "X1"):
-    _buf(_n, X0 + VOID + 16, "bfloat16")
-_buf("iota", VOID + 8, "float32")
+_buf("X", X0 + 2 * W + 16, "bfloat16")
+_buf("iota", W + 8, "float32")
 for _n, _c, _d in (("RI", 256, "int32"), ("sgI", 256, "int32"), ("sgB", 256, "bfloat16"), ("wI", 8, "int32"),
-                   ("pI", 16, "int32"), ("pF", 24, "float32"), ("ci", 792, "float32"), ("lst", 128, "uint16"),
-                   ("Zc", 144, "bfloat16"), ("QB", 64, RT),
+                   ("pI", 16, "int32"), ("pF", 24, "float32"), ("ci", 776, "float32"), ("lst", 128, "uint16"),
                    ("ones", 144, "bfloat16"), ("Z8", 144, "bfloat16"), ("Zw", 144, "bfloat16"),
-                   ("Zn", 144, "bfloat16"), ("G8", 16, "bfloat16"), ("I1", 128, "bfloat16"), ("I23", 128, "bfloat16"),
-                   ("In", 128, "bfloat16"), ("Ik", 768, "bfloat16"), ("CC", 512, "bfloat16"), ("MB", 2192, "bfloat16"), ("sameB", 128, "bfloat16"),
-                   ("blk", 128, "bfloat16"), ("nblk", 128, "bfloat16"), ("If", 512, "bfloat16"), ("mask", 368, "bfloat16"),
-                   ("d0", 368, "bfloat16"), ("pm", 16, "bfloat16"), ("ysb", 256, "float32")):
+                   ("Zn", 144, "bfloat16"), ("G8", 16, "bfloat16"), ("Ik", 1408, "bfloat16"), ("CC", 768, "bfloat16"),
+                   ("sameB", 128, "bfloat16"), ("blk", 128, "bfloat16"), ("nblk", 128, "bfloat16"), ("mask", 64, "bfloat16"),
+                   ("d0", 768, "bfloat16"), ("pm", 16, "bfloat16")):
     _buf(_n, _c, _d)
 for _h in (0, 1):
     for _t in range(NS + 1):
@@ -47,14 +42,16 @@ for _h in (0, 1):
         _buf("OB%d%d" % (_t, _h), 256, "bfloat16")
     for _n, _c, _d in (("XR", 2048, "bfloat16"), ("D", 2048, "bfloat16"), ("AD", 2048, "bfloat16"),
                        ("u16", 320, "uint16"), ("wi", 1168, "int32"), ("KB", (3, 64), "float32"),
-                       ("si", 64, "int32"), ("sf", 208, "float32"), ("wb", 2944, "bfloat16"), ("hh", 32, RT), ("wf", 768, "float32"),
-                       ("tr", 640, "float32"), ("VB", 240, "bfloat16"), ("SC", 240, "bfloat16"),
+                       ("si", 64, "int32"), ("sf", 208, "float32"), ("wb", 3200, "bfloat16"), ("hh", 416, RT), ("wf", 1024, "float32"),
+                       ("tr", 640, "float32"), ("VB", 256, "bfloat16"), ("SC", 512, "bfloat16"), ("pg", 256, "bfloat16"),
+                       ("OG", 256, "float32"),
                        ("ZA", (2, 4, 2, 8), "float32"), ("ZB", (2, 4, 2, 8), "float32")):
         _buf("%s%d" % (_n, _h), _c, _d)
-    for _n in ("P", "Q", "S", "E"):
+    _buf("P%d" % _h, (8, 64), "float32", "psum")
+    for _n in ("Q", "S", "E"):
         _buf("%s%d" % (_n, _h), 512, "float32", "psum")
 
-DMAS = (["ldR", "ldW", "ldS", "ldX0", "ldX1", "cp0", "cp1", "cp2", "cp3", "tw1", "tw2", "tw3", "stX"]
+DMAS = (["ldR", "ldW", "ldS", "ldX0", "ldX1", "tw1", "tw2", "tw3", "stX"]
         + ["%s%d" % (a, h) for a in ("ldA", "ldB", "stR", "stA", "stS") for h in (0, 1)])
 SEMAPHORES = ["V", "A", "T", "G", "sent"] + DMAS + ["arr%s%d%d" % (x, t, h) for x in "FB" for t in range(NS) for h in (0, 1)]
 
@@ -62,6 +59,12 @@ SEMAPHORES = ["V", "A", "T", "G", "sent"] + DMAS + ["arr%s%d%d" % (x, t, h) for 
 def a(name, lo, hi, step=1, p=128):
     if name[:2] in ("LF", "OF"):
         lo, hi = lo + 8, hi + 8
+    shape = SCRATCH[name][1][1:]
+    if len(shape) == 2:
+        c = shape[1]
+        if lo // c == (hi - 1) // c:
+            return ("n", name, (lo // c, (lo % c, lo % c + hi - lo, step)), p)
+        return ("n", name, ((lo // c, hi // c, 1), (0, c, 1)), p)
     return ("n", name, ((lo, hi, step),), p)
 
 
@@ -109,8 +112,8 @@ def spans(s):
         at = [v * n + r for v in at for r in (range(*x) if isinstance(x, tuple) else [x])]
     x = s[2][-1]
     r = range(*x) if isinstance(x, tuple) else [x]
-    if 1 < len(r) <= 8 and len(at) == 1 and x[2] > 1:
-        return [(s[1], v, v + 1) for v in r]
+    if 1 < len(r) <= 17 and len(at) == 1 and x[2] > 1:
+        return [(s[1], at[0] * shape[-1] + v, at[0] * shape[-1] + v + 1) for v in r]
     runs = []
     for v in at:
         lo, hi = v * shape[-1] + r[0], v * shape[-1] + r[-1] + 1
@@ -133,8 +136,8 @@ def width(s):
 def build(cfg):
     ops = []
     tag = ["setup"]
-    CYC, PEC, GA, SCA, FIX = cfg["cyc"], cfg["pec"], cfg.get("ga", 1.56), cfg.get("sca", 3.8), cfg["fix"]
-    FL, VF = cfg.get("fl", 64), cfg.get("vf", 0)
+    CYC, PEC, GA, SCA = cfg["cyc"], cfg["pec"], cfg.get("ga", 1.56), cfg.get("sca", 3.8)
+    FL = 64
 
     def add(eng, call, outs, ins, cost, sem=None, lat=0.0):
         wr, rd = [], []
@@ -146,7 +149,7 @@ def build(cfg):
                 wr += spans(s)
         for s in ins:
             rd += spans(s)
-        ops.append({"eng": eng, "call": call, "wr": wr, "rd": rd, "cost": cost + FIX, "sem": sem, "lat": lat, "tag": tag[0],
+        ops.append({"eng": eng, "call": call, "wr": wr, "rd": rd, "cost": cost + (cfg.get("fix", 0.0) if eng in "VA" else 0.0), "sem": sem, "lat": lat, "tag": tag[0],
                     "key": tag[0][0] + tag[0][2:] + eng + (wr[0][0][:2] + str(wr[0][1]) if wr else str(sem))})
 
     def vcost(out, ins, tt=False):
@@ -159,7 +162,7 @@ def build(cfg):
             f = 2.0 if all(where(s) == "sbuf" for s in ins) else 1.0
         else:
             f = 0.5 if all(width(s) == 2 for s in [out] + ins) else 1.0
-        return (VF + max(FL, n * f)) * CYC
+        return max(FL, n * f) * CYC
 
     def cp(out, in_):
         add("V", lambda q, T: q.tensor_copy(real(T, out), real(T, in_)), [out], [in_], vcost(out, [in_]))
@@ -174,12 +177,16 @@ def build(cfg):
             return q.tensor_scalar(real(T, out), real(T, x), real(T, s1), real(T, s2), op0, op1)
         add("V", call, [out], [x] + [s for s in (s1, s2) if isinstance(s, tuple)], vcost(out, [x]))
 
+    def scan(out, d0, d1):
+        add("V", lambda q, T: q.tensor_tensor_scan(real(T, out), real(T, d0), real(T, d1), 0.0, ALU.mult, ALU.add),
+            [out], [d0, d1], vcost(out, [d0, d1]))
+
     def ms(out, v):
-        add("V", lambda q, T: q.memset(real(T, out), v), [out], [], (VF + max(FL, count(out) * width(out) / 4)) * CYC)
+        add("V", lambda q, T: q.memset(real(T, out), v), [out], [], max(FL, count(out) * width(out) / 4) * CYC)
 
     def act(out, in_, func=ACT.Identity, bias=0.0, scale=1.0):
         n = count(out)
-        c = 65 + GA * n * CYC if in_[0] == "i" else (VF + max(FL, n)) * CYC
+        c = 65 + GA * n * CYC if in_[0] == "i" else max(FL, n) * CYC
         if bias == 0.0 and func == ACT.Identity:
             func = ACT.Copy
         if func == ACT.Copy:
@@ -187,6 +194,9 @@ def build(cfg):
         else:
             add("A", lambda q, T: q.activation(real(T, out), real(T, in_), func, bias=real(T, bias), scale=scale), [out],
                 [in_] + ([bias] if isinstance(bias, tuple) else []), c)
+
+    def fill(out, v):
+        act(out, a("ones", 0, count(out), 1, out[3]), scale=v)
 
     def gat(eng, out, in_):
         if eng == "V":
@@ -210,11 +220,21 @@ def build(cfg):
             add("G", lambda q, T: q.iota(real(T, out), pattern, base, cm, allow_small_or_imprecise_dtypes=True),
                 [out], [], 130 + 2 * count(out) * CYC)
 
-    def dma(out, in_, sem, nbytes, eng="S"):
-        add(eng, lambda q, T: q.dma_start(real(T, out), real(T, in_)), [out], [in_], 60, sem, 1500 + nbytes / 300.0)
+    def select(out, in_, pattern, op, fill_, base, cm):
+        add("G", lambda q, T: q.affine_select(real(T, out), real(T, in_), pattern, op, fill_, base, cm), [out], [in_],
+            170 + 2 * count(out) * CYC)
+
+    def gfill(out, v):
+        if v == int(v) and abs(v) < 1 << 24:
+            iota(out, [[0, count(out)]], int(v))
+        else:
+            select(out, a("ones", 0, count(out), 1, out[3]), [[0, count(out)]], ALU.is_gt, v, -1, 0)
+
+    def dma(out, in_, sem, nbytes, eng="S", after=()):
+        add(eng, lambda q, T: q.dma_start(real(T, out), real(T, in_)), [out], [in_] + list(after), 60, sem, cfg["dl"] + nbytes / 300.0)
 
     def transpose(tr):
-        add("V", lambda q, T: q.transpose(T[tr][:, 256:512], T[tr][:, 0:256]), [a(tr, 256, 512)], [a(tr, 0, 256)], (VF + 256) * CYC)
+        add("V", lambda q, T: q.transpose(T[tr][:, 256:512], T[tr][:, 0:256]), [a(tr, 256, 512)], [a(tr, 0, 256)], 256 * CYC)
 
     def zwin(name, b, p=128):
         return a(name, 15 - b, 143 - b, 1, p)
@@ -225,183 +245,177 @@ def build(cfg):
     def zone(t):
         return 144 if t % 2 else -8
 
+    XM = a("X", X0, TW)
     dma(a("RI", 0, 256), dram("rl"), "ldR", 131072, "A")
-    dma(a("X0", X0, X0 + W), dram("xt"), "ldX0", 600000)
+    dma(XM, dram("xt"), "ldX0", 600000)
     dma(a("wI", 0, 1), dram("wt"), "ldW", 512, "A")
     dma(a("sgI", 0, 256, 1, 8), dram("sg"), "ldS", 8192, "A")
     for h in ORDER:
-        dma(a("LB0%d" % h, 0, 128), dram("av", 128 * h, 128 * h + 128), "ldA%d" % h, 400000)
-        dma(a("LB0%d" % h, 128, 256), dram("av", 128 * h, 128 * h + 128), "ldB%d" % h, 400000)
-    dma(a("X0", X0 + W, X0 + 2 * W), dram("xt"), "ldX1", 1000000)
+        dma(a("LB0%d" % h, 0, 128), dram("av", 128 * h, 128 * h + 128), "ldA%d" % h, 400000, after=[XM])
+        dma(a("LB0%d" % h, 128, 256), dram("av", 128 * h, 128 * h + 128), "ldB%d" % h, 400000, after=[XM])
+    dma(a("X", TW, TW + W), dram("xt"), "ldX1", 1000000, after=[XM])
+    ms(a("ones", 0, 144), 1.0)
     iota(a("pI", 0, 1), [[0, 1]], 0, 1)
     col = lambda j: a("pF", j, j + 1)
-    PP, PR, PR7, PG, P31, P16, PR3, PRH, PR1, PW, PN, PK, PT = range(13)
+    PP, PR, PR7, PG, P31, P16, PR3, PRH, PR1, PW, PN, PT, PS, NR, BU, BD = range(16)
     for j, (sh, mk) in enumerate(((0, 15), (0, 7), (4, 7), (0, 31), (0, 16), (2, 2), (1, 7), (0, 1))):
         ts(a("pI", j + 1, j + 2), a("pI", 0, 1), sh, ALU.arith_shift_right, mk, ALU.bitwise_and)
-    cp(a("pF", 0, 9), a("pI", 0, 9))
+        cp(col(j + 1), a("pI", j + 1, j + 2)) if j == 0 else None
+    cp(col(PP), a("pI", 0, 1))
+    cp(a("pF", 2, 9), a("pI", 2, 9))
     cp(col(PW), a("wI", 0, 1))
-    ts(col(13), col(PR7), 32.0, ALU.mult, col(P16), ALU.add)
-    ts(col(PN), col(13), col(PR3), ALU.add)
-    ts(col(14), col(PR1), -8.0, ALU.mult, col(PRH), ALU.add)
-    ts(col(PT), col(14), 8.0, ALU.add, 8.0, ALU.mult)
-    DUP, N2T, BCB, T2W, W2N, BCK = (a("lst", 0, 32), a("lst", 32, 40), a("lst", 40, 48), a("lst", 64, 80), a("lst", 80, 88),
-                                    a("lst", 96, 105))
-    for lst, pat, base, c in ((DUP, [[16, 16], [0, 2]], 0, PR), (N2T, [[-1, 2], [4, 4]], 1, PN), (BCB, [[1, 8]], 0, None),
-                              (T2W, [[1, 8], [0, 2]], 0, PT), (W2N, [[32, 8]], 0, P31)):
+    ts(col(16), col(PR7), 32.0, ALU.mult, col(P16), ALU.add)
+    ts(col(PN), col(16), col(PR3), ALU.add)
+    ts(col(17), col(PR1), -8.0, ALU.mult, col(PRH), ALU.add)
+    ts(col(PT), col(17), 8.0, ALU.add, 8.0, ALU.mult)
+    act(col(PS), col(PR), bias=16.0)
+    act(col(NR), col(PR), scale=-1.0)
+    ts(col(BU), col(PR), 15.0, ALU.is_equal, 8192.0, ALU.mult)
+    ts(col(BD), col(PR), 0.0, ALU.is_equal, -8192.0, ALU.mult)
+    DUP, N2T, T2W, W2N, BCK = (a("lst", 0, 32), a("lst", 32, 40), a("lst", 64, 80), a("lst", 80, 88), a("lst", 96, 105))
+    for lst, pat, base, c in ((DUP, [[16, 16], [0, 2]], 0, PR), (N2T, [[-1, 2], [4, 4]], 1, PN), (T2W, [[1, 8], [0, 2]], 0, PT)):
         lo, hi = lst[2][0][:2]
         src = a("ci", lo, hi)
         iota(src, pat, base)
-        if c is None:
-            cp(lst, src)
-        else:
-            ts(lst, src, col(c), ALU.add)
-    iota(a("ci", 96, 104), [[0, 8]])
-    ts(a("lst", 96, 104), a("ci", 96, 104), col(PR7), ALU.add)
-    ts(a("lst", 104, 105), col(PR), 8.0, ALU.min)
-    iota(a("ci", 88, 96), [[16, 8]])
-    for h in ORDER:
-        ts(a("sf%d" % h, 0, 8), a("ci", 88, 96), col(PR), ALU.add, -128.0, ALU.add)
-        ms(a("sf%d" % h, 136, 168), -5.0)
-        ms(a("wb%d" % h, 1536, 1552), 0.0)
-        for t in range(NS - 1):
-            cp(a("LF%d%d" % (t, h), zone(t + 1), zone(t + 1) + 8), a("wb%d" % h, 1536, 1544))
-    IB, IG, IC = a("ci", 128, 256), a("ci", 256, 384), a("ci", 384, 512)
+        ts(lst, src, col(c), ALU.add)
+    IB, IG, IC, I8, IM = a("ci", 128, 256), a("ci", 256, 384), a("ci", 384, 512), a("ci", 384, 392), a("ci", 512, 576)
+    iota(IC, [[1, 128]])
     iota(IB, [[0, 8], [1, 16]])
     iota(IG, [[1, 8], [0, 16]])
-    iota(IC, [[1, 128]])
-    ts(a("G8", 0, 8), a("ci", 40, 48), col(PG), ALU.is_equal)
-    ms(a("Zw", 0, 144), 0.0)
-    ms(a("Zn", 0, 144), 0.0)
+    iota(IM, [[-100, 2], [100, 2], [1, 16]])
+    ts(W2N, I8, 32.0, ALU.mult, col(P31), ALU.add)
+    ts(a("lst", 96, 104), I8, 0.0, ALU.mult, col(PR7), ALU.add)
+    ts(a("lst", 104, 105), col(PR), 8.0, ALU.min)
+    for h in ORDER:
+        gfill(a("sf%d" % h, 160, 168), 0.0)
+        gfill(a("wb%d" % h, 2704, 2960), 0.0)
+        gfill(a("OG%d" % h, 128, 256), -1.0)
+        for t in range(NS - 1):
+            fill(a("LF%d%d" % (t, h), zone(t + 1), zone(t + 1) + 8), 0.0)
+            if "e" in cfg["opt"][0]:
+                fill(a("OF%d%d" % (t, h), 136, 144), 0.0)
+    ts(a("G8", 0, 8), I8, col(PG), ALU.is_equal)
+    fill(a("Zw", 0, 144), 0.0)
+    gfill(a("Zn", 0, 144), 0.0)
     ts(a("Zw", 15, 143, 16), a("G8", 0, 8), col(PW), ALU.mult)
-    ts(a("Zn", 15, 143, 16), a("G8", 0, 8), -4096.0, ALU.mult)
-    I1, IN = a("I1", 0, 128), a("In", 0, 128)
+    act(a("Zn", 15, 143, 16), a("G8", 0, 8), scale=-4096.0)
+    I1, IN, IFP, IFN, BL1, I4N, IKN, IKP, I23, SU, SD = [a("Ik", 128 * j, 128 * j + 128) for j in range(11)]
+    C75 = a("CC", 384, 512, 1, 1)
     ts(I1, IC, col(PP), ALU.is_equal)
-    IF, IFP, IFN = a("If", 0, 128), a("If", 128, 256), a("If", 256, 384)
-    I4N, IKP, IKN = a("Ik", 0, 128), a("Ik", 128, 256), a("Ik", 256, 384)
-    IFM, IFH = IN, a("If", 384, 512)
-    for o, v in ((IFP, 1.0 / 256), (IFN, -1.0 / 256), (IFH, -0.5), (I4N, -4.0), (IKN, -1024.0), (IKP, -BIG), (a("Ik", 640, 768), 1024.0),
-                 (a("I23", 0, 128), 8388608.0), (IN, -1.0)):
+    for o, v in ((IFP, 1.0 / 256), (IFN, -1.0 / 256), (I4N, -4.0), (IKN, -1024.0), (IKP, 1024.0), (I23, 8388608.0), (IN, -1.0)):
         act(o, I1, scale=v)
-    IF = I1
-    CD, CR, CK, CX = [a("CC", 128 * j, 128 * j + 128, 1, 2) for j in range(4)]
-    for lo, v0, v1 in ((0, 4.0, 0.0), (128, 1024.0, -255.0 / 512), (256, 8388608.0, -1024.0), (384, BIG, -float(X0))):
-        ms(a("CC", lo, lo + 128, 1, 2), v1)
-        if v0 != v1:
-            ms(a("CC", lo, lo + 128, 1, 1), v0)
+    for o, base in ((SU, -1), (SD, 1)):
+        select(o, IN, [[-1, 128]], ALU.not_equal, 1.0, base, 1)
+    CD, CR, CK = a("CC", 0, 128, 1, 1), a("CC", 128, 256, 1, 2), a("CC", 256, 384, 1, 2)
+    gfill(CD, 4.0)
+    for lo, v0, v1 in ((128, -255.0 / 512, 1024.0), (256, 3 * 8388608.0, -9216.0)):
+        gfill(a("CC", lo, lo + 128, 1, 2), v1)
+        gfill(a("CC", lo, lo + 128, 1, 1), v0)
+    BLK, NBLK = a("blk", 0, 128), a("nblk", 0, 128)
     ts(a("sameB", 0, 128), IB, col(PR), ALU.is_equal)
-    ts(a("blk", 0, 128), IG, col(PG), ALU.is_equal, 2.0 ** -12, ALU.mult)
-    act(a("nblk", 0, 128), a("blk", 0, 128), scale=-1.0)
-    if "n" in cfg["opt"][0] + cfg["opt"][1]:
-        act(a("If", 0, 128), I1, scale=-1.0 / 8)
-        mm([(a("E1", 0, 128), I1, a("blk", 0, 128), True, False), (a("E1", 0, 128), IFP, a("If", 0, 128), False, True)])
-        act(a("MB", 2048, 2176), a("E1", 0, 128), scale=4096.0)
-        act(a("MB", 2176, 2192), a("sameB", 0, 16), bias=-1.0)
-        for b in range(16):
-            ts(a("MB", 128 * b, 128 * b + 128), a("MB", 2048, 2176), a("MB", 2176 + b, 2177 + b), ALU.max, a("sameB", b, b + 1), ALU.min)
-    ts(a("mask", 0, 128), IB, col(PR), ALU.is_gt, -1.0, ALU.mult)
-    ts(a("d0", 0, 128), a("sameB", 0, 128), -33.0 / 32, ALU.mult, 1.0, ALU.add)
-    ms(a("d0", 0, 128, 16), 0.0)
-    every = cfg["opt"][0] + cfg["opt"][1]
-    if "d" in every:
-        iota(a("ci", 528, 656), [[0, 4], [100, 2], [1, 16]], -100)
-        iota(a("ci", 656, 664), [[2, 4], [0, 2]], 1)
-        ts(col(17), col(PR), 16.0, ALU.add)
-        cp(a("lst", 112, 119), a("ci", 40, 47))
-        cp(a("lst", 119, 127), a("ci", 656, 664))
-        act(a("mask", 128, 240), a("mask", 0, 112))
-        ts(a("mask", 240, 368), a("ci", 528, 656), col(PR), ALU.is_gt, -1.0, ALU.mult)
-        act(a("d0", 128, 240), a("d0", 0, 112))
-        ts(a("ci", 664, 792), a("ci", 528, 656), col(PR), ALU.is_equal, -65.0 / 64, ALU.mult)
-        act(a("d0", 240, 368), a("ci", 664, 792), bias=1.0)
-        ms(a("d0", 240, 368, 32), 0.0)
+    ts(BLK, IG, col(PG), ALU.is_equal, 2.0 ** -12, ALU.mult)
+    act(NBLK, BLK, scale=-1.0)
+    if "a" in cfg["opt"][0]:
+        act(BL1, BLK, scale=2.0 ** 27)
+        fill(C75, -7.5 * 32768)
+        fill(a("CC", 512, 768, 2, 1), 1.0)
+        fill(a("CC", 513, 768, 2, 1), 0.0)
+        ts(a("pg1", 0, 256, 2), IB, col(PR), ALU.is_gt, 64.0, ALU.mult)
+        act(a("pg0", 0, 256, 2), a("pg1", 0, 256, 2))
         for h in ORDER:
-            act(a("wb%d" % h, 2704, 2816), a("mask", 0, 112))
-    if "k" in every:
-        ts(a("wI", 1, 2), a("wI", 0, 1), 128.0, ALU.add)
-        ts(a("wI", 2, 3), a("wI", 1, 2), 255, ALU.bitwise_and)
-        ts(col(15), a("wI", 2, 3), -128.0, ALU.add)
-        ms(a("Zc", 0, 144), 0.0)
-        ts(a("Zc", 15, 143, 16), a("G8", 0, 8), col(15), ALU.mult, 32.0, ALU.mult)
-        ts(a("G8", 8, 9), col(15), 0.0, ALU.max)
-        mm([(a("E1", 128, 129), a("blk", 0, 128), a("G8", 8, 9), True, True)])
-        ts(a("wI", 3, 4), a("E1", 128, 129), 4080.0, ALU.mult)
-        ts(col(16), a("wI", 3, 4), 1.0, ALU.add)
-        ts(a("QB", 0, 64), a("ci", 128, 192), 0.0, ALU.mult, col(16), ALU.add)
-        act(a("Ik", 384, 512), I1, scale=-8192.0)
-        act(a("Ik", 512, 640), a("sameB", 0, 128), scale=32.0)
-    ms(a("ones", 0, 144), 1.0)
-    add("G", lambda q, T: q.affine_select(T["Z8"][0:8, 0:144], T["ones"][0:8, 0:144], [[1, 144]], ALU.is_equal, 0.0, -15, -16),
-        [a("Z8", 0, 144)], [a("ones", 0, 144)], 170 + 288 * CYC)
-    ms(a("pm", 0, 1), -1.0)
-    ms(a("pm", 1, 16), 1.0)
-    for x in ("X0", "X1"):
-        ms(a(x, X0 + VOID, X0 + VOID + 16), 4096.0)
-        ms(a(x, 0, X0), 0.0)
-    iota(a("iota", 0, VOID + 8), [[2, VOID + 8]])
-    cp(a("sgB", 0, 256, 1, 8), a("sgI", 0, 256, 1, 8))
+            fill(a("pg%d" % h, 1, 256, 2), 1.0)
+    else:
+        ts(a("pg0", 0, 128), IB, col(PR), ALU.is_gt, 64.0, ALU.mult)
+        act(a("pg0", 128, 144), a("sameB", 0, 16), scale=-7.5 / 4096)
+        scan(a("ci", 96, 112), a("pg0", 0, 16), a("pg0", 128, 144))
+    act(a("mask", 0, 64), IM, ACT.Relu, bias=col(NR))
+    ts(a("ci", 576, 640), IM, col(PR), ALU.is_equal)
+    if "R" in cfg["opt"][0]:
+        ts(col(18), col(PR7), 32.0, ALU.mult, 31.0, ALU.add)
+        ts(a("lst", 112, 121), a("ci", 384, 393), 0.0, ALU.mult, col(18), ALU.add)
+    every = cfg["opt"][0] + cfg["opt"][1]
+    for lo, v in ([(256, -3.0)] if "d" in every else []) + ([(512, -1.0)] if set("drR") & set(every) else []) + [(0, -65.0 / 64)]:
+        for j in range(4):
+            act(a("d0", lo + 64 * j, lo + 64 * j + 64), a("ci", 576, 640), bias=1.0, scale=v)
+        if lo < 512:
+            fill(a("d0", lo, lo + 256, 32), 0.0)
+    select(a("Z8", 0, 144, 1, 8), a("ones", 0, 144, 1, 8), [[1, 144]], ALU.is_equal, 0.0, -15, -16)
+    iota(a("pm", 0, 16), [[-2, 16]], 1)
+    gfill(a("X", TW + W, TW + W + 16), 4096.0)
+    iota(a("iota", 0, W + 8), [[1, W + 8]])
+    whole = "i" in cfg["opt"][0]
+    (act if whole else cp)(a("sgB", 0, 256, 1, 8), a("sgI", 0, 256, 1, 8))
     mm([(a("E0", 0, 16), zwin("Z8", b, 8), a("sgB", b, 256, 16, 8), b == 0, b == 15) for b in range(16)])
     for h in ORDER:
         tr = "tr%d" % h
-        cp(a(tr, 0, 256), ind(a("RI", 0, 256), a("lst", 16 * h, 16 * h + 16)))
+        (act if whole and h == 0 else cp)(a(tr, 0, 256), ind(a("RI", 0, 256), a("lst", 16 * h, 16 * h + 16)))
         transpose(tr)
-        cp(a("LF0%d" % h, 0, 128), ind(a(tr, 256, 512), N2T))
-        cp(a("LF0%d" % h, 128, 136), a("LF0%d" % h, 64, 72))
-        ts(a("LF0%d" % h, 136, 144), a("E0", 8 * h, 8 * h + 8), 1.0 if cfg["sg"][h] == "A" else 2.0, ALU.mult)
+        (act if whole and h == 0 else cp)(a("u16%d" % h, 0, 128), ind(a(tr, 256, 512), N2T))
+        act(a("LF0%d" % h, 0, 128), ind(a(tr, 256, 512), N2T))
+        act(a("LF0%d" % h, 128, 136), a("LF0%d" % h, 64, 72))
+        act(a("LF0%d" % h, 136, 144), a("E0", 8 * h, 8 * h + 8))
 
     def names(t, h):
-        return ("LF%d%d" % (t, h), "LB%d%d" % (t, h), "P%d" % h, "Q%d" % h, "S%d" % h, "u16%d" % h, "wi%d" % h,
-                "wb%d" % h, "X%d" % (t % 2))
+        return ("LF%d%d" % (t, h), "LB%d%d" % (t, h), "P%d" % h, "Q%d" % h, "S%d" % h, "u16%d" % h, "wi%d" % h, "wb%d" % h)
 
     def front(t, h):
         tag[0] = "f%d%d" % (t, h)
-        LF, LB, P, Q, S, U, WI, WB, X = names(t, h)
+        LF, LB, P, Q, S, U, WI, WB = names(t, h)
         XR, D, AD, KB = "XR%d" % h, "D%d" % h, "AD%d" % h, "KB%d" % h
         NXT = (72, 0)
-        cp(a(U, 0, 128), a(LF, 0, 128))
-        SGN, DD, RR, ones2 = a(WB, 1280, 1408), a(S, 0, 128), a(S, 128, 256), a("ones", 0, 128, 1, 2)
+        if t > 0:
+            (act if "u" in cfg["opt"][0] else cp)(a(U, 0, 128), a(LF, 0, 128))
+        SGN, RR, ones2 = a(WB, 1280, 1408), a(S, 128, 256), a("ones", 0, 128, 1, 2)
         raw = lambda o, f, end: [(a(S, o + 64 * f, o + 64 + 64 * f), IFP, a(LF, NXT[f], NXT[f] + 64), True, False),
                                  (a(S, o + 64 * f, o + 64 + 64 * f), IFN, a(LF, 64 * f, 64 * f + 64), False, end)]
         mm(raw(256, 0, True) + raw(256, 1, True))
         act(SGN, a(S, 256, 384), ACT.Sign)
         mm([x for f in (0, 1) for x in raw(0, f, False)
             + [(a(S, 64 * f, 64 * f + 64), I4N, a(WB, 1280 + 64 * f, 1344 + 64 * f), False, False),
-               (a(S, 64 * f, 64 * f + 64), CD, a("ones", 0, 64, 1, 2), False, True)]])
-        mm([(RR, IF, a(LF, 0, 128), True, False), (RR, a("Ik", 640, 768), SGN, False, False), (RR, CR, ones2, False, True)])
+               (a(S, 64 * f, 64 * f + 64), CD, a("ones", 0, 64, 1, 1), False, True)]])
+        mm([(RR, I1, a(LF, 0, 128), True, False), (RR, IKP, SGN, False, False), (RR, CR, ones2, False, True)])
         for f in (0, 1):
             e = cfg["aeng"][(h, f)]
             for j in range(len(e)):
                 w = 64 // len(e)
                 c = 64 * f + j * w
-                gat(e[j], a(XR, 16 * c, 16 * (c + w)), ind(a(X, X0, X0 + W), a(U, c, c + w)))
-        TB, GO, two = a(WB, 1552, 1616), a(LF, zone(t), zone(t) + 8), "k" in cfg["opt"][h]
-        withn = t > 0 and not two
-        if withn:
+                gat(e[j], a(XR, 16 * c, 16 * (c + w)), ind(XM, a(U, c, c + w)))
+        TB, GO = a(WB, 1552, 1616), a(LF, zone(t), zone(t) + 8)
+        withn = t > 0
+        if withn and "n" in cfg["opt"][0]:
+            mm([(a(Q, 384, 392), a("sameB", 0, 128), GO, True, True)])
+            act(a("sf%d" % h, 0, 8), a(Q, 384, 392))
+            act(TB, ind(a("sf%d" % h, 0, 8), a("lst", 96, 100)))
+        elif withn:
             mm([(a(Q, 384 + 8 * k, 392 + 8 * k), a("sameB", 0, 128), GO, True, True) for k in range(8)])
             act(TB, a(Q, 384, 448))
         for f in (0, 1):
             o = a(P, 64 * f, 64 * f + 64)
             mm([(o, zwin("Zw", b), a(XR, 1024 * f + b, 1024 * f + 1024, 16), b == 0, b == 15 and not withn) for b in range(16)]
                + ([(o, I1, TB, False, True)] if withn else []))
-        for f in (1, 0) if two else ():
-            o = a(Q, 128 + 64 * f, 192 + 64 * f)
-            mm([(o, a("Ik", 384, 512), a("QB", 0, 64), True, False)]
-               + [(a(Q, 128 + 64 * f + 8 * k, 136 + 64 * f + 8 * k), a("Ik", 512, 640), GO, False, False) for k in range(8 if t > 0 else 0)]
-               + [(o, zwin("Zc", b), a(XR, 1024 * f + b, 1024 * f + 1024, 16), False, b == 15) for b in range(16)])
         UI, UU, W1, W2, W3, W4, QQ = 0, 128, 272, 400, 528, 656, 1040
-        parts = ((0, 64), (64, 128)) if cfg["split"][h] else ((0, 128),)
+        parts = ((0, 64), (64, 128))
         wi = lambda b, p: a(WI, b + p[0], b + p[1])
-        for p in ((0, 64), (64, 128)) if withn else parts:
+        lin, LI = "l" in cfg["opt"][0] and h in cfg["lin"], 784
+        for p in parts:
             if withn:
                 tt(wi(UI, p), a(P, p[0], p[1]), TB, ALU.subtract)
-            else:
+            elif not lin:
                 cp(wi(UI, p), a(P, p[0], p[1]))
+            if lin:
+                ts(wi(LI, p), a(P, p[0], p[1]), 32.0, ALU.mult)
         for p in parts:
-            ts(wi(UU, p), wi(UI, p), 4095, ALU.bitwise_and)
+            if lin and not withn:
+                ts(wi(UU, p), wi(LI, p), 5, ALU.arith_shift_right, 4095, ALU.bitwise_and)
+            else:
+                ts(wi(UU, p), wi(UI, p), 4095, ALU.bitwise_and)
+            if lin:
+                ts(wi(W2, p), wi(LI, p), 8191, ALU.bitwise_and)
         for lo, hi, nx in ((64, 128, 0), (0, 56, 72), (56, 64, 64)):
             tt(a(WI, W1 + lo, W1 + hi), a(WI, UU + lo, UU + hi), a(WI, UU + nx, UU + nx + hi - lo), ALU.mult)
         for p in parts[::-1]:
-            if two:
-                tt(wi(W3, p), wi(W1, p), a(Q, 128 + p[0], 128 + p[1]), ALU.add)
+            if lin:
+                tt(wi(W3, p), wi(W1, p), wi(W2, p), ALU.add)
                 ts(wi(W4, p), wi(W3, p), 5, ALU.arith_shift_right, 255, ALU.bitwise_and)
             else:
                 ts(wi(W2, p), wi(W1, p), 5, ALU.arith_shift_right)
@@ -409,10 +423,13 @@ def build(cfg):
                 ts(wi(W4, p), wi(W3, p), 255, ALU.bitwise_and)
             dh = a("wf%d" % h, 384 + p[0], 384 + p[1])
             tt(dh, wi(W4, p), a(S, p[0], p[1]), ALU.mult)
-            tt(wi(QQ, p), dh, a(S, 128 + p[0], 128 + p[1]), ALU.add)
-            cp(a(U, 128 + p[0], 128 + p[1]), wi(QQ, p))
+            if "q" in cfg["opt"][0]:
+                tt(a(U, 128 + p[0], 128 + p[1]), dh, a(S, 128 + p[0], 128 + p[1]), ALU.add)
+            else:
+                tt(wi(QQ, p), dh, a(S, 128 + p[0], 128 + p[1]), ALU.add)
+                cp(a(U, 128 + p[0], 128 + p[1]), wi(QQ, p))
             act(a(WB, p[0], p[1]), dh, ACT.Sign, bias=255.5 / 256, scale=-1.0)
-        win = a(X, X0, X0 + VOID)
+        win = a("X", X0, X0 + 2 * W)
         AA = a(LB, 0, 256)
         for f in (1, 0):
             mode = cfg["bmode"][(h, f)]
@@ -424,8 +441,12 @@ def build(cfg):
                 if md == "Z":
                     act(y, ind(win, a(U, c, c + 32)), scale=-1.0)
                     e = "E%d" % j
-                    mm([(a(e, 0, 512), I1, y, True, False), (a(e, 0, 256), I1, AA, False, False),
-                        (a(e, 256, 512), I1, AA, False, True)])
+                    if "z" in cfg["opt"][0]:
+                        mm([(a(e, 0, 256), I1, AA, True, False), (a(e, 256, 512), I1, AA, False, False)])
+                        mm([(a(e, 0, 512), I1, y, False, True)])
+                    else:
+                        mm([(a(e, 0, 512), I1, y, True, False), (a(e, 0, 256), I1, AA, False, False),
+                            (a(e, 256, 512), I1, AA, False, True)])
                     act(x, a(e, 0, 512), ACT.Abs)
                 else:
                     for i in (0, 1):
@@ -436,9 +457,8 @@ def build(cfg):
                         act(x, y, ACT.Abs)
             kb, ko = (Q, 0) if f == 0 else (P, 128)
             K = a(kb, ko, ko + 64)
-            it = [(K, a("I23", 0, 128), a(WB, 64 * f, 64 * f + 64), True, False), (K, CK, a("ones", 0, 64, 1, 2), False, False),
-                  (K, IKN, a(WB, 1280 + 64 * f, 1344 + 64 * f), False, False)]
-            mm(it)
+            mm([(K, I23, a(WB, 64 * f, 64 * f + 64), True, False), (K, CK, a("ones", 0, 64, 1, 2), False, False),
+                (K, IKN, a(WB, 1280 + 64 * f, 1344 + 64 * f), False, False)])
             if mode == "WW":
                 mm([(K, zwin("Zn", b), a(D, o + b, o + 1024, 16), False, False) for b in range(16)])
             else:
@@ -448,199 +468,19 @@ def build(cfg):
                              False, False) for b in range(16)])
             mm([(K, zwin("Zn", b), a(AD, o + b, o + 1024, 16), False, b == 15) for b in range(16)])
             ev = a(LF, 72, 136) if f == 0 else a(LF, 64, 128)
-            for j, pay in enumerate((a(WI, QQ + 64 * f, QQ + 64 * f + 64), ev, a(LF, 0, 64))):
+            qq = a(U, 128 + 64 * f, 192 + 64 * f) if "q" in cfg["opt"][0] else a(WI, QQ + 64 * f, QQ + 64 * f + 64)
+            for j, pay in enumerate((qq, ev, a(LF, 0, 64))):
                 tt(nd(KB, j, None) if f == 1 else a(S, 272 + 64 * j, 336 + 64 * j), K, pay, ALU.add)
 
-    def back(t, h):
-        tag[0] = "b%d%d" % (t, h)
-        LF, LB, P, Q, S, U, WI, WB, X = names(t, h)
-        KB, SI, SF, WF, VB, SC = ["%s%d" % (x, h) for x in ("KB", "si", "sf", "wf", "VB", "SC")]
-        OF, OB, XN = "OF%d%d" % (t, h), "OB%d%d" % (t, h), "X%d" % ((t + 1) % 2)
-        win = a(X, X0, X0 + VOID + 1)
-        A0 = a(LB, 0, 128)
-        f8 = lambda j, n=1: a(SF, 8 * j, 8 * (j + n))
-        tt(nd(KB, None, None), nd(KB, None, None), a(S, 272, 464), ALU.min)
-        tt(nd(KB, None, (0, 32)), nd(KB, None, (0, 32)), nd(KB, None, (32, 64)), ALU.min)
-        tt(nd(KB, None, (0, 16)), nd(KB, None, (0, 16)), nd(KB, None, (16, 32)), ALU.min)
-        tt(a(SI, 0, 24), nd(KB, None, (0, 8)), nd(KB, None, (8, 16)), ALU.min)
-        ts(a(SI, 24, 48), a(SI, 0, 24), 2047, ALU.bitwise_and)
-        cp(a(U, 256, 264), a(SI, 24, 32))
-        DQ, GT, AQ, DL, RL, NE, CL, TB = [a(WB, 128 * j, 128 * j + 128) for j in range(1, 9)]
-        CQ = a(WB, 1408, 1536)
-        XQ, XL, C1, C2, SS, R1, R2 = [a(WB, 1664 + 128 * j, 1792 + 128 * j) for j in range(7)]
-        YA, HH = a(WB, 2560, 2704), "hh%d" % h
-        qw = ind(a(X, X0, X0 + W), a(U, 256, 264))
-        gt, opt = cfg["gt"][h], cfg["opt"][h]
-        if gt == "G":
-            tt(GT, qw, A0, ALU.is_gt)
-        if "q" in opt:
-            act(XQ, qw)
-            DQ = a(Q, 256, 384)
-            mm([(DQ, I1, XQ, True, False), (DQ, IN, A0, False, True)])
-        else:
-            tt(DQ, qw, A0, ALU.subtract)
-        if gt == "A":
-            act(GT, DQ, ACT.Sign, bias=-0.5)
-        elif gt == "V":
-            ts(GT, DQ, 0.0, ALU.is_gt)
-        thr = 1024.0 if gt == "A" else -7.5 * 4096
-        act(AQ, DQ, ACT.Abs)
-        if "v" not in opt:
-            ts(CQ, DQ, -2.0, ALU.max, 2.0, ALU.min)
-        ts(f8(5, 3), a(SI, 0, 24), 8192.0, ALU.is_ge, float(VOID), ALU.mult)
-        tt(a(HH, 0, 24), a(SI, 24, 48), f8(5, 3), ALU.max)
-        QH, EV, OD, L2H = [a(HH, 8 * j, 8 * j + 8) for j in range(4)]
-        SG, L2, LL, DE, DF, SM = a(LF, 136, 144), f8(1), f8(17), f8(19), f8(8), f8(10)
-        if "s" in opt:
-            DF, SM = a(S, 464, 472), a(S, 472, 480)
-            mm([(DF, IF, EV, True, False), (DF, IFM, OD, False, True), (SM, IF, EV, True, False), (SM, IF, OD, False, True)])
-        else:
-            tt(DF, EV, OD, ALU.subtract)
-            tt(SM, EV, OD, ALU.add)
-        tt(f8(9), DF, SG, ALU.mult)
-        mm([(a(P, 128, 136), zwin("Zn", b), a(WB, 256 + b, 384, 16), b == 0, b == 15) for b in range(16)])
-        if cfg["sg"][h] == "A":
-            act(f8(11), a(P, 128, 136), ACT.Sign, bias=thr, scale=-1.0)
-        else:
-            ts(f8(11), a(P, 128, 136), thr, ALU.is_lt, 0.5, ALU.subtract)
-        tt(f8(12), f8(11), f8(9), ALU.mult)
-        wide, narrow = not all(x in opt for x in "nexs"), any(x in opt for x in "nexs")
-        if wide:
-            tt(L2, f8(12), SM, ALU.add)
-        if narrow:
-            tt(L2H, f8(12), SM, ALU.add)
-        ts(a(U, 264, 272), L2 if wide else L2H, 0.5, ALU.mult)
-        lw = ind(win, a(U, 264, 272))
-        if "l" in opt:
-            act(XL, lw)
-            DL = a(S, 0, 128)
-            mm([(DL, I1, XL, True, False), (DL, IN, A0, False, True)])
-        else:
-            tt(DL, lw, A0, ALU.subtract)
-        if "n" in opt:
-            mm([(a(Q, 384 + b, 512, 16), a("MB", 128 * b, 128 * b + 128), L2H, True, True) for b in range(16)])
-            act(NE, a(Q, 384, 512), ACT.Abs)
-        elif "a" in opt:
-            act(f8(24), L2, scale=-1.0)
-            act(a(WF, 0, 128), ind(a("iota", 0, VOID + 8), a(U, 264, 272)))
-            for m in range(8):
-                lo, k, to = (16 * m - 16, 32, 96 + 16 * m) if "d" in opt and m % 2 else (16 * m, 16, 16 * m)
-                act(a(WB, 2704 + to, 2704 + to + k), a(WF, lo, lo + k), ACT.Abs, bias=a(SF, 192 + m, 193 + m))
-            NE = a(WB, 2704, 2944 if "d" in opt else 2832)
-        elif "d" in opt:
-            act(a(WF, 512, 752), ind(L2, a("lst", 112, 127)))
-            for lo, k in ((0, 7), (112, 8)):
-                tt(a(WB, 2704 + lo, 2704 + lo + 16 * k), ind(a("iota", 0, VOID + 8), a(U, 264, 264 + k)),
-                   a(WF, 512 + lo, 512 + lo + 16 * k), ALU.not_equal)
-            NE = a(WB, 2704, 2944)
-        else:
-            act(a(WF, 0, 128), ind(L2, BCB))
-            tt(NE, ind(a("iota", 0, VOID + 8), a(U, 264, 272)), a(WF, 0, 128), ALU.not_equal)
-        BLK, NBLK = a("blk", 0, 128), a("nblk", 0, 128)
-        cut = lambda s, n: a(s[1], s[2][0][0], s[2][0][0] + n)
-        if cfg["rl"][h] == "A" or "l" in opt:
-            act(RL, DL, ACT.Abs)
-            terms = ((BLK, AQ), (NBLK, RL))
-        else:
-            ts(RL, DL, 0.0, ALU.max, -2.0, ALU.mult)
-            terms = ((BLK, AQ), (BLK, DL), (BLK, RL))
-        margin = lambda o, st: [(o, l, cut(x, count(o)), st and x is AQ, x is RL) for l, x in terms]
-        n, mk, d0 = (240, 128, 128) if "d" in opt else (128, 0, 0)
-        E = a(P, 256, 256 + n)
-        cuts = [a(P, 256 + lo, 256 + hi) for lo, hi in (((0, 112), (112, 240)) if "d" in opt else ((0, 128),))]
-        mm([(E, I1, a("mask", mk, mk + n), True, False)] + [(o, BLK, cut(AQ, count(o)), False, False) for o in cuts])
-        mm([(o, l, cut(x, count(o)), False, x is RL and o is cuts[-1]) for o in cuts for l, x in terms[1:]])
-        if "e" not in opt or "s" not in opt:
-            act(LL, L2, scale=0.5)
-        if "x" not in opt:
-            act(f8(14), L2, bias=X0 / BIG - 1.0, scale=0.5 / BIG)
-        tt(a(VB, 0, n), E, NE, ALU.is_gt)
-        add("V", lambda q, T: q.tensor_tensor_scan(T[SC][:, 0:n], T["d0"][:, d0:d0 + n], T[VB][:, 0:n], 0.0, ALU.mult, ALU.add),
-            [a(SC, 0, n)], [a(VB, 0, n), a("d0", d0, d0 + n)], (VF + max(FL, n / 2)) * CYC)
-        FIN = a(SC, 15, 128, 16)
-        DD = a(P, 152, 160) if "s" in opt else f8(13)
-        it = [(DD, IF, QH, True, False), (DD, IFH, L2H, False, True)] if "s" in opt else []
-        if "d" in opt:
-            if it:
-                mm(it)
-            for e in (0, 1):
-                tt(a(SF, 120 + e, 128, 2), a(SC, 15 + 128 * e, 128 + 112 * e, 32), a(SF, 112 + e, 120, 2), ALU.add)
-            for e in (0, 1):
-                ts(a(U, 288 + e, 296, 2), a(SF, 120 + e, 128, 2), BIG, ALU.mult, col(17 if e else PR), ALU.max)
-        elif "x" in opt:
-            XX = a(P, 160, 168)
-            mm(it + [(XX, CX, a("ones", 0, 8, 1, 2), True, False), (XX, IFH, L2H, False, False), (XX, IKP, FIN, False, True)])
-            ts(a(U, 288, 304, 2), XX, -1.0, ALU.mult, col(PR), ALU.max)
-        else:
-            if it:
-                mm(it)
-            tt(f8(15), FIN, f8(14), ALU.add)
-            ts(a(U, 288, 304, 2), f8(15), BIG, ALU.mult, col(PR), ALU.max)
-        EQ = a(WF, 128, 272)
-        if "e" in opt:
-            mm([(a(Q, 0, 144), IF, a(LF, 0, 144), True, False)]
-               + [(a(Q, 8 * k, 8 * k + 8), IFH, L2H, False, k == 16) for k in range(17)])
-            act(YA, a(Q, 0, 144), ACT.Abs)
-            act(EQ, YA, ACT.Relu, bias=1.0, scale=-1.0)
-        B = a(Q, 256, 384)
-        if "c" in opt:
-            act(C1, DL, ACT.Relu, bias=-8.0)
-            act(C2, DL, ACT.Relu, bias=-8.0, scale=-1.0)
-            mm([(B, I1, A0, True, False), (B, I1, C1, False, False), (B, IN, C2, False, True)])
-        else:
-            ts(CL, DL, -8.0, ALU.max, 8.0, ALU.min)
-            mm(([(B, I1, XL, True, False)] if "l" in opt else [(B, I1, A0, True, False), (B, I1, DL, False, False)])
-               + [(B, IN, CL, False, True)])
-        act(TB, B)
-        z = 2 if "d" in opt else 1
-        for m in range(8 // z - 1, -1, -1):
-            cp(ind(a(XN, 0, X0 + W), a(U, 288 + 2 * m, 288 + 2 * m + z)), a(WB, 1024 + 16 * z * m, 1024 + 16 * z * (m + 1)))
-        tag[0] = "u%d%d" % (t, h)
-        last = t == NS - 1
-        GO = a(OF, zone(t + 1), zone(t + 1) + 8)
-        if "s" not in opt:
-            tt(DD, QH, LL, ALU.subtract)
-        if "e" not in opt:
-            tt(EQ, ind(f8(17, 2), BCK), a(LF, 0, 144), ALU.is_equal)
-        if "d" in opt:
-            for e in (0, 1):
-                ts(a(OF, zone(t + 1) + e, zone(t + 1) + 8, 2), a(SC, 15 + 128 * e, 128 + 112 * e, 32), 0.5, ALU.is_gt)
-        else:
-            ts(GO, FIN, 0.5, ALU.is_gt)
-        tt(DE, DD, GO, ALU.mult)
-        LF2, LB2 = "LF%d%d" % (t + 1, h), "LB%d%d" % (t + 1, h)
-        TT = a(WF, 272, 416) if last else a(OF, 0, 144)
-        tt(TT, ind(f8(19, 2), BCK), a(WF, 128, 272), ALU.mult)
-        if not last:
-            lo = min(0, zone(t + 1))
-            send([a(LF2, lo, lo + 152)], [a(LF, lo, lo + 152), a(OF, lo, lo + 152)], "arrF%d%d" % (t, h))
-        if "v" in opt:
-            mm(margin(a(P, 0, 128), True))
-            act(SS, a(P, 0, 128), ACT.Sign, bias=-2.0 ** -13)
-            for o, r, pos, neg in ((a(S, 128, 256), R1, I1, IN), (a(Q, 384, 512), R2, IN, I1)):
-                mm(([(o, pos, XQ, True, False), (o, neg, A0, False, False)] if "q" in opt else [(o, pos, DQ, True, False)])
-                   + [(o, IN, SS, False, True)])
-                act(r, o, ACT.Relu, bias=-1.0)
-            G = a(S, 256, 384)
-            mm(([(G, I1, XQ, True, False)] if "q" in opt else [(G, I1, A0, True, False), (G, I1, DQ, False, False)])
-               + [(G, IN, R1, False, False), (G, I1, R2, False, True)])
-            act(a(OB, 0, 128), G)
-            srcs = [a(OB, 0, 128)]
-        else:
-            tt(f8(16), GO, f8(0), ALU.mult)
-            ts(a(U, 272, 280), f8(16), 128.0, ALU.add)
-            cw = ind(a(WB, 1408, 1552), a(U, 272, 280))
-            if last:
-                tt(a(OB, 0, 128), cw, A0, ALU.add)
-            else:
-                act(a(OB, 0, 128), cw)
-            srcs = [A0, a(OB, 0, 128)]
-        if not last:
-            send([a(LB2, 0, 128), a(LB2, 128, 256)], srcs, "arrB%d%d" % (t, h))
-            return
-        ZA, ZB, tr = "ZA%d" % h, "ZB%d" % h, "tr%d" % h
-        tt(nd(ZA, None, None, None, None), a(WF, 272, 400), a(LF, 0, 128), ALU.add)
-        for src, dst in ((ZA, ZB), (ZB, ZA), (ZA, ZB)):
+    def rising(h):
+        t = NS - 1
+        tag[0] = "s%d%d" % (t, h)
+        LF, LB, P, Q, S, U, WI, WB = names(t, h)
+        ZA, ZB, tr, OF, HH, WF, SF, E = "ZA%d" % h, "ZB%d" % h, "tr%d" % h, "OF%d%d" % (t, h), "hh%d" % h, "wf%d" % h, "sf%d" % h, "E%d" % h
+        for x in (0, 1):
+            for j, op in enumerate((ALU.min, ALU.max)):
+                tt(nd(ZB, x, None, j, None), a(LF, 64 * x, 64 * x + 32), a(LF, 64 * x + 32, 64 * x + 64), op)
+        for src, dst in ((ZB, ZA), (ZA, ZB)):
             for j, op in enumerate((ALU.min, ALU.max)):
                 tt(nd(dst, None, None, j, None), nd(src, None, (0, 2), None, None), nd(src, None, (2, 4), None, None), op)
         od, ev = nd(ZB, 0, None, None, None), nd(ZB, 1, None, None, None)
@@ -649,31 +489,209 @@ def build(cfg):
         act(a(tr, 0, 256), ind(a(tr, 512, 640), T2W))
         transpose(tr)
         act(a(OF, 0, 128), ind(a(tr, 256, 512), W2N))
-        send([a(LB2, 0, 128)], [a(OB, 0, 128)], "arrB%d%d" % (t, h))
-        tt(f8(22), nd(ZB, 0, 0, 0, None), nd(ZB, 1, 0, 0, None), ALU.subtract)
-        tt(f8(23), f8(22), SG, ALU.mult)
-        ts(a(U, 280, 288), f8(23), 0.0, ALU.is_gt)
-        act(a(OF, 128, 256), ind(a("pm", 0, 16), a(U, 280, 288)))
-        send([a(LF2, 0, 256)], [a(OF, 0, 256)], "arrF%d%d" % (t, h))
+        RS = a(HH, 16, 144)
+        act(RS, a(OF, 0, 128))
+        mm([(a(E, 0, 128), SU, RS, True, True), (a(E, 128, 256), SD, RS, True, True)])
+        act(a(WF, 512, 640), a(E, 0, 128), bias=col(BU))
+        act(a(WF, 640, 768), a(E, 128, 256), bias=col(BD))
+        tt(a(SF, 176, 184), nd(ZB, 0, 0, 0, None), nd(ZB, 1, 0, 0, None), ALU.subtract)
+        tt(a(SF, 184, 192), a(SF, 176, 184), a(LF, 136, 144), ALU.mult)
+        act(a(U, 280, 288), a(SF, 184, 192), ACT.Sign)
+        act(a(WB, 2960, 3088), ind(a("pm", 0, 16), a(U, 280, 288)))
+
+    def back(t, h):
+        tag[0] = "b%d%d" % (t, h)
+        LF, LB, P, Q, S, U, WI, WB = names(t, h)
+        KB, SI, SF, WF, VB, SC, HH, E = ["%s%d" % (x, h) for x in ("KB", "si", "sf", "wf", "VB", "SC", "hh", "E")]
+        OF, OB = "OF%d%d" % (t, h), "OB%d%d" % (t, h)
+        last = t == NS - 1
+        A0 = a(LB, 0, 128)
+        f8 = lambda j, n=1: a(SF, 8 * j, 8 * (j + n))
+        opt = cfg["opt"][last]
+        for r in ((0, 1), (1, 3)) if "f" in opt else ((0, 3),):
+            tt(nd(KB, r, None), nd(KB, r, None), a(S, 272 + 64 * r[0], 272 + 64 * r[1]), ALU.min)
+            tt(nd(KB, r, (0, 32)), nd(KB, r, (0, 32)), nd(KB, r, (32, 64)), ALU.min)
+            tt(nd(KB, r, (0, 16)), nd(KB, r, (0, 16)), nd(KB, r, (16, 32)), ALU.min)
+            tt(a(SI, 8 * r[0], 8 * r[1]), nd(KB, r, (0, 8)), nd(KB, r, (8, 16)), ALU.min)
+            if r[1] == 1 and "b" in opt:
+                ts(a(U, 256, 264), a(SI, 0, 8), W - 1, ALU.bitwise_and)
+            else:
+                ts(a(SI, 24 + 8 * r[0], 24 + 8 * r[1]), a(SI, 8 * r[0], 8 * r[1]), (1 << 24) + W - 1, ALU.bitwise_and)
+        QI, EV, OD = [a(SI, 24 + 8 * j, 32 + 8 * j) for j in range(3)]
+        UQ, UL = a(U, 256, 264), a(U, 264, 272)
+        if "b" in opt:
+            QI = UQ
+        else:
+            ts(UQ, QI, W - 1.0, ALU.min)
+        GT, AQ, DL, RL, CL, TB = [a(WB, 128 * j, 128 * j + 128) for j in (2, 3, 4, 5, 7, 8)]
+        XQ, SS, R1, R2, S2, PEN, MK = [a(WB, 1664 + 128 * j, 1792 + 128 * j) for j in range(7)]
+        YA, NE = a(WB, 2560, 2704), a(WB, 2704, 2960)
+        qw = ind(a("X", TW, TW + W), UQ)
+        PG_ = "pg%d" % h
+        tt(GT, qw, A0, ALU.is_gt)
+        act(XQ, qw)
+        DQ = a(Q, 256, 384)
+        mm([(DQ, I1, XQ, True, False), (DQ, IN, A0, False, True)])
+        act(AQ, DQ, ACT.Abs)
+        if "v" in opt:
+            ts(R2, DQ, -2.0, ALU.max, 2.0, ALU.min)
+        LH, L16, Q16, RS = a(HH, 0, 8), a(HH, 144, 272), a(HH, 272, 400), a(HH, 16, 144)
+        SG, L, LL, DE, DF, HI, LO = a(LF, 136, 144), f8(1), f8(17), f8(19), f8(8), f8(10), f8(9)
+        tt(DF, EV, OD, ALU.subtract)
+        if "a" in opt:
+            tt(a(PG_, 31, 256, 32), DF, SG, ALU.mult)
+            tt(HI, EV, OD, ALU.max)
+            tt(LO, EV, OD, ALU.min)
+            mm([(a(S, 0, 256), C75, a("CC", 512, 768, 1, 1), True, False), (a(S, 0, 256, 2), BL1, GT, False, True)])
+            scan(a(WF, 128, 384), a(PG_, 0, 256), a(S, 0, 256))
+            tt(f8(12), a(WF, 159, 384, 32), HI, ALU.min)
+            tt(L, f8(12), LO, ALU.max)
+            ts(UL, L, float(W), ALU.min)
+            ts(LH, L, float(W), ALU.min)
+        else:
+            tt(LO, DF, SG, ALU.mult)
+            tt(HI, EV, OD, ALU.add)
+            mm([(a(S, 0, 128), BLK, GT, True, True)])
+            scan(a(WF, 272, 400), a("pg0", 0, 128), a(S, 0, 128))
+            act(f8(11), a(WF, 287, 400, 16), ACT.Sign, bias=a("ci", 111, 112))
+            tt(f8(12), f8(11), LO, ALU.mult)
+            tt(L, f8(12), HI, ALU.add)
+            ts(UL, L, 0.5, ALU.mult, float(W), ALU.min)
+            if "h" in opt:
+                act(LH, UL)
+            else:
+                ts(LH, L, 0.5, ALU.mult, float(W), ALU.min)
+        tt(DL, ind(a("X", TW, TW + W + 16), UL), A0, ALU.subtract)
+        LS = UL if "h" in opt else LH
+        act(f8(24), LS, scale=-1.0)
+        act(L16, ind(a("iota", 0, W + 8), UL))
+        for m in range(8):
+            lo, k = (16 * m - 16, 32) if m % 2 else (16 * m, 16)
+            act(a(WB, 2704 + 32 * m, 2704 + 32 * m + k), a(HH, 144 + lo, 144 + lo + k), ACT.Abs, bias=a(SF, 192 + m, 193 + m))
+        act(RL, DL, ACT.Abs)
+        EE, two = a(P, 256, 512), [nd(P, (4, 8), (0, 32)), nd(P, (4, 8), (32, 64))]
+        mm([(a(P, 256 + 64 * j, 320 + 64 * j), IN, a("mask", 0, 64), j == 0, False) for j in range(4)]
+           + [(o, BLK, AQ, False, False) for o in two])
+        mm([(o, NBLK, RL, False, o is two[1]) for o in two])
+        tt(a(VB, 0, 256), EE, NE, ALU.is_gt)
+        FIN = a(SC, 31, 256, 32)
+        if "d" in opt:
+            act(f8(14), LH, bias=float(X0))
+            scan(a(SC, 0, 256), a("d0", 256, 512), a(VB, 0, 256))
+            for m in range(7, -1, -1):
+                ts(a(U, 288 + m, 289 + m), a(SC, 31 + 32 * m, 32 + 32 * m), a(SF, 112 + m, 113 + m), ALU.mult, col(PS if m % 2 else PR), ALU.max)
+            if not last:
+                scan(a(SC, 256, 512), a("d0", 512, 768), a(VB, 0, 256))
+        else:
+            act(f8(14), LS, bias=X0 / BIG - 1.0, scale=1.0 / BIG)
+            scan(a(SC, 0, 256), a("d0", 0, 256), a(VB, 0, 256))
+            tt(f8(15), FIN, f8(14), ALU.add)
+            for e in (0, 1):
+                ts(a(U, 288 + e, 296, 2), a(SF, 120 + e, 128, 2), BIG, ALU.mult, col(PS if e else PR), ALU.max)
+        EQ = a(WF, 128, 272)
+        if not last and "e" in opt:
+            act(LL, LH)
+        if not last and "e" not in opt:
+            mm([(a(Q, 0, 144), I1, a(LF, 0, 144), True, False)]
+               + [(a(Q, 8 * k, 8 * k + 8), IN, LH, False, k == 16) for k in range(17)])
+            act(YA, a(Q, 0, 144), ACT.Abs)
+            act(EQ, YA, ACT.Relu, bias=1.0, scale=-1.0)
+        B = a(Q, 256, 384)
+        if "c" in opt:
+            act(CL, DL, ACT.Relu, bias=-8.0)
+            act(MK, DL, ACT.Relu, bias=-8.0, scale=-1.0)
+            mm([(B, I1, A0, True, False), (B, I1, CL, False, False), (B, IN, MK, False, True)])
+        else:
+            ts(CL, DL, -8.0, ALU.max, 8.0, ALU.min)
+            mm([(B, I1, A0, True, False), (B, I1, DL, False, False), (B, IN, CL, False, True)])
+        act(TB, B)
+        for m in range(3, -1, -1):
+            cp(ind(a("X", 0, TW), a(U, 288 + 2 * m, 290 + 2 * m)), a(WB, 1024 + 32 * m, 1056 + 32 * m))
+        tag[0] = "u%d%d" % (t, h)
+        LF2, LB2 = "LF%d%d" % (t + 1, h), "LB%d%d" % (t + 1, h)
+        MG = a(P, 0, 128)
+        if not last:
+            GO = a(OF, zone(t + 1), zone(t + 1) + 8)
+            if "R" not in opt:
+                tt(f8(13), QI, LS, ALU.subtract)
+            if "r" in opt or "R" in opt:
+                scan(a(SC, 256, 512), a("d0", 512, 768), a(VB, 0, 256))
+            if "R" in opt:
+                tt(DE, QI, LH, ALU.subtract)
+                tt(a(HH, 272, 416), ind(f8(19, 2), BCK), EQ, ALU.mult)
+                act(GO, a(SC, 287, 512, 32))
+            elif "d" in opt or "r" in opt:
+                tt(DE, f8(13), a(SC, 287, 512, 32), ALU.mult)
+                act(GO, a(SC, 287, 512, 32))
+            else:
+                ts(GO, FIN, 0.5, ALU.is_gt)
+                tt(DE, f8(13), GO, ALU.mult)
+            if "R" in opt:
+                tt(a(OF, 0, 144), ind(a(SC, 256, 512), a("lst", 112, 121)), a(HH, 272, 416), ALU.mult)
+            elif "e" in opt:
+                for m in range(8):
+                    ts(a(OF, m, 136, 8), a(LF, m, 136, 8), a(SF, 136 + m, 137 + m), ALU.is_equal, a(SF, 152 + m, 153 + m), ALU.mult)
+            else:
+                tt(a(OF, 0, 144), ind(f8(19, 2), BCK), EQ, ALU.mult)
+            lo = min(0, zone(t + 1))
+            send([a(LF2, lo, lo + 152)], [a(LF, lo, lo + 152), a(OF, lo, lo + 152)], "arrF%d%d" % (t, h))
+        mm([(MG, BLK, AQ, True, False), (MG, NBLK, RL, False, True)])
+        if last:
+            OG, GU, GD, T1, DC, PP_ = "OG%d" % h, a(WF, 512, 640), a(WF, 640, 768), a(WF, 768, 896), a(WF, 896, 1024), a(WF, 0, 128)
+            act(Q16, ind(a("iota", 0, W + 8), UQ))
+            mm([(a(E, 256, 384), I1, Q16, True, False), (a(E, 256, 384), IN, RS, False, True)])
+            T1 = a(E, 256, 384)
+            tt(T1, T1, GD, ALU.max)
+            tt(DC, T1, GU, ALU.min)
+            mm([(a(E, 384, 512), I1, RS, True, False), (a(E, 384, 512), IN, L16, False, True)])
+            tt(PP_, a(E, 384, 512), DC, ALU.mult)
+            act(PEN, PP_, ACT.Relu, scale=-4096.0)
+            tt(T1, MG, PEN, ALU.is_gt)
+            tt(a(OG, 0, 128), T1, DC, ALU.mult)
+            M2, M3 = a(S, 0, 128), a(S, 384, 512)
+            mm([(M2, BLK, AQ, True, False), (M2, NBLK, RL, False, False), (M2, NBLK, PEN, False, True)])
+            act(S2, M2, ACT.Sign, bias=-2.0 ** -13)
+            mm([(M3, I1, S2, True, False), (M3, I1, a(WB, 2960, 3088), False, True)])
+            act(a(OF, 128, 256), M3, ACT.Abs)
+            send([a(LF2, 0, 256)], [a(OF, 0, 256), a(OG, 0, 256)], "arrF%d%d" % (t, h))
+        act(SS, MG, ACT.Sign, bias=-2.0 ** -13)
+        if "v" in opt:
+            act(a(Q, 384, 512), SS, ACT.Relu)
+            tt(a(OB, 0, 128), a(Q, 384, 512), R2, ALU.mult)
+        else:
+            for o, r, pos, neg in ((a(S, 128, 256), R1, I1, IN), (a(Q, 384, 512), R2, IN, I1)):
+                mm([(o, pos, XQ, True, False), (o, neg, A0, False, False), (o, IN, SS, False, True)])
+                act(r, o, ACT.Relu, bias=-1.0)
+            G = a(S, 256, 384)
+            mm([(G, I1, XQ, True, False), (G, IN, R1, False, False), (G, I1, R2, False, True)])
+            act(a(OB, 0, 128), G)
+
+    def levels(t, h):
+        tag[0] = "u%d%d" % (t, h)
+        LB2, last = "LB%d%d" % (t + 1, h), t == NS - 1
+        send([a(LB2, 0, 128)] + ([] if last else [a(LB2, 128, 256)]),
+             ([a("LB%d%d" % (t, h), 0, 128)] if "v" in cfg["opt"][last] else []) + [a("OB%d%d" % (t, h), 0, 128)], "arrB%d%d" % (t, h))
+        if not last:
+            ops[-1]["after"] = [i for i, o in enumerate(ops) if o["sem"] == "arrF%d0" % t]
 
     for t in range(NS):
-        tag[0] = "copy"
-        X, XN = "X%d" % (t % 2), "X%d" % ((t + 1) % 2)
         if t > 0:
             tag[0] = "twin"
-            dma(a(X, X0 + W, X0 + 2 * W), a(X, X0, X0 + W), "tw%d" % t, 524288)
-            tag[0] = "copy"
-        dma(a(XN, X0, X0 + W), a(X, X0, X0 + W), "cp%d" % t, 1048576)
+            dma(a("X", TW, TW + W), XM, "tw%d" % t, 524288)
         for h in ORDER:
             front(t, h)
+        for h in ORDER if t == NS - 1 else ():
+            rising(h)
         for h in ORDER:
             back(t, h)
+        for h in ORDER:
+            levels(t, h)
     tag[0] = "end"
-    dma(dram("yx"), a("X%d" % (NS % 2), X0, X0 + W), "stX", 524288)
+    dma(dram("yx"), XM, "stX", 524288)
     for h in ORDER:
         LF, LB = "LF%d%d" % (NS, h), "LB%d%d" % (NS, h)
         dma(dram("yr", 128 * h, 128 * h + 128), a(LF, 0, 128), "stR%d" % h, 65536)
-        dma(dram("ya", 128 * h, 128 * h + 128), a(LB, 0, 128), "stA%d" % h, 32768)
+        dma(dram("ya", 128 * h, 128 * h + 128), a(LB, 0, 128), "stA%d" % h, 32768, "A")
         dma(dram("ys", 128 * h, 128 * h + 128), a(LF, 128, 256, 1, -16), "stS%d" % h, 4096, "A")
     return ops
 
@@ -681,7 +699,7 @@ def build(cfg):
 def link(ops):
     hist = {}
     for i, o in enumerate(ops):
-        deps = {}
+        deps = {j: False for j in o.get("after", ())}
         for kind, lst in (("r", o["rd"]), ("w", o["wr"])):
             for name, lo, hi in lst:
                 ps = SCRATCH[name][0] == "psum"
@@ -721,9 +739,6 @@ def arrange(ops, cfg):
     for i in range(n - 1, -1, -1):
         o = ops[i]
         prio[i] = o["cost"] + o["lat"] + max([prio[j] + (LAT if ops[j]["deps"][i] else 0.0) for j in succ[i]] + [0.0])
-    for i in range(n):
-        g = ops[i]["tag"]
-        prio[i] += cfg["boost"].get(g[0] + g[2:], 0.0) + cfg["fine"].get(ops[i]["key"], 0.0)
     left = [len(o["deps"]) for o in ops]
     ready = {e: [] for e in "VATGS"}
     avail = [0.0] * n
@@ -801,8 +816,8 @@ def improve(ops, cfg):
         g = o["tag"]
         seen[g, o["key"]] = seen.get((g, o["key"]), 0) + 1
         each = len(g) == 3 and g != "end"
-        key.append(g if g in ("copy", "twin") else ("" if each and g[:2] not in ("f0", "b3", "u3") else g) + o["key"].replace("X1", "X0") + "#%d" % seen[g, o["key"]])
-        step.append(int(o["sem"][2]) if g in ("copy", "twin") else int(g[1]) if each else 0)
+        key.append(g if g == "twin" else ("" if each and g[:2] not in cfg["own"] else g) + o["key"] + "#%d" % seen[g, o["key"]])
+        step.append(int(o["sem"][2]) if g == "twin" else int(g[1]) if each else 0)
     first = [min(o["start"] for o in ops if o["tag"] == "f%d1" % t and o["eng"] == "V") for t in range(NS)]
     period = (first[3] - first[1]) / 2
     tau = {}
@@ -826,36 +841,50 @@ def improve(ops, cfg):
         models.append(([o["cost"] for o in alt], [o["lat"] for o in alt],
                        [[(j, alt[j]["lat"] + (m["lat"] if o["deps"][j] else 0.0)) for j in d] for o, d in zip(ops, deps)]))
 
-    def run():
-        at = [0.0] * n
-        for i in range(n):
-            x = tau[key[i]] + period * step[i]
-            for j in deps[i]:
+    rows = [(key[i], period * step[i], deps[i]) for i in range(n)]
+    ends = [i for i, o in enumerate(ops) if o["tag"] == "end"]
+
+    def run(was, room):
+        at = []
+        for k, x, d in rows:
+            x += tau[k]
+            for j in d:
                 if at[j] > x:
                     x = at[j]
-            at[i] = x
+            at.append(x)
         seq = sorted(range(n), key=lambda i: at[i])
-        total, arcs = 0.0, []
-        for cost, lat, pre in models:
-            fin, free, last, why, end, top = [0.0] * n, [0.0] * 5, [-1] * 5, [0] * n, 0.0, 0
+        out, fins, over = [], [], 0.0
+        for (cost, lat, pre), old in zip(models, was):
+            fin, free = [0.0] * n, [0.0] * 5
             for i in seq:
                 e = eng[i]
-                s, w = free[e], -2 - last[e]
+                s = free[e]
                 for j, d in pre[i]:
-                    if fin[j] + d > s:
-                        s, w = fin[j] + d, j
-                s += cost[i]
-                why[i], free[e], fin[i], last[e] = w, s, s, i
-                if s + lat[i] > end:
-                    end, top = s + lat[i], i
-            total += end
-            while why[top] != -1:
-                if why[top] < 0:
-                    arcs.append((-2 - why[top], top))
-                    top = -2 - why[top]
+                    d += fin[j]
+                    if d > s:
+                        s = d
+                free[e] = fin[i] = s + cost[i]
+            out.append(max(fin[i] + lat[i] for i in ends))
+            fins.append(fin)
+            over += out[-1] - old
+            if over > room + 150.0 * (len(models) - len(out)):
+                return None
+        return out, fins, seq
+
+    def tight(fins, seq):
+        before, last, arcs = [-1] * n, [-1] * 5, []
+        for i in seq:
+            before[i], last[eng[i]] = last[eng[i]], i
+        for (cost, lat, pre), fin in zip(models, fins):
+            i = max(ends, key=lambda i: fin[i] + lat[i])
+            while i >= 0:
+                s, j = fin[i] - cost[i], before[i]
+                if j >= 0 and fin[j] > s - 0.01:
+                    arcs.append((j, i))
                 else:
-                    top = why[top]
-        return total / len(models), arcs, seq
+                    j = next((j for j, d in pre[i] if fin[j] + d > s - 0.01), -1)
+                i = j
+        return arcs
 
     seed = [cfg["seed"]]
 
@@ -864,9 +893,21 @@ def improve(ops, cfg):
         return seed[0] / 2147483648.0
 
     keys = sorted(tau)
-    cur, arcs, seq = run()
-    best = (cur, seq)
-    for r in range(cfg["rounds"]):
+    cur, fins, seq = run([1e9] * len(models), 0.0)
+    arcs = tight(fins, seq)
+    best = (sum(cur), seq)
+    best += (fins[0],)
+    same, heat, span, r0 = 2, cfg["heat"], cfg["rounds"], 0
+    for r in range(cfg["rounds"] + cfg["apart"]):
+        if r == cfg["rounds"]:
+            for i, o in enumerate(ops):
+                key[i], step[i] = "%-4s%d" % (o["tag"][:4], i), 0
+                tau[key[i]] = best[2][i] - models[0][0][i]
+                rows[i] = (key[i], 0.0, deps[i])
+            keys = sorted(key)
+            cur, fins, seq = run([1e9] * len(models), 0.0)
+            arcs = tight(fins, seq)
+            same, heat, span, r0 = 3, cfg["heat2"], cfg["apart"], r
         far = (1.0, 1.0, 100.0, 400.0, 1000.0, 3000.0)[int(6 * rnd())] * rnd()
         u = rnd()
         j, i = arcs[int(len(arcs) * rnd())]
@@ -881,14 +922,16 @@ def improve(ops, cfg):
             k = key[i] if u < 0.9 else key[j]
             wide, by = 3000.0 * rnd(), (-1500.0 if u < 0.9 else 1500.0) * rnd()
             side = 1.0 if rnd() < 0.5 else -1.0
-            new = {x: tau[x] + by for x in keys if x[:2] == k[:2] and 0.0 <= (tau[k] - tau[x]) * side <= wide}
+            new = {x: tau[x] + by for x in keys if x[:same] == k[:same] and 0.0 <= (tau[k] - tau[x]) * side <= wide}
         old = {k: tau[k] for k in new}
         tau.update(new)
-        s, a2, seq = run()
-        if s <= cur or rnd() < math.exp((cur - s) / (3.0 + cfg["heat"] * (1.0 - r / cfg["rounds"]))):
-            cur, arcs = s, a2
-            if s < best[0]:
-                best = (s, seq)
+        got = run(cur, -math.log(1.0 - rnd()) * len(models) * (3.0 + heat * (1.0 - (r - r0) / span)))
+        if got:
+            if got[0] != cur or r % 8 == 0:
+                arcs = tight(got[1], got[2])
+            cur = got[0]
+            if sum(cur) < best[0]:
+                best = (sum(cur), got[2], got[1][0])
         else:
             tau.update(old)
     order = {e: [i for i in best[1] if ops[i]["eng"] == e] for e in "VATGS"}
@@ -964,7 +1007,7 @@ def rank_program(g, core, T, topo):
                     q.remote_dma(dsts[0], srcs[0], T.sem[o["sem"]], T.sem.sent, pid, rid, mask)
                 else:
                     q.remote_dma_fused([RemoteDMATransfer(dst_ids=[DstId(rid=rid, pnc=pid)] * len(dsts), dma_engine_mask=mask,
-                                                          remote_sem=T.sem[o["sem"]], srcs=srcs, dsts=dsts, alu_op=len(srcs) - 1)],
+                                                          remote_sem=T.sem[o["sem"]], srcs=srcs, dsts=dsts, alu_op=min(1, len(srcs) - 1))],
                                        local_sem=T.sem.sent)
                 sent += len(eng)
             else:

import math
from concourse.bass import DstId, RemoteDMATransfer
from concourse.mybir import AluOpType, ActivationFunctionType

ALU = AluOpType
ACT = ActivationFunctionType
NS, HOP, W = 4, 3, 2048
ORDER = (1, 0)
X0, BIG = 32, 262144.0
TW = X0 + W
RT = "float16"
CFG = {"bmode": {(1, 1): "WW", (1, 0): "ZZ", (0, 1): "ZY", (0, 0): "YZ"},
       "aeng": {(1, 1): "VA", (1, 0): "VA", (0, 1): "VA", (0, 0): "AA"},
       "slack": 30.0, "lat": 170.0, "passes": 1, "wire": 2500.0, "cyc": 0.9, "pec": 0.56,
       "rounds": 30000, "apart": 30000, "seed": 5, "heat": 30.0, "heat2": 5.0, "opt": ("vfqi", "vf"), "own": ("s3", "b3", "u3"), "lin": (0, 1), "dl": 1200.0,
       "models": ({"cyc": 1.04, "pec": 0.59, "lat": 100.0, "wire": 2600.0, "gc": 400.0, "dl": 1000.0},
                  {"cyc": 0.9, "pec": 0.52, "lat": 200.0, "wire": 3200.0, "gc": 450.0, "dl": 1000.0},
                  {"cyc": 1.2, "pec": 0.7, "ga": 1.9, "sca": 5.0, "lat": 200.0, "wire": 3600.0, "gc": 500.0})}

SCRATCH = {}


def _buf(name, cols, dtype, where="sbuf"):
    SCRATCH[name] = (where, [128] + (list(cols) if isinstance(cols, tuple) else [cols]), dtype)


_buf("X", X0 + 2 * W + 16, "bfloat16")
_buf("iota", W + 8, "float32")
for _n, _c, _d in (("RI", 256, "int32"), ("sgI", 256, "int32"), ("sgB", 256, "bfloat16"), ("wI", 8, "int32"),
                   ("pI", 16, "int32"), ("pF", 24, "float32"), ("ci", 776, "float32"), ("lst", 128, "uint16"),
                   ("ones", 144, "bfloat16"), ("Z8", 144, "bfloat16"), ("Zw", 144, "bfloat16"),
                   ("Zn", 144, "bfloat16"), ("G8", 16, "bfloat16"), ("Ik", 1408, "bfloat16"), ("CC", 768, "bfloat16"),
                   ("sameB", 128, "bfloat16"), ("blk", 128, "bfloat16"), ("nblk", 128, "bfloat16"), ("mask", 64, "bfloat16"),
                   ("d0", 768, "bfloat16"), ("pm", 16, "bfloat16")):
    _buf(_n, _c, _d)
for _h in (0, 1):
    for _t in range(NS + 1):
        _buf("LF%d%d" % (_t, _h), *((160, RT) if _t < NS else (264, "float32")))
        _buf("LB%d%d" % (_t, _h), 256, "bfloat16")
    for _t in range(NS):
        _buf("OF%d%d" % (_t, _h), *((160, RT) if _t < NS - 1 else (264, "float32")))
        _buf("OB%d%d" % (_t, _h), 256, "bfloat16")
    for _n, _c, _d in (("XR", 2048, "bfloat16"), ("D", 2048, "bfloat16"), ("AD", 2048, "bfloat16"),
                       ("u16", 320, "uint16"), ("wi", 1168, "int32"), ("KB", (3, 64), "float32"),
                       ("si", 64, "int32"), ("sf", 208, "float32"), ("wb", 3200, "bfloat16"), ("hh", 416, RT), ("wf", 1024, "float32"),
                       ("tr", 640, "float32"), ("VB", 256, "bfloat16"), ("SC", 512, "bfloat16"), ("pg", 256, "bfloat16"),
                       ("OG", 256, "float32"),
                       ("ZA", (2, 4, 2, 8), "float32"), ("ZB", (2, 4, 2, 8), "float32")):
        _buf("%s%d" % (_n, _h), _c, _d)
    _buf("P%d" % _h, (8, 64), "float32", "psum")
    for _n in ("Q", "S", "E"):
        _buf("%s%d" % (_n, _h), 512, "float32", "psum")

DMAS = (["ldR", "ldW", "ldS", "ldX0", "ldX1", "tw1", "tw2", "tw3", "stX"]
        + ["%s%d" % (a, h) for a in ("ldA", "ldB", "stR", "stA", "stS") for h in (0, 1)])
SEMAPHORES = ["V", "A", "T", "G", "sent"] + DMAS + ["arr%s%d%d" % (x, t, h) for x in "FB" for t in range(NS) for h in (0, 1)]


def a(name, lo, hi, step=1, p=128):
    if name[:2] in ("LF", "OF"):
        lo, hi = lo + 8, hi + 8
    shape = SCRATCH[name][1][1:]
    if len(shape) == 2:
        c = shape[1]
        if lo // c == (hi - 1) // c:
            return ("n", name, (lo // c, (lo % c, lo % c + hi - lo, step)), p)
        return ("n", name, ((lo // c, hi // c, 1), (0, c, 1)), p)
    return ("n", name, ((lo, hi, step),), p)


def nd(name, *ix):
    shape = SCRATCH[name][1][1:]
    return ("n", name, tuple((0, n, 1) if x is None else (x + (1,) if isinstance(x, tuple) else x) for x, n in zip(ix, shape)), 128)


def ind(win, off):
    return ("i", win, off)


def dram(name, lo=None, hi=None):
    return ("d", name, lo, hi)


def real(T, s):
    if not isinstance(s, tuple):
        return s
    if s[0] == "n":
        return T[s[1]][(slice(0, s[3]) if s[3] > 0 else slice(0, 128, -s[3]),) + tuple(slice(x[0], x[1], x[2] if x[2] != 1 else None) if isinstance(x, tuple) else x for x in s[2])]
    if s[0] == "d":
        return T[s[1]][:] if s[2] is None else T[s[1]][:, s[2]:s[3]]
    return real(T, s[1]).indirect(real(T, s[2]))


def count(s):
    if s[0] == "i":
        return 16 * count(s[2])
    n = 1
    for x in s[2]:
        if isinstance(x, tuple):
            n *= len(range(*x))
    return n


def spans(s):
    if not isinstance(s, tuple) or s[0] == "d":
        return []
    if s[0] == "i":
        return spans(s[1]) + spans(s[2])
    shape = SCRATCH[s[1]][1][1:]
    at = [0]
    for x, n in zip(s[2][:-1], shape):
        at = [v * n + r for v in at for r in (range(*x) if isinstance(x, tuple) else [x])]
    x = s[2][-1]
    r = range(*x) if isinstance(x, tuple) else [x]
    if 1 < len(r) <= 17 and len(at) == 1 and x[2] > 1:
        return [(s[1], at[0] * shape[-1] + v, at[0] * shape[-1] + v + 1) for v in r]
    runs = []
    for v in at:
        lo, hi = v * shape[-1] + r[0], v * shape[-1] + r[-1] + 1
        if runs and runs[-1][2] == lo:
            runs[-1] = (s[1], runs[-1][1], hi)
        else:
            runs.append((s[1], lo, hi))
    return runs


def where(s):
    return SCRATCH[s[1]][0] if s[0] != "i" else "sbuf"


def width(s):
    n = s[1] if s[0] != "i" else s[1][1]
    return 2 if SCRATCH[n][2] in ("bfloat16", "uint16", "float16") else 4


def build(cfg):
    ops = []
    tag = ["setup"]
    CYC, PEC, GA, SCA = cfg["cyc"], cfg["pec"], cfg.get("ga", 1.56), cfg.get("sca", 3.8)
    FL = 64

    def add(eng, call, outs, ins, cost, sem=None, lat=0.0):
        wr, rd = [], []
        for s in outs:
            if s[0] == "i":
                wr += spans(s[1])
                rd += spans(s[2])
            else:
                wr += spans(s)
        for s in ins:
            rd += spans(s)
        ops.append({"eng": eng, "call": call, "wr": wr, "rd": rd, "cost": cost + (cfg.get("fix", 0.0) if eng in "VA" else 0.0), "sem": sem, "lat": lat, "tag": tag[0],
                    "key": tag[0][0] + tag[0][2:] + eng + (wr[0][0][:2] + str(wr[0][1]) if wr else str(sem))})

    def vcost(out, ins, tt=False):
        n = count(out)
        if out[0] == "i":
            return 50 + SCA * n * CYC
        if ins[0][0] == "i":
            return 50 + GA * n * CYC
        if tt:
            f = 2.0 if all(where(s) == "sbuf" for s in ins) else 1.0
        else:
            f = 0.5 if all(width(s) == 2 for s in [out] + ins) else 1.0
        return max(FL, n * f) * CYC

    def cp(out, in_):
        add("V", lambda q, T: q.tensor_copy(real(T, out), real(T, in_)), [out], [in_], vcost(out, [in_]))

    def tt(out, x, y, op):
        add("V", lambda q, T: q.tensor_tensor(real(T, out), real(T, x), real(T, y), op), [out], [x, y], vcost(out, [x, y], True))

    def ts(out, x, s1, op0, s2=None, op1=None):
        def call(q, T):
            if op1 is None:
                return q.tensor_scalar(real(T, out), real(T, x), real(T, s1), None, op0)
            return q.tensor_scalar(real(T, out), real(T, x), real(T, s1), real(T, s2), op0, op1)
        add("V", call, [out], [x] + [s for s in (s1, s2) if isinstance(s, tuple)], vcost(out, [x]))

    def scan(out, d0, d1):
        add("V", lambda q, T: q.tensor_tensor_scan(real(T, out), real(T, d0), real(T, d1), 0.0, ALU.mult, ALU.add),
            [out], [d0, d1], vcost(out, [d0, d1]))

    def ms(out, v):
        add("V", lambda q, T: q.memset(real(T, out), v), [out], [], max(FL, count(out) * width(out) / 4) * CYC)

    def act(out, in_, func=ACT.Identity, bias=0.0, scale=1.0):
        n = count(out)
        c = 65 + GA * n * CYC if in_[0] == "i" else max(FL, n) * CYC
        if bias == 0.0 and func == ACT.Identity:
            func = ACT.Copy
        if func == ACT.Copy:
            add("A", lambda q, T: q.activation(real(T, out), real(T, in_), func, scale=scale), [out], [in_], c)
        else:
            add("A", lambda q, T: q.activation(real(T, out), real(T, in_), func, bias=real(T, bias), scale=scale), [out],
                [in_] + ([bias] if isinstance(bias, tuple) else []), c)

    def fill(out, v):
        act(out, a("ones", 0, count(out), 1, out[3]), scale=v)

    def gat(eng, out, in_):
        if eng == "V":
            cp(out, in_)
        else:
            act(out, in_)

    def mm(items):
        def call(q, T):
            r = None
            for o, l, x, st, sp in items:
                r = q.matmul(real(T, o), real(T, l), real(T, x), st, sp)
            return r
        add("T", call, [i[0] for i in items], [i[1] for i in items] + [i[2] for i in items],
            60 + sum(max(min(64, count(i[1])), count(i[2])) * (4 if width(i[1]) == 4 else 1) for i in items) * PEC)

    def iota(out, pattern, base=0, cm=0):
        if SCRATCH[out[1]][2] == "int32":
            add("G", lambda q, T: q.iota(real(T, out), pattern, base, cm), [out], [], 130 + 2 * count(out) * CYC)
        else:
            add("G", lambda q, T: q.iota(real(T, out), pattern, base, cm, allow_small_or_imprecise_dtypes=True),
                [out], [], 130 + 2 * count(out) * CYC)

    def select(out, in_, pattern, op, fill_, base, cm):
        add("G", lambda q, T: q.affine_select(real(T, out), real(T, in_), pattern, op, fill_, base, cm), [out], [in_],
            170 + 2 * count(out) * CYC)

    def gfill(out, v):
        if v == int(v) and abs(v) < 1 << 24:
            iota(out, [[0, count(out)]], int(v))
        else:
            select(out, a("ones", 0, count(out), 1, out[3]), [[0, count(out)]], ALU.is_gt, v, -1, 0)

    def dma(out, in_, sem, nbytes, eng="S", after=()):
        add(eng, lambda q, T: q.dma_start(real(T, out), real(T, in_)), [out], [in_] + list(after), 60, sem, cfg["dl"] + nbytes / 300.0)

    def transpose(tr):
        add("V", lambda q, T: q.transpose(T[tr][:, 256:512], T[tr][:, 0:256]), [a(tr, 256, 512)], [a(tr, 0, 256)], 256 * CYC)

    def zwin(name, b, p=128):
        return a(name, 15 - b, 143 - b, 1, p)

    def send(dsts, srcs, sem):
        add("G", ("send", dsts, srcs), dsts, srcs, cfg.get("gc", 250), sem, cfg["wire"])

    def zone(t):
        return 144 if t % 2 else -8

    XM = a("X", X0, TW)
    dma(a("RI", 0, 256), dram("rl"), "ldR", 131072, "A")
    dma(XM, dram("xt"), "ldX0", 600000)
    dma(a("wI", 0, 1), dram("wt"), "ldW", 512, "A")
    dma(a("sgI", 0, 256, 1, 8), dram("sg"), "ldS", 8192, "A")
    for h in ORDER:
        dma(a("LB0%d" % h, 0, 128), dram("av", 128 * h, 128 * h + 128), "ldA%d" % h, 400000, after=[XM])
        dma(a("LB0%d" % h, 128, 256), dram("av", 128 * h, 128 * h + 128), "ldB%d" % h, 400000, after=[XM])
    dma(a("X", TW, TW + W), dram("xt"), "ldX1", 1000000, after=[XM])
    ms(a("ones", 0, 144), 1.0)
    iota(a("pI", 0, 1), [[0, 1]], 0, 1)
    col = lambda j: a("pF", j, j + 1)
    PP, PR, PR7, PG, P31, P16, PR3, PRH, PR1, PW, PN, PT, PS, NR, BU, BD = range(16)
    for j, (sh, mk) in enumerate(((0, 15), (0, 7), (4, 7), (0, 31), (0, 16), (2, 2), (1, 7), (0, 1))):
        ts(a("pI", j + 1, j + 2), a("pI", 0, 1), sh, ALU.arith_shift_right, mk, ALU.bitwise_and)
        cp(col(j + 1), a("pI", j + 1, j + 2)) if j == 0 else None
    cp(col(PP), a("pI", 0, 1))
    cp(a("pF", 2, 9), a("pI", 2, 9))
    cp(col(PW), a("wI", 0, 1))
    ts(col(16), col(PR7), 32.0, ALU.mult, col(P16), ALU.add)
    ts(col(PN), col(16), col(PR3), ALU.add)
    ts(col(17), col(PR1), -8.0, ALU.mult, col(PRH), ALU.add)
    ts(col(PT), col(17), 8.0, ALU.add, 8.0, ALU.mult)
    act(col(PS), col(PR), bias=16.0)
    act(col(NR), col(PR), scale=-1.0)
    ts(col(BU), col(PR), 15.0, ALU.is_equal, 8192.0, ALU.mult)
    ts(col(BD), col(PR), 0.0, ALU.is_equal, -8192.0, ALU.mult)
    DUP, N2T, T2W, W2N, BCK = (a("lst", 0, 32), a("lst", 32, 40), a("lst", 64, 80), a("lst", 80, 88), a("lst", 96, 105))
    for lst, pat, base, c in ((DUP, [[16, 16], [0, 2]], 0, PR), (N2T, [[-1, 2], [4, 4]], 1, PN), (T2W, [[1, 8], [0, 2]], 0, PT)):
        lo, hi = lst[2][0][:2]
        src = a("ci", lo, hi)
        iota(src, pat, base)
        ts(lst, src, col(c), ALU.add)
    IB, IG, IC, I8, IM = a("ci", 128, 256), a("ci", 256, 384), a("ci", 384, 512), a("ci", 384, 392), a("ci", 512, 576)
    iota(IC, [[1, 128]])
    iota(IB, [[0, 8], [1, 16]])
    iota(IG, [[1, 8], [0, 16]])
    iota(IM, [[-100, 2], [100, 2], [1, 16]])
    ts(W2N, I8, 32.0, ALU.mult, col(P31), ALU.add)
    ts(a("lst", 96, 104), I8, 0.0, ALU.mult, col(PR7), ALU.add)
    ts(a("lst", 104, 105), col(PR), 8.0, ALU.min)
    for h in ORDER:
        gfill(a("sf%d" % h, 160, 168), 0.0)
        gfill(a("wb%d" % h, 2704, 2960), 0.0)
        gfill(a("OG%d" % h, 128, 256), -1.0)
        for t in range(NS - 1):
            fill(a("LF%d%d" % (t, h), zone(t + 1), zone(t + 1) + 8), 0.0)
            if "e" in cfg["opt"][0]:
                fill(a("OF%d%d" % (t, h), 136, 144), 0.0)
    ts(a("G8", 0, 8), I8, col(PG), ALU.is_equal)
    fill(a("Zw", 0, 144), 0.0)
    gfill(a("Zn", 0, 144), 0.0)
    ts(a("Zw", 15, 143, 16), a("G8", 0, 8), col(PW), ALU.mult)
    act(a("Zn", 15, 143, 16), a("G8", 0, 8), scale=-4096.0)
    I1, IN, IFP, IFN, BL1, I4N, IKN, IKP, I23, SU, SD = [a("Ik", 128 * j, 128 * j + 128) for j in range(11)]
    C75 = a("CC", 384, 512, 1, 1)
    ts(I1, IC, col(PP), ALU.is_equal)
    for o, v in ((IFP, 1.0 / 256), (IFN, -1.0 / 256), (I4N, -4.0), (IKN, -1024.0), (IKP, 1024.0), (I23, 8388608.0), (IN, -1.0)):
        act(o, I1, scale=v)
    for o, base in ((SU, -1), (SD, 1)):
        select(o, IN, [[-1, 128]], ALU.not_equal, 1.0, base, 1)
    CD, CR, CK = a("CC", 0, 128, 1, 1), a("CC", 128, 256, 1, 2), a("CC", 256, 384, 1, 2)
    gfill(CD, 4.0)
    for lo, v0, v1 in ((128, -255.0 / 512, 1024.0), (256, 3 * 8388608.0, -9216.0)):
        gfill(a("CC", lo, lo + 128, 1, 2), v1)
        gfill(a("CC", lo, lo + 128, 1, 1), v0)
    BLK, NBLK = a("blk", 0, 128), a("nblk", 0, 128)
    ts(a("sameB", 0, 128), IB, col(PR), ALU.is_equal)
    ts(BLK, IG, col(PG), ALU.is_equal, 2.0 ** -12, ALU.mult)
    act(NBLK, BLK, scale=-1.0)
    if "a" in cfg["opt"][0]:
        act(BL1, BLK, scale=2.0 ** 27)
        fill(C75, -7.5 * 32768)
        fill(a("CC", 512, 768, 2, 1), 1.0)
        fill(a("CC", 513, 768, 2, 1), 0.0)
        ts(a("pg1", 0, 256, 2), IB, col(PR), ALU.is_gt, 64.0, ALU.mult)
        act(a("pg0", 0, 256, 2), a("pg1", 0, 256, 2))
        for h in ORDER:
            fill(a("pg%d" % h, 1, 256, 2), 1.0)
    else:
        ts(a("pg0", 0, 128), IB, col(PR), ALU.is_gt, 64.0, ALU.mult)
        act(a("pg0", 128, 144), a("sameB", 0, 16), scale=-7.5 / 4096)
        scan(a("ci", 96, 112), a("pg0", 0, 16), a("pg0", 128, 144))
    act(a("mask", 0, 64), IM, ACT.Relu, bias=col(NR))
    ts(a("ci", 576, 640), IM, col(PR), ALU.is_equal)
    if "R" in cfg["opt"][0]:
        ts(col(18), col(PR7), 32.0, ALU.mult, 31.0, ALU.add)
        ts(a("lst", 112, 121), a("ci", 384, 393), 0.0, ALU.mult, col(18), ALU.add)
    every = cfg["opt"][0] + cfg["opt"][1]
    for lo, v in ([(256, -3.0)] if "d" in every else []) + ([(512, -1.0)] if set("drR") & set(every) else []) + [(0, -65.0 / 64)]:
        for j in range(4):
            act(a("d0", lo + 64 * j, lo + 64 * j + 64), a("ci", 576, 640), bias=1.0, scale=v)
        if lo < 512:
            fill(a("d0", lo, lo + 256, 32), 0.0)
    select(a("Z8", 0, 144, 1, 8), a("ones", 0, 144, 1, 8), [[1, 144]], ALU.is_equal, 0.0, -15, -16)
    iota(a("pm", 0, 16), [[-2, 16]], 1)
    gfill(a("X", TW + W, TW + W + 16), 4096.0)
    iota(a("iota", 0, W + 8), [[1, W + 8]])
    whole = "i" in cfg["opt"][0]
    (act if whole else cp)(a("sgB", 0, 256, 1, 8), a("sgI", 0, 256, 1, 8))
    mm([(a("E0", 0, 16), zwin("Z8", b, 8), a("sgB", b, 256, 16, 8), b == 0, b == 15) for b in range(16)])
    for h in ORDER:
        tr = "tr%d" % h
        (act if whole and h == 0 else cp)(a(tr, 0, 256), ind(a("RI", 0, 256), a("lst", 16 * h, 16 * h + 16)))
        transpose(tr)
        (act if whole and h == 0 else cp)(a("u16%d" % h, 0, 128), ind(a(tr, 256, 512), N2T))
        act(a("LF0%d" % h, 0, 128), ind(a(tr, 256, 512), N2T))
        act(a("LF0%d" % h, 128, 136), a("LF0%d" % h, 64, 72))
        act(a("LF0%d" % h, 136, 144), a("E0", 8 * h, 8 * h + 8))

    def names(t, h):
        return ("LF%d%d" % (t, h), "LB%d%d" % (t, h), "P%d" % h, "Q%d" % h, "S%d" % h, "u16%d" % h, "wi%d" % h, "wb%d" % h)

    def front(t, h):
        tag[0] = "f%d%d" % (t, h)
        LF, LB, P, Q, S, U, WI, WB = names(t, h)
        XR, D, AD, KB = "XR%d" % h, "D%d" % h, "AD%d" % h, "KB%d" % h
        NXT = (72, 0)
        if t > 0:
            (act if "u" in cfg["opt"][0] else cp)(a(U, 0, 128), a(LF, 0, 128))
        SGN, RR, ones2 = a(WB, 1280, 1408), a(S, 128, 256), a("ones", 0, 128, 1, 2)
        raw = lambda o, f, end: [(a(S, o + 64 * f, o + 64 + 64 * f), IFP, a(LF, NXT[f], NXT[f] + 64), True, False),
                                 (a(S, o + 64 * f, o + 64 + 64 * f), IFN, a(LF, 64 * f, 64 * f + 64), False, end)]
        mm(raw(256, 0, True) + raw(256, 1, True))
        act(SGN, a(S, 256, 384), ACT.Sign)
        mm([x for f in (0, 1) for x in raw(0, f, False)
            + [(a(S, 64 * f, 64 * f + 64), I4N, a(WB, 1280 + 64 * f, 1344 + 64 * f), False, False),
               (a(S, 64 * f, 64 * f + 64), CD, a("ones", 0, 64, 1, 1), False, True)]])
        mm([(RR, I1, a(LF, 0, 128), True, False), (RR, IKP, SGN, False, False), (RR, CR, ones2, False, True)])
        for f in (0, 1):
            e = cfg["aeng"][(h, f)]
            for j in range(len(e)):
                w = 64 // len(e)
                c = 64 * f + j * w
                gat(e[j], a(XR, 16 * c, 16 * (c + w)), ind(XM, a(U, c, c + w)))
        TB, GO = a(WB, 1552, 1616), a(LF, zone(t), zone(t) + 8)
        withn = t > 0
        if withn and "n" in cfg["opt"][0]:
            mm([(a(Q, 384, 392), a("sameB", 0, 128), GO, True, True)])
            act(a("sf%d" % h, 0, 8), a(Q, 384, 392))
            act(TB, ind(a("sf%d" % h, 0, 8), a("lst", 96, 100)))
        elif withn:
            mm([(a(Q, 384 + 8 * k, 392 + 8 * k), a("sameB", 0, 128), GO, True, True) for k in range(8)])
            act(TB, a(Q, 384, 448))
        for f in (0, 1):
            o = a(P, 64 * f, 64 * f + 64)
            mm([(o, zwin("Zw", b), a(XR, 1024 * f + b, 1024 * f + 1024, 16), b == 0, b == 15 and not withn) for b in range(16)]
               + ([(o, I1, TB, False, True)] if withn else []))
        UI, UU, W1, W2, W3, W4, QQ = 0, 128, 272, 400, 528, 656, 1040
        parts = ((0, 64), (64, 128))
        wi = lambda b, p: a(WI, b + p[0], b + p[1])
        lin, LI = "l" in cfg["opt"][0] and h in cfg["lin"], 784
        for p in parts:
            if withn:
                tt(wi(UI, p), a(P, p[0], p[1]), TB, ALU.subtract)
            elif not lin:
                cp(wi(UI, p), a(P, p[0], p[1]))
            if lin:
                ts(wi(LI, p), a(P, p[0], p[1]), 32.0, ALU.mult)
        for p in parts:
            if lin and not withn:
                ts(wi(UU, p), wi(LI, p), 5, ALU.arith_shift_right, 4095, ALU.bitwise_and)
            else:
                ts(wi(UU, p), wi(UI, p), 4095, ALU.bitwise_and)
            if lin:
                ts(wi(W2, p), wi(LI, p), 8191, ALU.bitwise_and)
        for lo, hi, nx in ((64, 128, 0), (0, 56, 72), (56, 64, 64)):
            tt(a(WI, W1 + lo, W1 + hi), a(WI, UU + lo, UU + hi), a(WI, UU + nx, UU + nx + hi - lo), ALU.mult)
        for p in parts[::-1]:
            if lin:
                tt(wi(W3, p), wi(W1, p), wi(W2, p), ALU.add)
                ts(wi(W4, p), wi(W3, p), 5, ALU.arith_shift_right, 255, ALU.bitwise_and)
            else:
                ts(wi(W2, p), wi(W1, p), 5, ALU.arith_shift_right)
                tt(wi(W3, p), wi(W2, p), a(P, p[0], p[1]), ALU.add)
                ts(wi(W4, p), wi(W3, p), 255, ALU.bitwise_and)
            dh = a("wf%d" % h, 384 + p[0], 384 + p[1])
            tt(dh, wi(W4, p), a(S, p[0], p[1]), ALU.mult)
            if "q" in cfg["opt"][0]:
                tt(a(U, 128 + p[0], 128 + p[1]), dh, a(S, 128 + p[0], 128 + p[1]), ALU.add)
            else:
                tt(wi(QQ, p), dh, a(S, 128 + p[0], 128 + p[1]), ALU.add)
                cp(a(U, 128 + p[0], 128 + p[1]), wi(QQ, p))
            act(a(WB, p[0], p[1]), dh, ACT.Sign, bias=255.5 / 256, scale=-1.0)
        win = a("X", X0, X0 + 2 * W)
        AA = a(LB, 0, 256)
        for f in (1, 0):
            mode = cfg["bmode"][(h, f)]
            o = 1024 * f
            for j in (0, 1):
                md = mode[j]
                lo = o + 512 * j
                x, y, c = a(AD, lo, lo + 512), a(D, lo, lo + 512), 128 + 64 * f + 32 * j
                if md == "Z":
                    act(y, ind(win, a(U, c, c + 32)), scale=-1.0)
                    e = "E%d" % j
                    if "z" in cfg["opt"][0]:
                        mm([(a(e, 0, 256), I1, AA, True, False), (a(e, 256, 512), I1, AA, False, False)])
                        mm([(a(e, 0, 512), I1, y, False, True)])
                    else:
                        mm([(a(e, 0, 512), I1, y, True, False), (a(e, 0, 256), I1, AA, False, False),
                            (a(e, 256, 512), I1, AA, False, True)])
                    act(x, a(e, 0, 512), ACT.Abs)
                else:
                    for i in (0, 1):
                        tt(a(D, lo + 256 * i, lo + 256 * i + 256), ind(win, a(U, c + 16 * i, c + 16 * i + 16)), AA, ALU.subtract)
                    if md == "W":
                        ts(x, y, 0.0, ALU.min, -2.0, ALU.mult)
                    else:
                        act(x, y, ACT.Abs)
            kb, ko = (Q, 0) if f == 0 else (P, 128)
            K = a(kb, ko, ko + 64)
            mm([(K, I23, a(WB, 64 * f, 64 * f + 64), True, False), (K, CK, a("ones", 0, 64, 1, 2), False, False),
                (K, IKN, a(WB, 1280 + 64 * f, 1344 + 64 * f), False, False)])
            if mode == "WW":
                mm([(K, zwin("Zn", b), a(D, o + b, o + 1024, 16), False, False) for b in range(16)])
            else:
                for j in (0, 1):
                    if mode[j] == "W":
                        mm([(a(kb, ko + 32 * j, ko + 32 * j + 32), zwin("Zn", b), a(D, o + 512 * j + b, o + 512 * j + 512, 16),
                             False, False) for b in range(16)])
            mm([(K, zwin("Zn", b), a(AD, o + b, o + 1024, 16), False, b == 15) for b in range(16)])
            ev = a(LF, 72, 136) if f == 0 else a(LF, 64, 128)
            qq = a(U, 128 + 64 * f, 192 + 64 * f) if "q" in cfg["opt"][0] else a(WI, QQ + 64 * f, QQ + 64 * f + 64)
            for j, pay in enumerate((qq, ev, a(LF, 0, 64))):
                tt(nd(KB, j, None) if f == 1 else a(S, 272 + 64 * j, 336 + 64 * j), K, pay, ALU.add)

    def rising(h):
        t = NS - 1
        tag[0] = "s%d%d" % (t, h)
        LF, LB, P, Q, S, U, WI, WB = names(t, h)
        ZA, ZB, tr, OF, HH, WF, SF, E = "ZA%d" % h, "ZB%d" % h, "tr%d" % h, "OF%d%d" % (t, h), "hh%d" % h, "wf%d" % h, "sf%d" % h, "E%d" % h
        for x in (0, 1):
            for j, op in enumerate((ALU.min, ALU.max)):
                tt(nd(ZB, x, None, j, None), a(LF, 64 * x, 64 * x + 32), a(LF, 64 * x + 32, 64 * x + 64), op)
        for src, dst in ((ZB, ZA), (ZA, ZB)):
            for j, op in enumerate((ALU.min, ALU.max)):
                tt(nd(dst, None, None, j, None), nd(src, None, (0, 2), None, None), nd(src, None, (2, 4), None, None), op)
        od, ev = nd(ZB, 0, None, None, None), nd(ZB, 1, None, None, None)
        tt(a(tr, 512, 576), od, ev, ALU.max)
        tt(a(tr, 576, 640), od, ev, ALU.min)
        act(a(tr, 0, 256), ind(a(tr, 512, 640), T2W))
        transpose(tr)
        act(a(OF, 0, 128), ind(a(tr, 256, 512), W2N))
        RS = a(HH, 16, 144)
        act(RS, a(OF, 0, 128))
        mm([(a(E, 0, 128), SU, RS, True, True), (a(E, 128, 256), SD, RS, True, True)])
        act(a(WF, 512, 640), a(E, 0, 128), bias=col(BU))
        act(a(WF, 640, 768), a(E, 128, 256), bias=col(BD))
        tt(a(SF, 176, 184), nd(ZB, 0, 0, 0, None), nd(ZB, 1, 0, 0, None), ALU.subtract)
        tt(a(SF, 184, 192), a(SF, 176, 184), a(LF, 136, 144), ALU.mult)
        act(a(U, 280, 288), a(SF, 184, 192), ACT.Sign)
        act(a(WB, 2960, 3088), ind(a("pm", 0, 16), a(U, 280, 288)))

    def back(t, h):
        tag[0] = "b%d%d" % (t, h)
        LF, LB, P, Q, S, U, WI, WB = names(t, h)
        KB, SI, SF, WF, VB, SC, HH, E = ["%s%d" % (x, h) for x in ("KB", "si", "sf", "wf", "VB", "SC", "hh", "E")]
        OF, OB = "OF%d%d" % (t, h), "OB%d%d" % (t, h)
        last = t == NS - 1
        A0 = a(LB, 0, 128)
        f8 = lambda j, n=1: a(SF, 8 * j, 8 * (j + n))
        opt = cfg["opt"][last]
        for r in ((0, 1), (1, 3)) if "f" in opt else ((0, 3),):
            tt(nd(KB, r, None), nd(KB, r, None), a(S, 272 + 64 * r[0], 272 + 64 * r[1]), ALU.min)
            tt(nd(KB, r, (0, 32)), nd(KB, r, (0, 32)), nd(KB, r, (32, 64)), ALU.min)
            tt(nd(KB, r, (0, 16)), nd(KB, r, (0, 16)), nd(KB, r, (16, 32)), ALU.min)
            tt(a(SI, 8 * r[0], 8 * r[1]), nd(KB, r, (0, 8)), nd(KB, r, (8, 16)), ALU.min)
            if r[1] == 1 and "b" in opt:
                ts(a(U, 256, 264), a(SI, 0, 8), W - 1, ALU.bitwise_and)
            else:
                ts(a(SI, 24 + 8 * r[0], 24 + 8 * r[1]), a(SI, 8 * r[0], 8 * r[1]), (1 << 24) + W - 1, ALU.bitwise_and)
        QI, EV, OD = [a(SI, 24 + 8 * j, 32 + 8 * j) for j in range(3)]
        UQ, UL = a(U, 256, 264), a(U, 264, 272)
        if "b" in opt:
            QI = UQ
        else:
            ts(UQ, QI, W - 1.0, ALU.min)
        GT, AQ, DL, RL, CL, TB = [a(WB, 128 * j, 128 * j + 128) for j in (2, 3, 4, 5, 7, 8)]
        XQ, SS, R1, R2, S2, PEN, MK = [a(WB, 1664 + 128 * j, 1792 + 128 * j) for j in range(7)]
        YA, NE = a(WB, 2560, 2704), a(WB, 2704, 2960)
        qw = ind(a("X", TW, TW + W), UQ)
        PG_ = "pg%d" % h
        tt(GT, qw, A0, ALU.is_gt)
        act(XQ, qw)
        DQ = a(Q, 256, 384)
        mm([(DQ, I1, XQ, True, False), (DQ, IN, A0, False, True)])
        act(AQ, DQ, ACT.Abs)
        if "v" in opt:
            ts(R2, DQ, -2.0, ALU.max, 2.0, ALU.min)
        LH, L16, Q16, RS = a(HH, 0, 8), a(HH, 144, 272), a(HH, 272, 400), a(HH, 16, 144)
        SG, L, LL, DE, DF, HI, LO = a(LF, 136, 144), f8(1), f8(17), f8(19), f8(8), f8(10), f8(9)
        tt(DF, EV, OD, ALU.subtract)
        if "a" in opt:
            tt(a(PG_, 31, 256, 32), DF, SG, ALU.mult)
            tt(HI, EV, OD, ALU.max)
            tt(LO, EV, OD, ALU.min)
            mm([(a(S, 0, 256), C75, a("CC", 512, 768, 1, 1), True, False), (a(S, 0, 256, 2), BL1, GT, False, True)])
            scan(a(WF, 128, 384), a(PG_, 0, 256), a(S, 0, 256))
            tt(f8(12), a(WF, 159, 384, 32), HI, ALU.min)
            tt(L, f8(12), LO, ALU.max)
            ts(UL, L, float(W), ALU.min)
            ts(LH, L, float(W), ALU.min)
        else:
            tt(LO, DF, SG, ALU.mult)
            tt(HI, EV, OD, ALU.add)
            mm([(a(S, 0, 128), BLK, GT, True, True)])
            scan(a(WF, 272, 400), a("pg0", 0, 128), a(S, 0, 128))
            act(f8(11), a(WF, 287, 400, 16), ACT.Sign, bias=a("ci", 111, 112))
            tt(f8(12), f8(11), LO, ALU.mult)
            tt(L, f8(12), HI, ALU.add)
            ts(UL, L, 0.5, ALU.mult, float(W), ALU.min)
            if "h" in opt:
                act(LH, UL)
            else:
                ts(LH, L, 0.5, ALU.mult, float(W), ALU.min)
        tt(DL, ind(a("X", TW, TW + W + 16), UL), A0, ALU.subtract)
        LS = UL if "h" in opt else LH
        act(f8(24), LS, scale=-1.0)
        act(L16, ind(a("iota", 0, W + 8), UL))
        for m in range(8):
            lo, k = (16 * m - 16, 32) if m % 2 else (16 * m, 16)
            act(a(WB, 2704 + 32 * m, 2704 + 32 * m + k), a(HH, 144 + lo, 144 + lo + k), ACT.Abs, bias=a(SF, 192 + m, 193 + m))
        act(RL, DL, ACT.Abs)
        EE, two = a(P, 256, 512), [nd(P, (4, 8), (0, 32)), nd(P, (4, 8), (32, 64))]
        mm([(a(P, 256 + 64 * j, 320 + 64 * j), IN, a("mask", 0, 64), j == 0, False) for j in range(4)]
           + [(o, BLK, AQ, False, False) for o in two])
        mm([(o, NBLK, RL, False, o is two[1]) for o in two])
        tt(a(VB, 0, 256), EE, NE, ALU.is_gt)
        FIN = a(SC, 31, 256, 32)
        if "d" in opt:
            act(f8(14), LH, bias=float(X0))
            scan(a(SC, 0, 256), a("d0", 256, 512), a(VB, 0, 256))
            for m in range(7, -1, -1):
                ts(a(U, 288 + m, 289 + m), a(SC, 31 + 32 * m, 32 + 32 * m), a(SF, 112 + m, 113 + m), ALU.mult, col(PS if m % 2 else PR), ALU.max)
            if not last:
                scan(a(SC, 256, 512), a("d0", 512, 768), a(VB, 0, 256))
        else:
            act(f8(14), LS, bias=X0 / BIG - 1.0, scale=1.0 / BIG)
            scan(a(SC, 0, 256), a("d0", 0, 256), a(VB, 0, 256))
            tt(f8(15), FIN, f8(14), ALU.add)
            for e in (0, 1):
                ts(a(U, 288 + e, 296, 2), a(SF, 120 + e, 128, 2), BIG, ALU.mult, col(PS if e else PR), ALU.max)
        EQ = a(WF, 128, 272)
        if not last and "e" in opt:
            act(LL, LH)
        if not last and "e" not in opt:
            mm([(a(Q, 0, 144), I1, a(LF, 0, 144), True, False)]
               + [(a(Q, 8 * k, 8 * k + 8), IN, LH, False, k == 16) for k in range(17)])
            act(YA, a(Q, 0, 144), ACT.Abs)
            act(EQ, YA, ACT.Relu, bias=1.0, scale=-1.0)
        B = a(Q, 256, 384)
        if "c" in opt:
            act(CL, DL, ACT.Relu, bias=-8.0)
            act(MK, DL, ACT.Relu, bias=-8.0, scale=-1.0)
            mm([(B, I1, A0, True, False), (B, I1, CL, False, False), (B, IN, MK, False, True)])
        else:
            ts(CL, DL, -8.0, ALU.max, 8.0, ALU.min)
            mm([(B, I1, A0, True, False), (B, I1, DL, False, False), (B, IN, CL, False, True)])
        act(TB, B)
        for m in range(3, -1, -1):
            cp(ind(a("X", 0, TW), a(U, 288 + 2 * m, 290 + 2 * m)), a(WB, 1024 + 32 * m, 1056 + 32 * m))
        tag[0] = "u%d%d" % (t, h)
        LF2, LB2 = "LF%d%d" % (t + 1, h), "LB%d%d" % (t + 1, h)
        MG = a(P, 0, 128)
        if not last:
            GO = a(OF, zone(t + 1), zone(t + 1) + 8)
            if "R" not in opt:
                tt(f8(13), QI, LS, ALU.subtract)
            if "r" in opt or "R" in opt:
                scan(a(SC, 256, 512), a("d0", 512, 768), a(VB, 0, 256))
            if "R" in opt:
                tt(DE, QI, LH, ALU.subtract)
                tt(a(HH, 272, 416), ind(f8(19, 2), BCK), EQ, ALU.mult)
                act(GO, a(SC, 287, 512, 32))
            elif "d" in opt or "r" in opt:
                tt(DE, f8(13), a(SC, 287, 512, 32), ALU.mult)
                act(GO, a(SC, 287, 512, 32))
            else:
                ts(GO, FIN, 0.5, ALU.is_gt)
                tt(DE, f8(13), GO, ALU.mult)
            if "R" in opt:
                tt(a(OF, 0, 144), ind(a(SC, 256, 512), a("lst", 112, 121)), a(HH, 272, 416), ALU.mult)
            elif "e" in opt:
                for m in range(8):
                    ts(a(OF, m, 136, 8), a(LF, m, 136, 8), a(SF, 136 + m, 137 + m), ALU.is_equal, a(SF, 152 + m, 153 + m), ALU.mult)
            else:
                tt(a(OF, 0, 144), ind(f8(19, 2), BCK), EQ, ALU.mult)
            lo = min(0, zone(t + 1))
            send([a(LF2, lo, lo + 152)], [a(LF, lo, lo + 152), a(OF, lo, lo + 152)], "arrF%d%d" % (t, h))
        mm([(MG, BLK, AQ, True, False), (MG, NBLK, RL, False, True)])
        if last:
            OG, GU, GD, T1, DC, PP_ = "OG%d" % h, a(WF, 512, 640), a(WF, 640, 768), a(WF, 768, 896), a(WF, 896, 1024), a(WF, 0, 128)
            act(Q16, ind(a("iota", 0, W + 8), UQ))
            mm([(a(E, 256, 384), I1, Q16, True, False), (a(E, 256, 384), IN, RS, False, True)])
            T1 = a(E, 256, 384)
            tt(T1, T1, GD, ALU.max)
            tt(DC, T1, GU, ALU.min)
            mm([(a(E, 384, 512), I1, RS, True, False), (a(E, 384, 512), IN, L16, False, True)])
            tt(PP_, a(E, 384, 512), DC, ALU.mult)
            act(PEN, PP_, ACT.Relu, scale=-4096.0)
            tt(T1, MG, PEN, ALU.is_gt)
            tt(a(OG, 0, 128), T1, DC, ALU.mult)
            M2, M3 = a(S, 0, 128), a(S, 384, 512)
            mm([(M2, BLK, AQ, True, False), (M2, NBLK, RL, False, False), (M2, NBLK, PEN, False, True)])
            act(S2, M2, ACT.Sign, bias=-2.0 ** -13)
            mm([(M3, I1, S2, True, False), (M3, I1, a(WB, 2960, 3088), False, True)])
            act(a(OF, 128, 256), M3, ACT.Abs)
            send([a(LF2, 0, 256)], [a(OF, 0, 256), a(OG, 0, 256)], "arrF%d%d" % (t, h))
        act(SS, MG, ACT.Sign, bias=-2.0 ** -13)
        if "v" in opt:
            act(a(Q, 384, 512), SS, ACT.Relu)
            tt(a(OB, 0, 128), a(Q, 384, 512), R2, ALU.mult)
        else:
            for o, r, pos, neg in ((a(S, 128, 256), R1, I1, IN), (a(Q, 384, 512), R2, IN, I1)):
                mm([(o, pos, XQ, True, False), (o, neg, A0, False, False), (o, IN, SS, False, True)])
                act(r, o, ACT.Relu, bias=-1.0)
            G = a(S, 256, 384)
            mm([(G, I1, XQ, True, False), (G, IN, R1, False, False), (G, I1, R2, False, True)])
            act(a(OB, 0, 128), G)

    def levels(t, h):
        tag[0] = "u%d%d" % (t, h)
        LB2, last = "LB%d%d" % (t + 1, h), t == NS - 1
        send([a(LB2, 0, 128)] + ([] if last else [a(LB2, 128, 256)]),
             ([a("LB%d%d" % (t, h), 0, 128)] if "v" in cfg["opt"][last] else []) + [a("OB%d%d" % (t, h), 0, 128)], "arrB%d%d" % (t, h))
        if not last:
            ops[-1]["after"] = [i for i, o in enumerate(ops) if o["sem"] == "arrF%d0" % t]

    for t in range(NS):
        if t > 0:
            tag[0] = "twin"
            dma(a("X", TW, TW + W), XM, "tw%d" % t, 524288)
        for h in ORDER:
            front(t, h)
        for h in ORDER if t == NS - 1 else ():
            rising(h)
        for h in ORDER:
            back(t, h)
        for h in ORDER:
            levels(t, h)
    tag[0] = "end"
    dma(dram("yx"), XM, "stX", 524288)
    for h in ORDER:
        LF, LB = "LF%d%d" % (NS, h), "LB%d%d" % (NS, h)
        dma(dram("yr", 128 * h, 128 * h + 128), a(LF, 0, 128), "stR%d" % h, 65536)
        dma(dram("ya", 128 * h, 128 * h + 128), a(LB, 0, 128), "stA%d" % h, 32768, "A")
        dma(dram("ys", 128 * h, 128 * h + 128), a(LF, 128, 256, 1, -16), "stS%d" % h, 4096, "A")
    return ops


def link(ops):
    hist = {}
    for i, o in enumerate(ops):
        deps = {j: False for j in o.get("after", ())}
        for kind, lst in (("r", o["rd"]), ("w", o["wr"])):
            for name, lo, hi in lst:
                ps = SCRATCH[name][0] == "psum"
                for j, k2, l2, h2 in hist.get(name, ()):
                    if j == i:
                        continue
                    other = ops[j]["eng"] != o["eng"] or ops[j]["sem"] is not None or o["sem"] is not None
                    if ps and other:
                        deps[j] = True
                    elif ps and o["eng"] == "T":
                        deps[j] = deps.get(j, False)
                    elif lo < h2 and l2 < hi and (kind == "w" or k2 == "w"):
                        deps[j] = deps.get(j, False) or other or o["eng"] != "T"
        for kind, lst in (("r", o["rd"]), ("w", o["wr"])):
            for name, lo, hi in sorted(set(lst)):
                old = hist.get(name, [])
                if kind == "w" and SCRATCH[name][0] != "psum":
                    old = [e for e in old if not (lo <= e[2] and e[3] <= hi) or e[0] == i]
                if SCRATCH[name][0] == "psum":
                    k, turns, e = len(old), 0, o["eng"]
                    while k > 0 and (turns < 1 or ops[old[k - 1][0]]["eng"] == e):
                        if ops[old[k - 1][0]]["eng"] != e:
                            turns, e = turns + 1, ops[old[k - 1][0]]["eng"]
                        k -= 1
                    old = old[k:]
                hist[name] = old + [(i, kind, lo, hi)]
        o["deps"] = deps


def arrange(ops, cfg):
    n, LAT = len(ops), cfg["lat"]
    succ = [[] for _ in ops]
    for i, o in enumerate(ops):
        for j in o["deps"]:
            succ[j].append(i)
    prio = [0.0] * n
    for i in range(n - 1, -1, -1):
        o = ops[i]
        prio[i] = o["cost"] + o["lat"] + max([prio[j] + (LAT if ops[j]["deps"][i] else 0.0) for j in succ[i]] + [0.0])
    left = [len(o["deps"]) for o in ops]
    ready = {e: [] for e in "VATGS"}
    avail = [0.0] * n
    for i in range(n):
        if left[i] == 0:
            ready[ops[i]["eng"]].append(i)
    free = {e: 0.0 for e in "VATGS"}
    fin = [0.0] * n
    for _ in range(n):
        best = None
        for e in "VATGS":
            if ready[e]:
                s = max(free[e], min(avail[i] for i in ready[e]))
                if best is None or s < best[0]:
                    best = (s, e)
        s, e = best
        i = max((i for i in ready[e] if avail[i] <= s + cfg["slack"]), key=lambda i: (prio[i], -i))
        ready[e].remove(i)
        st = max(free[e], avail[i])
        o = ops[i]
        o["start"] = st
        free[e] = st + o["cost"]
        fin[i] = free[e] + o["lat"]
        for j in succ[i]:
            avail[j] = max(avail[j], fin[i] + (LAT if ops[j]["deps"][i] else 0.0))
            left[j] -= 1
            if left[j] == 0:
                ready[ops[j]["eng"]].append(j)
    pre = [[(j, ops[j]["lat"] + (LAT if w else 0.0)) for j, w in o["deps"].items()] for o in ops]
    post = [[] for _ in ops]
    for i in range(n):
        for j, d in pre[i]:
            post[j].append((i, d))
    start = [o["start"] for o in ops]
    best = (max(fin), start)
    for _ in range(cfg["passes"]):
        back = place(ops, sorted(range(n), key=lambda i: (-start[i] - ops[i]["cost"], -i)), post, [o["lat"] for o in ops])
        start = place(ops, sorted(range(n), key=lambda i: (-back[i] - ops[i]["cost"], i)), pre, [0.0] * n)
        end = max(start[i] + ops[i]["cost"] + ops[i]["lat"] for i in range(n))
        if end < best[0]:
            best = (end, start)
    start = best[1]
    order = {e: [] for e in "VATGS"}
    for i in sorted(range(n), key=lambda i: (start[i], i)):
        ops[i]["start"] = start[i]
        order[ops[i]["eng"]].append(i)
    return order, [start[i] + ops[i]["cost"] + ops[i]["lat"] for i in range(n)]


def place(ops, seq, pre, first):
    at = [0.0] * len(ops)
    busy = {e: ([], []) for e in "VATGS"}
    for i in seq:
        s, c = first[i], ops[i]["cost"]
        for j, d in pre[i]:
            x = at[j] + ops[j]["cost"] + d
            if x > s:
                s = x
        lo, hi = busy[ops[i]["eng"]]
        k = len(lo)
        while k > 0 and hi[k - 1] > s:
            k -= 1
        while k < len(lo) and lo[k] < s + c:
            s = max(s, hi[k])
            k += 1
        lo.insert(k, s)
        hi.insert(k, s + c)
        at[i] = s
    return at


def improve(ops, cfg):
    n, seen, key, step = len(ops), {}, [], []
    for o in ops:
        g = o["tag"]
        seen[g, o["key"]] = seen.get((g, o["key"]), 0) + 1
        each = len(g) == 3 and g != "end"
        key.append(g if g == "twin" else ("" if each and g[:2] not in cfg["own"] else g) + o["key"] + "#%d" % seen[g, o["key"]])
        step.append(int(o["sem"][2]) if g == "twin" else int(g[1]) if each else 0)
    first = [min(o["start"] for o in ops if o["tag"] == "f%d1" % t and o["eng"] == "V") for t in range(NS)]
    period = (first[3] - first[1]) / 2
    tau = {}
    for t in (2, 1, 3, 0):
        for i, o in enumerate(ops):
            if step[i] == t and key[i] not in tau:
                tau[key[i]] = o["start"] - period * t
    eng = ["VATGS".index(o["eng"]) for o in ops]
    below, deps = [0] * n, []
    for i, o in enumerate(ops):
        cover = 0
        for j, w in o["deps"].items():
            if w:
                cover |= below[j]
        deps.append([j for j in o["deps"] if not cover >> j & 1])
        for j in o["deps"]:
            below[i] |= below[j] | 1 << j
    models = []
    for m in cfg["models"]:
        alt = build(dict(cfg, **m))
        models.append(([o["cost"] for o in alt], [o["lat"] for o in alt],
                       [[(j, alt[j]["lat"] + (m["lat"] if o["deps"][j] else 0.0)) for j in d] for o, d in zip(ops, deps)]))

    rows = [(key[i], period * step[i], deps[i]) for i in range(n)]
    ends = [i for i, o in enumerate(ops) if o["tag"] == "end"]

    def run(was, room):
        at = []
        for k, x, d in rows:
            x += tau[k]
            for j in d:
                if at[j] > x:
                    x = at[j]
            at.append(x)
        seq = sorted(range(n), key=lambda i: at[i])
        out, fins, over = [], [], 0.0
        for (cost, lat, pre), old in zip(models, was):
            fin, free = [0.0] * n, [0.0] * 5
            for i in seq:
                e = eng[i]
                s = free[e]
                for j, d in pre[i]:
                    d += fin[j]
                    if d > s:
                        s = d
                free[e] = fin[i] = s + cost[i]
            out.append(max(fin[i] + lat[i] for i in ends))
            fins.append(fin)
            over += out[-1] - old
            if over > room + 150.0 * (len(models) - len(out)):
                return None
        return out, fins, seq

    def tight(fins, seq):
        before, last, arcs = [-1] * n, [-1] * 5, []
        for i in seq:
            before[i], last[eng[i]] = last[eng[i]], i
        for (cost, lat, pre), fin in zip(models, fins):
            i = max(ends, key=lambda i: fin[i] + lat[i])
            while i >= 0:
                s, j = fin[i] - cost[i], before[i]
                if j >= 0 and fin[j] > s - 0.01:
                    arcs.append((j, i))
                else:
                    j = next((j for j, d in pre[i] if fin[j] + d > s - 0.01), -1)
                i = j
        return arcs

    seed = [cfg["seed"]]

    def rnd():
        seed[0] = (seed[0] * 1103515245 + 12345) % 2147483648
        return seed[0] / 2147483648.0

    keys = sorted(tau)
    cur, fins, seq = run([1e9] * len(models), 0.0)
    arcs = tight(fins, seq)
    best = (sum(cur), seq)
    best += (fins[0],)
    same, heat, span, r0 = 2, cfg["heat"], cfg["rounds"], 0
    for r in range(cfg["rounds"] + cfg["apart"]):
        if r == cfg["rounds"]:
            for i, o in enumerate(ops):
                key[i], step[i] = "%-4s%d" % (o["tag"][:4], i), 0
                tau[key[i]] = best[2][i] - models[0][0][i]
                rows[i] = (key[i], 0.0, deps[i])
            keys = sorted(key)
            cur, fins, seq = run([1e9] * len(models), 0.0)
            arcs = tight(fins, seq)
            same, heat, span, r0 = 3, cfg["heat2"], cfg["apart"], r
        far = (1.0, 1.0, 100.0, 400.0, 1000.0, 3000.0)[int(6 * rnd())] * rnd()
        u = rnd()
        j, i = arcs[int(len(arcs) * rnd())]
        if u < 0.35:
            new = {key[i]: tau[key[j]] + period * (step[j] - step[i]) - far}
        elif u < 0.7:
            new = {key[j]: tau[key[i]] + period * (step[i] - step[j]) + far}
        elif u < 0.8:
            k = keys[int(len(keys) * rnd())]
            new = {k: tau[k] + (far if u < 0.75 else -far)}
        else:
            k = key[i] if u < 0.9 else key[j]
            wide, by = 3000.0 * rnd(), (-1500.0 if u < 0.9 else 1500.0) * rnd()
            side = 1.0 if rnd() < 0.5 else -1.0
            new = {x: tau[x] + by for x in keys if x[:same] == k[:same] and 0.0 <= (tau[k] - tau[x]) * side <= wide}
        old = {k: tau[k] for k in new}
        tau.update(new)
        got = run(cur, -math.log(1.0 - rnd()) * len(models) * (3.0 + heat * (1.0 - (r - r0) / span)))
        if got:
            if got[0] != cur or r % 8 == 0:
                arcs = tight(got[1], got[2])
            cur = got[0]
            if sum(cur) < best[0]:
                best = (sum(cur), got[2], got[1][0])
        else:
            tau.update(old)
    order = {e: [i for i in best[1] if ops[i]["eng"] == e] for e in "VATGS"}
    return order, [best[0]]


def plan(cfg):
    ops = build(cfg)
    link(ops)
    order, fin = arrange(ops, cfg)
    if cfg["rounds"]:
        order, fin = improve(ops, cfg)
    pos = {}
    for e in order:
        for k, i in enumerate(order[e]):
            pos[i] = k
    need = set()
    waits = {}
    for e in order:
        seen = {}
        for i in order[e]:
            top = {}
            for j, w in ops[i]["deps"].items():
                if not w:
                    continue
                key = ops[j]["sem"] or ops[j]["eng"]
                if pos[j] > seen.get(key, -1) and (key not in top or pos[j] > pos[top[key]]):
                    top[key] = j
            for key, j in top.items():
                seen[key] = pos[j]
                need.add(j)
            waits[i] = list(top.values())
    cnt = {}
    for e in order:
        c = 0
        for i in order[e]:
            if ops[i]["sem"] is None and i in need:
                c += 1
                cnt[i] = c
    return {"ops": ops, "order": order, "waits": waits, "cnt": cnt, "need": need, "end": max(fin), "fin": fin}


_PLAN = {}


def rank_program(g, core, T, topo):
    rank = T.rank_of(core)
    if rank is None:
        return
    if "p" not in _PLAN:
        _PLAN["p"] = plan(CFG)
    p = _PLAN["p"]
    ops, cores = p["ops"], T.cores
    nxt, prv = cores[(rank + HOP) % len(cores)], cores[(rank - HOP) % len(cores)]
    rid, pid = topo.addr(nxt, core)
    eng, mask = topo.engines(core, nxt), topo.mask(core, nxt)
    arrive = len(topo.engines(prv, core))
    queues = {"V": g.vector, "A": g.scalar, "T": g.tensor, "G": g, "S": g.sync}
    sent = 0
    for e in "SGTAV":
        q = queues[e]
        for i in p["order"][e]:
            o = ops[i]
            for j in p["waits"][i]:
                s = ops[j]["sem"]
                if s is None:
                    q.wait_ge(T.sem[ops[j]["eng"]], p["cnt"][j])
                else:
                    q.wait_ge(T.sem[s], arrive * len(ops[j]["call"][1]) if s.startswith("arr") else 16)
            if isinstance(o["call"], tuple):
                dsts, srcs = [real(T, s) for s in o["call"][1]], [real(T, s) for s in o["call"][2]]
                if len(srcs) == 1 and len(dsts) == 1:
                    q.remote_dma(dsts[0], srcs[0], T.sem[o["sem"]], T.sem.sent, pid, rid, mask)
                else:
                    q.remote_dma_fused([RemoteDMATransfer(dst_ids=[DstId(rid=rid, pnc=pid)] * len(dsts), dma_engine_mask=mask,
                                                          remote_sem=T.sem[o["sem"]], srcs=srcs, dsts=dsts, alu_op=min(1, len(srcs) - 1))],
                                       local_sem=T.sem.sent)
                sent += len(eng)
            else:
                r = o["call"](q, T)
                if o["sem"] is not None:
                    r.then_inc(T.sem[o["sem"]], 16)
                elif i in p["cnt"]:
                    r.then_inc(T.sem[e], 1)
    g.wait_ge(T.sem.sent, sent)
    for i, o in enumerate(ops):
        if o["sem"] in DMAS and i not in p["need"]:
            g.sync.wait_ge(T.sem[o["sem"]], 16)
